import numpy as np, ml_dtypes
CORES = [2,6,10,14,18,22,26,30]
N = 8
BF = ml_dtypes.bfloat16
def gentries(a):
    return np.ascontiguousarray(a.reshape(8, 16, -1).transpose(0, 2, 1)).reshape(8, -1)
def gtable(e):
    e = np.asarray(e); return np.ascontiguousarray(e.reshape(8, -1, 16).transpose(0, 2, 1)).reshape(128, -1).astype(np.int32)
W, V, KC, R = 3072, 3072, 64, 2
LO, HI = 30, 190
def peps(rng):
    p = rng.integers(LO, HI + 1, (N, 8, V, 16)); i = np.arange(16); s = rng.integers(0, 15, (N, 8, V // 2, 1))
    p[:, :, 1::2] = np.take_along_axis(p[:, :, 0::2], np.where(i == s, s + 1, np.where(i == s + 1, s, i)), axis=-1); return p
def wants(rng):
    w = rng.integers(0, V, (N, 8, N, KC)); w[..., 1::2] = np.where(rng.random((N, 8, N, KC // 2)) < 0.25, w[..., 0::2] ^ 1, w[..., 1::2])
    w[..., KC - 1] = w[..., 2]; return w
def own(rng):
    e = np.argsort(rng.random((N, 8, V // 2)), axis=-1)[:, :, :N * KC // 2]; x = rng.integers(0, 2, e.shape)
    return np.stack([2 * e + x, 2 * e + 1 - x], axis=-1).reshape(N, 8, N, KC).transpose(2, 1, 0, 3).copy()
def bins(p, w):
    m = p[np.arange(N)[None, None, :, None], np.arange(8)[None, :, None, None], w].reshape(N, 8, N * KC, 16)
    b = np.add.accumulate(m, axis=-1); return b, b[..., -1:] + 64 - b
def noise(rng):
    return rng.integers(1, 4, (N, 8, 16, W)) * (rng.random((N, 8, 16, W)) < 0.3)
def some(rng):
    return np.argsort(rng.random((N, 8, N * KC)), axis=-1)[..., :R + 1]
def shine(rng, s, b, y, n, a, z):
    for r in range(N):
        for g in range(8):
            for t in n[r, g]:
                s[r, g][:, b[r, g, t]] = rng.integers(a, z + 1, (16, 16)); s[r, g][:, y[r, g, t]] = rng.integers(a, z + 1, (16, 16))
def pack(s, p, w):
    return {"spec": s.reshape(N, 128, W).astype(np.float32).astype(BF), "pep": p.transpose(0, 1, 3, 2).reshape(N, 128, V).astype(np.float32).astype(BF),
            "want": np.stack([gtable(w[r].reshape(8, N * KC)) for r in range(N)])}
def setup_inputs(rng):
    p, w, s, n = peps(rng), wants(rng), noise(rng), some(rng); b, y = bins(p, w)
    n[:, ::2, 0] = KC * rng.integers(0, N, (N, 4)) + 2; shine(rng, s, b, y, n, 4, 15)
    return pack(s, p, w)
def setup_inputs_kin(rng):
    p, w, s = peps(rng), own(rng), noise(rng); b, y = bins(p, w)
    n = 2 * np.argsort(rng.random((N, 8, N * KC // 2)), axis=-1)[..., :R + 1]
    shine(rng, s, b, y, n[..., 1:], 5, 9); shine(rng, s, b, y, n[..., :1], 12, 15)
    return pack(s, p, w)
def setup_inputs_twins(rng):
    p, w, s, n = peps(rng), own(rng), noise(rng), np.zeros((N, 8, 1), np.int64)
    for r in range(N):
        for g in range(8):
            q, k = [int(v) for v in rng.permutation(N)[:2]]; i, j = sorted([KC * q + int(rng.integers(KC)), KC * k + int(rng.integers(KC))])
            if g == 0: i, j = 0, N * KC - 1
            if g == 1: i = KC * q + int(rng.integers(KC - 1)); j = i + 1; w[r, g, q, j % KC] = w[r, g, q, i % KC]
            if g == 2: i, j = KC - 1, KC
            p[j // KC, g, w[r, g, j // KC, j % KC]] = p[i // KC, g, w[r, g, i // KC, i % KC]]; n[r, g, 0] = i
    b, y = bins(p, w); shine(rng, s, b, y, some(rng), 5, 9); shine(rng, s, b, y, n, 15, 15)
    s[:, 3] = rng.integers(1, 16, (N, 16, 1)); return pack(s, p, w)
def setup_inputs_ends(rng):
    p, w, s, n = peps(rng), wants(rng), noise(rng), np.zeros((N, 8, 1), np.int64)
    p[0, :, 0] = LO; p[N - 1, :, V - 1] = HI; p[:, :, 1] = 64; p[:, :, 2] = HI; p[:, :, 2, 0] = LO
    w[..., 0] = 0; w[..., 1] = 1; w[..., 2] = 2; w[..., KC - 1] = V - 1
    n[:, 0::4] = 1; n[:, 1::4] = 0; n[:, 2::4] = N * KC - 1; n[:, 3::4] = 2
    b, y = bins(p, w); shine(rng, s, b, y, some(rng), 5, 9); shine(rng, s, b, y, n, 15, 15)
    s[..., 0] = 15; s[..., W - 1] = 15; return pack(s, p, w)
def setup_inputs_dark(rng):
    p, w, s = peps(rng), own(rng), noise(rng)
    for r in range(N):
        for g in range(8): p[0, g, w[r, g, 0, 0], 0] = LO
    b, y = bins(p, w); shine(rng, s, b, y, some(rng), 4, 15)
    for r in range(N):
        d = rng.permutation(8)
        for g in d[:3]: s[r, g][:, y[r, g].reshape(-1)] = 0; s[r, g][:, LO] = rng.integers(1, 16, 16)
        s[r, d[3]] = 0
        g = d[4]; t = int(rng.integers(1, N * KC)); s[r, g][:, y[r, g].reshape(-1)] = 0
        s[r, g][:, b[r, g, t]] = rng.integers(8, 16, (16, 16)); s[r, g][:, y[r, g, t]] = rng.integers(8, 16, (16, 16))
    return pack(s, p, w)
def setup_inputs_spread(rng):
    p = np.minimum(HI, LO + ((HI - LO + 1) * rng.random((N, 8, V, 16)) ** 3).astype(np.int64)); k = (N, 8, 1, W)
    s = (rng.integers(0, 16, (N, 8, 16, W)) >> rng.integers(0, 3, k)) * (rng.random(k) > 0.0625)
    return pack(s, p, wants(rng))
def check_inputs(d):
    bad = []; s = d["spec"].astype(np.float32); p = d["pep"].astype(np.float32); w = d["want"]
    if not ((s >= 0) & (s <= 15) & (s == np.floor(s))).all(): bad.append("spec")
    if not ((p >= LO) & (p <= HI) & (p == np.floor(p))).all(): bad.append("pep")
    if not ((w >= 0) & (w < V)).all(): bad.append("want")
    return bad
def reference(spec, pep, want):
    left = spec.astype(np.float32).reshape(N, 8, 16, W); m_ = pep.astype(np.float32).astype(np.int64).reshape(N, 8, 16, V)
    win = np.zeros((N, 8, R), np.float32); score = np.zeros((N, 8, R), np.float32)
    for r in range(N):
        e = gentries(want[r]).reshape(8, N, KC)
        for g in range(8):
            m = np.concatenate([m_[q, g][:, e[g, q]] for q in range(N)], axis=1)
            b = np.add.accumulate(m, axis=0); y = b[15] + 64 - b
            s = left[r, g]
            for t in range(R):
                sc = np.sum(np.minimum(s[:, b], s[:, y]), axis=(0, 1))
                n = int(np.argmax(sc)); win[r, g, t] = n; score[r, g, t] = sc[n]
                s[:, b[:, n]] = 0; s[:, y[:, n]] = 0
    return {"win": win, "score": score, "left": left.reshape(N, 128, W).astype(BF)}

@@ -1,0 +1,278 @@
+from concourse.bass import DstId, RemoteDMATransfer
+from concourse.mybir import AluOpType, AxisListType, ActivationFunctionType
+
+N, KC, W = 8, 64, 3072
+NB = 15
+EARLY = 1024
+
+BF, F32, I32, U16 = "bfloat16", "float32", "int32", "uint16"
+SCRATCH = {"lland": ("sbuf", [128, 7, 32], I32), "ll": ("sbuf", [128, 2, 128], BF), "lt": ("sbuf", [128, 2, NB, 128], BF)}
+for _name, _cols, _dt in [
+        ("wants", 32, I32), ("loff", 32, U16), ("peps", W, BF), ("S", W, BF), ("gath", 448, BF), ("mass", 512, BF),
+        ("off", 960, U16), ("offt", 32, U16), ("gb0", 512 * NB, BF), ("gm0", 512 * NB, BF), ("gb1", 512 * NB, BF),
+        ("gm1", 512 * NB, BF), ("gt", 512, BF), ("tabs", 1024, F32), ("iw", 128, I32), ("iu", 128, I32), ("sg", 128, I32),
+        ("blk", 128, BF), ("blkn", 128, BF), ("blkp", 128, BF), ("ge", 128, BF), ("lbp", 128, BF), ("wd", 144, BF),
+        ("ones", 128, BF), ("lo", 448, BF), ("hi", 512, BF), ("zero", 16, BF), ("h8", 4, I32), ("half", 4, F32),
+        ("s64", 4, F32), ("kab", 4, F32), ("ki", 4, I32), ("woff", 4, U16), ("zl", 32, U16), ("res", 4, F32)]:
+    SCRATCH[_name] = ("sbuf", [128, _cols], _dt)
+for _name in ["pl0", "pl1", "pa0", "pb0", "pa1", "pb1", "pt", "ps"]:
+    SCRATCH[_name] = ("psum", [128, 512], F32)
+SEMAPHORES = ["qv", "qs", "qp", "qg", "dwant", "dpep", "dsa", "dsb", "dleft", "dres",
+              "lnear", "lfar", "sent_near", "sent", "rep0", "rep1", "rep2", "rep3"]
+
+ALU = AluOpType
+ACT = ActivationFunctionType
+
+
+def partner_order(T, topo, core):
+    ch = topo.chip(core)
+
+    def key(q):
+        c = T.cores[q]
+        cc = topo.chip(c)
+        kind = 0 if cc == ch else 1 if topo.mates(ch, cc) else 2 if topo.same_plane(ch, cc) else 3
+        return (kind, 0 if topo.die(c) == topo.die(core) else 1, q)
+    return sorted([q for q in range(N) if T.cores[q] != core], key=key)
+
+
+def bits(engines):
+    return sum(1 << e for e in engines)
+
+
+def rank_program(g, core, T, topo):
+    r = T.rank_of(core)
+    if r is None:
+        return
+    order = partner_order(T, topo, core)
+    src = [r] + order
+    place = [partner_order(T, topo, T.cores[q]).index(r) for q in order]
+    addr = [topo.addr(T.cores[q]) for q in order]
+    far = topo.engines(core, T.cores[order[1]])
+    near = [e for e in topo.engines(core, T.cores[order[0]]) if e not in far]
+    sem = T.sem
+    Q = {"v": g.vector, "s": g.scalar, "p": g.tensor, "g": g, "y": g.sync}
+    QS = {"v": "qv", "s": "qs", "p": "qp", "g": "qg"}
+    count = {"v": 0, "s": 0, "p": 0, "g": 0}
+    seen = {}
+
+    def wait(q, deps):
+        for name, val in deps:
+            if seen.get((q, name), 0) < val:
+                Q[q].wait_ge(sem[name], val)
+                seen[(q, name)] = val
+
+    def op(q, deps, method, *a, **k):
+        wait(q, deps)
+        method(*a, **k).then_inc(sem[QS[q]], 1)
+        count[q] += 1
+        return (QS[q], count[q])
+
+    V, S, P = g.vector, g.scalar, g.tensor
+
+    def v(deps, m, *a, **k):
+        return op("v", deps, m, *a, **k)
+
+    def s(deps, *a, **k):
+        return op("s", deps, S.activation, *a, **k)
+
+    def mm(deps, out, lhsT, rhs, start, stop):
+        return op("p", deps, P.matmul, out, lhsT, rhs, start, stop)
+
+    g.sync.dma_start(T.wants[:], T.want[:]).then_inc(sem.dwant, 16)
+    g.sync.dma_start(T.peps[:], T.pep[:]).then_inc(sem.dpep, 16)
+    WANT, PEP = ("dwant", 16), ("dpep", 16)
+    SPEC = [("dsb", 16)]
+    if EARLY:
+        g.sync.dma_start(T.S[:, 0:EARLY], T.spec[:, 0:EARLY]).then_inc(sem.dsa, 16)
+        SPEC.append(("dsa", 16))
+
+    t_iw = op("g", [], g.iota, T.iw[:], [[16, 8], [0, 16]], 15, -1)
+    t_iu = op("g", [], g.iota, T.iu[:], [[1, 128]], 0, -1)
+    wait("g", [WANT])
+    g.remote_dma_fused([RemoteDMATransfer(
+        dst_ids=[DstId(rid=addr[k][0], pnc=addr[k][1]) for k in range(1, 7)], dma_engine_mask=bits(far),
+        remote_sem=sem.lfar, src=T.wants[:], dsts=[T.lland[:, place[k], :] for k in range(1, 7)])], local_sem=sem.sent)
+    g.remote_dma(T.lland[:, place[0], :], T.wants[:], sem.lnear, sem.sent_near, addr[0][1], addr[0][0], bits(near))
+    t_lo = op("g", [], g.iota, T.lo[0:1, :], [[0, 7], [1, 64]], 0, 0, allow_small_or_imprecise_dtypes=True)
+    wait("y", [("sent_near", len(near))])
+    g.sync.dma_start(T.S[:, EARLY:W], T.spec[:, EARLY:W]).then_inc(sem.dsb, 16)
+
+    t_lt0 = v([], V.memset, T.lt[:], 0.0)
+    t_wd0 = v([], V.memset, T.wd[:], 0.0)
+    t_zero = v([], V.memset, T.zero[:], 0.0)
+    v([], V.memset, T.ones[0:1, :], 1.0)
+    for k in range(1, 7):
+        v([], V.memset, T.hi[0:1, 64 * (k - 1):64 * k], float(64 * src[k]))
+    v([], V.memset, T.hi[0:1, 384:448], float(64 * r))
+    t_hi = v([], V.memset, T.hi[0:1, 448:512], float(64 * src[7]))
+    t_sg = v([t_iw], V.tensor_scalar, T.sg[:], T.iw[:], 4, None, ALU.arith_shift_right)
+    t_h8 = v([], V.tensor_scalar, T.h8[:, 0:1], T.iw[:, 0:1], 8, None, ALU.bitwise_and)
+    t_ge = v([t_iu], V.tensor_scalar, T.ge[:], T.iu[:], 0.0, None, ALU.is_ge)
+    t_own = v([WANT], V.tensor_copy, T.loff[:, 0:4], T.wants[:, 4 * r:4 * r + 4])
+    t_blk = v([t_sg], V.tensor_scalar, T.blk[:], T.sg[:], 0.0, None, ALU.is_equal)
+    v([], V.tensor_scalar, T.blkn[:], T.sg[:], 0.0, -512.0, ALU.is_equal, ALU.mult)
+    v([], V.tensor_scalar, T.blkp[:], T.sg[:], 0.0, 512.0, ALU.is_equal, ALU.mult)
+    t_lb = v([t_ge, t_blk], V.tensor_tensor, T.ll[:, 0, :], T.ge[:], T.blk[:], ALU.mult)
+    t_wd = v([t_wd0], V.tensor_copy, T.wd[:, 15:128:16], T.blk[:, 15:128:16])
+    t_half = v([t_h8], V.tensor_scalar, T.half[:, 0:1], T.h8[:, 0:1], -64.0, 512.0, ALU.mult, ALU.add)
+    t_ly = v([t_lb], V.tensor_tensor, T.ll[:, 1, :], T.blk[:], T.ll[:, 0, :], ALU.subtract)
+    v([t_wd], V.tensor_tensor, T.lbp[:], T.ll[:, 0, :], T.wd[:, 0:128], ALU.subtract)
+    for gg in range(8):
+        t_const = v([t_ly, t_lt0], V.tensor_copy, T.lt[:, :, :, 16 * gg + 15], T.ll[:, :, 16 * gg:16 * gg + 15])
+
+    PA, PB = [T.pa0, T.pa1], [T.pb0, T.pb1]
+    for t in range(2):
+        mm([t_lo, t_hi], PA[t][:, 0:416], T.ones[0:1, :], T.lo[0:1, 0:416], True, False)
+        mm([], PA[t][:, 0:416], T.ones[0:1, :], T.hi[0:1, 0:416], False, False)
+        mm([], PB[t][:, 0:96], T.ones[0:1, :], T.lo[0:1, 32:128], True, False)
+        mm([], PB[t][:, 0:96], T.ones[0:1, :], T.hi[0:1, 416:512], False, False)
+
+    pepw = T.peps[:, 0:W]
+    mine = T.mass[:, 64 * r:64 * r + 64]
+    tail = T.mass[:, 64 * r + 32:64 * r + 64]
+    t_mine = s([t_own, PEP], mine, pepw.indirect(T.loff[:, 0:4]), ACT.Copy)
+    t_cn = v([("lnear", len(near))], V.tensor_copy, T.loff[:, 4:8], T.lland[:, 0, 4 * r:4 * r + 4])
+    t_gn = s([t_cn], T.gath[:, 0:64], pepw.indirect(T.loff[:, 4:8]), ACT.Copy)
+    wait("g", [t_gn])
+    g.remote_dma(mine, T.gath[:, 0:64], sem.rep0, sem.sent, addr[0][1], addr[0][0], bits(near))
+
+    PL = [T.pl0, T.pl1]
+
+    def obase(k):
+        return 0 if k == 0 else 64 + 128 * (k - 1)
+
+    def blocks(k):
+        return [0] if k == 0 else [2 * k - 1, 2 * k]
+
+    def lists(ks, bank, deps):
+        o = 0
+        for k in ks:
+            n = 32 * len(blocks(k))
+            rhs = T.mass[:, 64 * src[k]:64 * src[k] + n]
+            for side in range(2):
+                mm(deps, PL[bank][:, o:o + n], T.lbp[:] if side == 0 else T.ll[:, 1, :], rhs, True, False)
+                for h, b in enumerate(blocks(k)):
+                    tok = mm([], PL[bank][:, o + 32 * h:o + 32 * h + 32], T.lt[:, side, b, :], tail, False,
+                             h == len(blocks(k)) - 1)
+                o += n
+        return tok, o
+
+    def conv(ks, bank, made):
+        tok, n = made
+        return v([tok], V.tensor_copy, T.off[:, obase(ks[0]):obase(ks[0]) + n], PL[bank][:, 0:n])
+
+    l0 = lists([0], 0, [t_mine, t_const])
+    c0 = conv([0], 0, l0)
+    nfar = len(far)
+    t_cf = v([("lfar", 6 * nfar)], V.tensor_copy, T.loff[:, 8:32], T.lland[:, 1:7, 4 * r:4 * r + 4])
+    back = [v([t_cf, PEP], V.tensor_copy, T.gath[:, 64:192], pepw.indirect(T.loff[:, 8:16])),
+            s([t_cf], T.gath[:, 192:320], pepw.indirect(T.loff[:, 16:24]), ACT.Copy),
+            s([t_cf], T.gath[:, 320:448], pepw.indirect(T.loff[:, 24:32]), ACT.Copy)]
+    hf = nfar // 2
+    for j in range(3):
+        wait("g", [back[j]])
+        g.remote_dma_fused([RemoteDMATransfer(
+            dst_ids=[DstId(rid=addr[k][0], pnc=addr[k][1])], dma_engine_mask=bits(far[hf * h:hf * h + hf]),
+            remote_sem=sem["rep%d" % (j + 1)], src=T.gath[:, 64 * k:64 * k + 64], dst=mine)
+            for h, k in enumerate((2 * j + 1, 2 * j + 2))], local_sem=sem.sent)
+    l1 = lists([1], 1, [("rep0", len(near))])
+    c1 = conv([1], 1, l1)
+    ready = {0: c0, 1: c1}
+
+    wb, wy = T.S[:, 0:W], T.S[:, 64:W]
+
+    def offs(b, side, lo=0, n=32):
+        k = (b + 1) // 2
+        o = obase(k) + (32 * side if k == 0 else 64 * side + 32 * (b - (2 * k - 1))) + lo
+        return T.off[:, o:o + n]
+
+    def score(t, k, deps, stop_a, stop_b):
+        gm = T["gm%d" % t]
+        bs = blocks(k)
+        n = 32 * len(bs)
+        out = PA[t][:, 384:416] if k == 0 else PB[t][:, 32:96] if k == 7 else PA[t][:, 64 * (k - 1):64 * k]
+        for i in range(15):
+            tok = mm(deps, out, T.blkn[:], gm[:, 512 * bs[0] + i:512 * bs[0] + 16 * n:16], False, stop_a and i == 14)
+        ta = tok
+        for b in bs:
+            tok = mm([], PB[t][:, 0:32], T.blkn[:], gm[:, 512 * b + 15:512 * b + 512:16], False, stop_b and b == bs[-1])
+        return ta, tok
+
+    def results(t):
+        y = v([], V.tensor_copy, T.res[:, t:t + 1], T.ki[:, 2 * t + 1:2 * t + 2])
+        return v([y], V.tensor_scalar, T.res[:, 2 + t:3 + t], T.ki[:, 2 * t:2 * t + 1], T.res[:, t:t + 1],
+                 -1.0 / 512, ALU.subtract, ALU.mult)
+
+    sdeps = SPEC
+    for t in range(2):
+        gb, gm = T["gb%d" % t], T["gm%d" % t]
+        first = t == 0
+        gtok, mtok = {}, {}
+        va = v(sdeps + [c0], V.tensor_copy, gb[:, 0:256], wb.indirect(offs(0, 0, 0, 16)))
+        sa = s(sdeps + [c0], gb[:, 256:512], wb.indirect(offs(0, 0, 16, 16)), ACT.Copy)
+        if first:
+            p64 = mm(SPEC, T.ps[:, 0:2], T.blkp[:], T.S[:, 64:66], True, True)
+        else:
+            results(0)
+        v([va], V.tensor_tensor, gm[:, 0:256], wy.indirect(offs(0, 1, 0, 16)), gb[:, 0:256], ALU.min)
+        mtok[0] = v([sa], V.tensor_tensor, gm[:, 256:512], wy.indirect(offs(0, 1, 16, 16)), gb[:, 256:512], ALU.min)
+        for b in range(1, NB):
+            k = (b + 1) // 2
+            if first and b == 2:
+                l23 = lists([2, 3], 0, [("rep1", nfar), c0])
+                ready[2] = ready[3] = conv([2, 3], 0, l23)
+                score(0, 0, [mtok[0]], False, False)
+            if first and b == 5:
+                l45 = lists([4, 5], 1, [("rep2", nfar), c1])
+                ready[4] = ready[5] = conv([4, 5], 1, l45)
+            if first and b == 8:
+                l67 = lists([6, 7], 0, [("rep3", nfar), ready[2]])
+                for p in range(16):
+                    tl = mm([], T.pt[:, 0:32], T.wd[:, 15 - p:143 - p], T.mass[:, p:512:16], p == 0, p == 15)
+                ready[6] = ready[7] = conv([6, 7], 0, l67)
+                ct = v([tl], V.tensor_copy, T.offt[:], T.pt[:, 0:32])
+                mm([ready[4]], T.pl1[:], T.ll[:, 1, :], T.mass[:], True, True)
+                tabp = mm([ready[6]], T.pl0[:], T.ll[:, 0, :], T.mass[:], True, True)
+            gtok[b] = s([ready[k]], gb[:, 512 * b:512 * b + 512], wb.indirect(offs(b, 0)), ACT.Copy)
+            if first and b == 9:
+                t_s64 = s([p64], T.s64[:, 0:1], T.ps[:, 0:1], ACT.Copy)
+                t_col = s([], T.s64[:, 1:2], T.S[:, 64:65], ACT.Copy)
+            mtok[b] = v([gtok[b]], V.tensor_tensor, gm[:, 512 * b:512 * b + 512], wy.indirect(offs(b, 1)),
+                        gb[:, 512 * b:512 * b + 512], ALU.min)
+            if b == 1 and not first:
+                score(t, 0, [mtok[0]], False, False)
+            if b % 2 == 0 and k < 7:
+                ta, tb = score(t, k, [mtok[b]], k == 6 and not first, False)
+        if first:
+            tg = s([ct, t_col], T.gt[:], wb.indirect(T.offt[:]), ACT.Relu, bias=T.s64[:, 1:2], scale=-1.0)
+            mm([tg], PB[0][:, 0:32], T.blkp[:], T.gt[:, 64 * r + 32:64 * r + 64], False, False)
+            mm([], PB[0][:, 32:96], T.blkp[:], T.gt[:, 64 * src[7]:64 * src[7] + 64], False, False)
+            mm([], PA[0][:, 384:416], T.blkp[:], T.gt[:, 64 * r:64 * r + 32], False, False)
+            for k in range(1, 7):
+                ta = mm([], PA[0][:, 64 * (k - 1):64 * k], T.blkp[:], T.gt[:, 64 * src[k]:64 * src[k] + 64], False, k == 6)
+            s([tabp], T.tabs[:, 0:512], T.pl0[:], ACT.Copy)
+            t_tab = s([], T.tabs[:, 512:1024], T.pl1[:], ACT.Copy)
+        tx, tb = score(t, 7, [mtok[NB - 1]], False, True)
+        ka, kb = T.kab[:, 2 * t:2 * t + 1], T.kab[:, 2 * t + 1:2 * t + 2]
+        v([ta], V.tensor_reduce, ka, PA[t][:, 0:416], AxisListType.X, ALU.min)
+        x = v([tb], V.tensor_reduce, kb, PB[t][:, 0:96], AxisListType.X, ALU.min)
+        key, cand = T.ki[:, 2 * t:2 * t + 1], T.ki[:, 2 * t + 1:2 * t + 2]
+        if first:
+            x = v([x, t_s64], V.tensor_scalar, key, kb, ka, T.s64[:, 0:1], ALU.min, ALU.subtract)
+        else:
+            x = v([x], V.tensor_scalar, key, kb, ka, None, ALU.min)
+        x = v([x], V.tensor_scalar, cand, key, 511, None, ALU.bitwise_and)
+        x = v([x, t_half], V.tensor_scalar, T.woff[:, 2 * t:2 * t + 1], cand, T.half[:, 0:1], None, ALU.add)
+        x = v([x, t_tab], V.tensor_copy, T.zl[:, 16 * t:16 * t + 16], T.tabs[:, 0:1024].indirect(T.woff[:, 2 * t:2 * t + 1]))
+        x = v([x, t_zero], V.tensor_copy, wb.indirect(T.zl[:, 16 * t:16 * t + 1]), T.zero[:])
+        x = v([x], V.tensor_copy, wy.indirect(T.zl[:, 16 * t + 8:16 * t + 9]), T.zero[:])
+        sdeps = [x]
+
+    wait("y", sdeps)
+    g.sync.dma_start(T.left[:], T.S[:]).then_inc(sem.dleft, 16)
+    x = results(1)
+    wait("s", [x])
+    g.scalar.dma_start(T.win[:], T.res[0:128:16, 0:2]).then_inc(sem.dres, 16)
+    g.scalar.dma_start(T.score[:], T.res[0:128:16, 2:4]).then_inc(sem.dres, 16)
+    wait("g", [("sent", 4 * nfar + len(near)), ("qg", count["g"]), ("qp", count["p"]), ("qs", count["s"]),
+               ("qv", count["v"]), ("dres", 32), ("dleft", 16)])

@@ -3,22 +3,37 @@ from concourse.mybir import AluOpType, AxisListType, ActivationFunctionType
 
 N, KC, W = 8, 64, 3072
 NB = 15
+NC = 32 * NB
+CA = 352
 EARLY = 1024
+STAGE = (2, 5, 8)
+PAIRS = (6, 6)
+CLOSE = 3
+SPREAD = 0
+BIG = 1.5 * 2.0 ** 33
+KP, KS = max(PAIRS), 15 - 2 * min(PAIRS)
+C_B, C_Y, C_A, C_H, C_T, C_S = 0, 1, 2, 2 + KP, 2 + 2 * KP, 4 + 2 * KP
+NZ = C_S + KS
 
 BF, F32, I32, U16 = "bfloat16", "float32", "int32", "uint16"
-SCRATCH = {"lland": ("sbuf", [128, 7, 32], I32), "ll": ("sbuf", [128, 2, 128], BF), "lt": ("sbuf", [128, 2, NB, 128], BF)}
+SCRATCH = {"lland": ("sbuf", [128, 7, 32], I32), "ll": ("sbuf", [128, 2, 128], BF), "lt": ("sbuf", [128, 2, NB, 128], BF),
+           "off": ("sbuf", [128, 2, NC], U16), "u": ("sbuf", [128, 2, NC], F32), "u2": ("sbuf", [128, 2, NC], U16),
+           "fold": ("sbuf", [128, 2 * KP, NC], BF), "hit": ("sbuf", [128, 2 * KS + 4, NC], BF),
+           "px": ("psum", [128, 2, 512], F32)}
 for _name, _cols, _dt in [
         ("wants", 32, I32), ("loff", 32, U16), ("peps", W, BF), ("S", W, BF), ("gath", 448, BF), ("mass", 512, BF),
-        ("off", 960, U16), ("offt", 32, U16), ("gb0", 512 * NB, BF), ("gm0", 512 * NB, BF), ("gb1", 512 * NB, BF),
-        ("gm1", 512 * NB, BF), ("gt", 512, BF), ("tabs", 1024, F32), ("iw", 128, I32), ("iu", 128, I32), ("sg", 128, I32),
-        ("blk", 128, BF), ("blkn", 128, BF), ("blkp", 128, BF), ("ge", 128, BF), ("lbp", 128, BF), ("wd", 144, BF),
-        ("ones", 128, BF), ("lo", 448, BF), ("hi", 512, BF), ("zero", 16, BF), ("h8", 4, I32), ("half", 4, F32),
-        ("s64", 4, F32), ("kab", 4, F32), ("ki", 4, I32), ("woff", 4, U16), ("zl", 32, U16), ("res", 4, F32)]:
+        ("offt", 32, U16), ("gb", 512 * NB, BF), ("gm", 512 * NB, BF), ("gt", 512, BF), ("m0", NC, BF), ("m1", NC, BF),
+        ("iw", 128, I32), ("iu", 128, I32), ("sg", 128, I32), ("blk", 128, BF), ("blkn", 128, BF), ("blkp", 128, BF),
+        ("blkq", 128, BF), ("blkt", 128, BF), ("eye", 128, BF), ("eyen", 128, BF), ("ge", 128, BF), ("lbp", 128, BF),
+        ("wd", 144, BF), ("ones", 128, BF), ("lo", 448, BF), ("hi", 512, BF), ("zero", 16, BF), ("g16", 4, F32),
+        ("tri", 16, F32), ("coef", 32, BF), ("cz", 32, BF), ("nbig", 4, F32), ("wm", 32, BF), ("tabs", 1536, F32),
+        ("dist", 32, F32), ("mid", 8, F32), ("hh", 8, BF), ("dhi", 16, BF), ("dlo", 16, BF), ("s64", 4, F32),
+        ("kab", 8, F32), ("woff", 8, U16), ("zl", 32, U16), ("res", 4, F32)]:
     SCRATCH[_name] = ("sbuf", [128, _cols], _dt)
-for _name in ["pl0", "pl1", "pa0", "pb0", "pa1", "pb1", "pt", "ps"]:
+for _name in ["ma", "mb", "pa", "pb", "pt", "pz"]:
     SCRATCH[_name] = ("psum", [128, 512], F32)
-SEMAPHORES = ["qv", "qs", "qp", "qg", "dwant", "dpep", "dsa", "dsb", "dleft", "dres",
-              "lnear", "lfar", "sent_near", "sent", "rep0", "rep1", "rep2", "rep3"]
+SEMAPHORES = ["qv", "qs", "qp", "qg", "dwant", "dpep", "dsa", "dsb", "dleft", "dres", "go",
+              "lnear", "lfar", "sent", "rep0", "rep1", "rep2", "rep3"]
 
 ALU = AluOpType
 ACT = ActivationFunctionType
@@ -92,77 +107,96 @@ def rank_program(g, core, T, topo):
     g.remote_dma_fused([RemoteDMATransfer(
         dst_ids=[DstId(rid=addr[k][0], pnc=addr[k][1]) for k in range(1, 7)], dma_engine_mask=bits(far),
         remote_sem=sem.lfar, src=T.wants[:], dsts=[T.lland[:, place[k], :] for k in range(1, 7)])], local_sem=sem.sent)
-    g.remote_dma(T.lland[:, place[0], :], T.wants[:], sem.lnear, sem.sent_near, addr[0][1], addr[0][0], bits(near))
-    t_lo = op("g", [], g.iota, T.lo[0:1, :], [[0, 7], [1, 64]], 0, 0, allow_small_or_imprecise_dtypes=True)
-    wait("y", [("sent_near", len(near))])
+    g.remote_dma(T.lland[:, place[0], :], T.wants[:], sem.lnear, sem.sent, addr[0][1], addr[0][0], bits(near))
+    g.sem_inc(sem.go, 1)
+    t_lo = op("g", [], g.iota, T.lo[0:1, :], [[0, 7], [-1, 64]], 0, 0, allow_small_or_imprecise_dtypes=True)
+    wait("y", [("go", 1)])
     g.sync.dma_start(T.S[:, EARLY:W], T.spec[:, EARLY:W]).then_inc(sem.dsb, 16)
 
     t_lt0 = v([], V.memset, T.lt[:], 0.0)
     t_wd0 = v([], V.memset, T.wd[:], 0.0)
-    t_zero = v([], V.memset, T.zero[:], 0.0)
-    v([], V.memset, T.ones[0:1, :], 1.0)
-    for k in range(1, 7):
-        v([], V.memset, T.hi[0:1, 64 * (k - 1):64 * k], float(64 * src[k]))
-    v([], V.memset, T.hi[0:1, 384:448], float(64 * r))
-    t_hi = v([], V.memset, T.hi[0:1, 448:512], float(64 * src[7]))
     t_sg = v([t_iw], V.tensor_scalar, T.sg[:], T.iw[:], 4, None, ALU.arith_shift_right)
-    t_h8 = v([], V.tensor_scalar, T.h8[:, 0:1], T.iw[:, 0:1], 8, None, ALU.bitwise_and)
     t_ge = v([t_iu], V.tensor_scalar, T.ge[:], T.iu[:], 0.0, None, ALU.is_ge)
     t_own = v([WANT], V.tensor_copy, T.loff[:, 0:4], T.wants[:, 4 * r:4 * r + 4])
     t_blk = v([t_sg], V.tensor_scalar, T.blk[:], T.sg[:], 0.0, None, ALU.is_equal)
-    v([], V.tensor_scalar, T.blkn[:], T.sg[:], 0.0, -512.0, ALU.is_equal, ALU.mult)
-    v([], V.tensor_scalar, T.blkp[:], T.sg[:], 0.0, 512.0, ALU.is_equal, ALU.mult)
+    t_g16 = v([], V.tensor_scalar, T.g16[:, 0:1], T.sg[:, 0:1], -16.0, None, ALU.mult)
     t_lb = v([t_ge, t_blk], V.tensor_tensor, T.ll[:, 0, :], T.ge[:], T.blk[:], ALU.mult)
     t_wd = v([t_wd0], V.tensor_copy, T.wd[:, 15:128:16], T.blk[:, 15:128:16])
-    t_half = v([t_h8], V.tensor_scalar, T.half[:, 0:1], T.h8[:, 0:1], -64.0, 512.0, ALU.mult, ALU.add)
+    t_tri = v([t_g16], V.tensor_scalar, T.tri[:], T.iu[:, 0:16], T.g16[:, 0:1], 0.0, ALU.add, ALU.is_ge)
     t_ly = v([t_lb], V.tensor_tensor, T.ll[:, 1, :], T.blk[:], T.ll[:, 0, :], ALU.subtract)
     v([t_wd], V.tensor_tensor, T.lbp[:], T.ll[:, 0, :], T.wd[:, 0:128], ALU.subtract)
     for gg in range(8):
         t_const = v([t_ly, t_lt0], V.tensor_copy, T.lt[:, :, :, 16 * gg + 15], T.ll[:, :, 16 * gg:16 * gg + 15])
+    t_eye = v([], V.tensor_scalar, T.eye[:], T.iu[:], 0.0, None, ALU.is_equal)
+    t_blkp = s([t_blk], T.blkp[:], T.blk[:], ACT.Copy, scale=1024.0)
+    s([], T.blkn[:], T.blk[:], ACT.Copy, scale=-1024.0)
+    t_blkq = s([t_blkp, t_tri], T.blkq[:], T.blkp[:], ACT.Copy, scale=T.tri[:, 14:15])
 
-    PA, PB = [T.pa0, T.pa1], [T.pb0, T.pb1]
-    for t in range(2):
-        mm([t_lo, t_hi], PA[t][:, 0:416], T.ones[0:1, :], T.lo[0:1, 0:416], True, False)
-        mm([], PA[t][:, 0:416], T.ones[0:1, :], T.hi[0:1, 0:416], False, False)
-        mm([], PB[t][:, 0:96], T.ones[0:1, :], T.lo[0:1, 32:128], True, False)
-        mm([], PB[t][:, 0:96], T.ones[0:1, :], T.hi[0:1, 416:512], False, False)
+    def constants_of_scores():
+        v([], V.memset, T.ones[0:1, :], 1.0)
+        for k in range(1, 6):
+            v([], V.memset, T.hi[0:1, 64 * (k - 1):64 * k], float(-64 * src[k]))
+        v([], V.memset, T.hi[0:1, 320:384], float(-64 * r))
+        v([], V.memset, T.hi[0:1, 384:448], float(-64 * src[6]))
+        v([], V.memset, T.hi[0:1, 448:512], float(-64 * src[7]))
+        return v([t_blkq], V.tensor_tensor, T.blkt[:], T.blkp[:], T.blkq[:], ALU.subtract)
+
+    def constants_of_round_1():
+        x = v([], V.memset, T.coef[:], 0.5)
+        v([], V.memset, T.zero[:], 0.0)
+        v([], V.memset, T.nbig[:, 0:2], -BIG)
+        v([], V.tensor_scalar, T.nbig[:, 2:3], T.tri[:, 7:8], -1024.0, 1024.0 - BIG, ALU.mult, ALU.add)
+        for lo, hi, val in [(C_B, C_Y, 32.0), (C_Y, C_H, -32.0), (C_H, C_T + 1, 0.0), (C_T + 1, NZ, -64.0)]:
+            v([], V.memset, T.cz[0:1, lo:hi], val)
+        even, odd = T.tri[:, 0:2 * KP:2], T.tri[:, 1:2 * KP:2]
+        v([x], V.memset, T.coef[:, C_T:C_S], 1.0)
+        v([], V.tensor_tensor, T.mid[:, 0:KP], odd, even, ALU.add)
+        x = v([], V.tensor_tensor, T.hh[:, 0:KP], odd, even, ALU.subtract)
+        v([], V.tensor_scalar, T.coef[:, C_S:NZ], T.tri[:, 15 - KS:15], 2.0, -1.0, ALU.mult, ALU.add)
+        v([x], V.tensor_scalar, T.coef[:, C_A:C_H], T.mid[:, 0:KP], 0.5, -0.5, ALU.mult, ALU.add)
+        return v([], V.tensor_scalar, T.coef[:, C_H:C_T], T.hh[:, 0:KP], 0.5, None, ALU.mult)
+
+    def numbers(deps):
+        mm(deps, T.pa[:, 0:352], T.ones[0:1, :], T.lo[0:1, 0:352], True, False)
+        mm([], T.pa[:, 0:352], T.ones[0:1, :], T.hi[0:1, 0:352], False, False)
+        mm([], T.pb[:, 0:160], T.ones[0:1, :], T.lo[0:1, 32:192], True, False)
+        mm([], T.pb[:, 0:160], T.ones[0:1, :], T.hi[0:1, 352:512], False, False)
+
+    def bank(k):
+        return T.pa[:, 320:352] if k == 0 else T.pa[:, 64 * (k - 1):64 * k] if k < 6 else T.pb[:, 64 * k - 352:64 * k - 288]
 
     pepw = T.peps[:, 0:W]
     mine = T.mass[:, 64 * r:64 * r + 64]
     tail = T.mass[:, 64 * r + 32:64 * r + 64]
     t_mine = s([t_own, PEP], mine, pepw.indirect(T.loff[:, 0:4]), ACT.Copy)
+    t_blkt = constants_of_scores()
     t_cn = v([("lnear", len(near))], V.tensor_copy, T.loff[:, 4:8], T.lland[:, 0, 4 * r:4 * r + 4])
     t_gn = s([t_cn], T.gath[:, 0:64], pepw.indirect(T.loff[:, 4:8]), ACT.Copy)
     wait("g", [t_gn])
     g.remote_dma(mine, T.gath[:, 0:64], sem.rep0, sem.sent, addr[0][1], addr[0][0], bits(near))
 
-    PL = [T.pl0, T.pl1]
-
-    def obase(k):
-        return 0 if k == 0 else 64 + 128 * (k - 1)
-
     def blocks(k):
         return [0] if k == 0 else [2 * k - 1, 2 * k]
 
-    def lists(ks, bank, deps):
-        o = 0
+    def cols(ks):
+        return 32 * blocks(ks[0])[0], 32 * blocks(ks[-1])[-1] + 32
+
+    def lists(ks, deps):
         for k in ks:
-            n = 32 * len(blocks(k))
-            rhs = T.mass[:, 64 * src[k]:64 * src[k] + n]
+            lo, hi = cols([k])
+            rhs = T.mass[:, 64 * src[k]:64 * src[k] + hi - lo]
             for side in range(2):
-                mm(deps, PL[bank][:, o:o + n], T.lbp[:] if side == 0 else T.ll[:, 1, :], rhs, True, False)
-                for h, b in enumerate(blocks(k)):
-                    tok = mm([], PL[bank][:, o + 32 * h:o + 32 * h + 32], T.lt[:, side, b, :], tail, False,
-                             h == len(blocks(k)) - 1)
-                o += n
-        return tok, o
+                mm(deps, T.px[:, side, lo:hi], T.lbp[:] if side == 0 else T.ll[:, 1, :], rhs, True, False)
+                for b in blocks(k):
+                    tok = mm([], T.px[:, side, 32 * b:32 * b + 32], T.lt[:, side, b, :], tail, False, b == blocks(k)[-1])
+        return tok
 
-    def conv(ks, bank, made):
-        tok, n = made
-        return v([tok], V.tensor_copy, T.off[:, obase(ks[0]):obase(ks[0]) + n], PL[bank][:, 0:n])
+    def conv(ks, tok):
+        lo, hi = cols(ks)
+        return v([tok], V.tensor_copy, T.off[:, :, lo:hi], T.px[:, :, lo:hi])
 
-    l0 = lists([0], 0, [t_mine, t_const])
-    c0 = conv([0], 0, l0)
+    c0 = conv([0], lists([0], [t_mine, t_const]))
+    s([t_eye], T.eyen[:], T.eye[:], ACT.Copy, scale=-256.0)
     nfar = len(far)
     t_cf = v([("lfar", 6 * nfar)], V.tensor_copy, T.loff[:, 8:32], T.lland[:, 1:7, 4 * r:4 * r + 4])
     back = [v([t_cf, PEP], V.tensor_copy, T.gath[:, 64:192], pepw.indirect(T.loff[:, 8:16])),
@@ -175,104 +209,201 @@ def rank_program(g, core, T, topo):
             dst_ids=[DstId(rid=addr[k][0], pnc=addr[k][1])], dma_engine_mask=bits(far[hf * h:hf * h + hf]),
             remote_sem=sem["rep%d" % (j + 1)], src=T.gath[:, 64 * k:64 * k + 64], dst=mine)
             for h, k in enumerate((2 * j + 1, 2 * j + 2))], local_sem=sem.sent)
-    l1 = lists([1], 1, [("rep0", len(near))])
-    c1 = conv([1], 1, l1)
+    t_gap = op("g", [], g.iota, T.tabs[:, 512:1024], [[0, 512]], 0, 0, allow_small_or_imprecise_dtypes=True)
+    numbers([t_lo, t_blkt])
+    t_cz = constants_of_round_1()
+    c1 = conv([1], lists([1], [("rep0", len(near)), c0]))
     ready = {0: c0, 1: c1}
 
     wb, wy = T.S[:, 0:W], T.S[:, 64:W]
+    gb, gm = T.gb, T.gm
 
     def offs(b, side, lo=0, n=32):
-        k = (b + 1) // 2
-        o = obase(k) + (32 * side if k == 0 else 64 * side + 32 * (b - (2 * k - 1))) + lo
-        return T.off[:, o:o + n]
+        return T.off[:, side, 32 * b + lo:32 * b + lo + n]
 
-    def score(t, k, deps, stop_a, stop_b):
-        gm = T["gm%d" % t]
-        bs = blocks(k)
-        n = 32 * len(bs)
-        out = PA[t][:, 384:416] if k == 0 else PB[t][:, 32:96] if k == 7 else PA[t][:, 64 * (k - 1):64 * k]
-        for i in range(15):
-            tok = mm(deps, out, T.blkn[:], gm[:, 512 * bs[0] + i:512 * bs[0] + 16 * n:16], False, stop_a and i == 14)
-        ta = tok
+    def slot(k, i):
+        lo, hi = cols([k])
+        return gm[:, 16 * lo + i:16 * hi:16]
+
+    def compact(k, M, deps):
+        lo, hi = cols([k])
+        for i in range(16):
+            tok = mm(deps, M[:, lo:hi], T.wd[:, 15 - i:143 - i], slot(k, i), i == 0, i == 15)
+        return tok
+
+    def keep(ks, M, deps):
+        lo, hi = cols(ks)
+        return s(deps, T.m0[:, lo:hi], M[:, lo:hi], ACT.Copy)
+
+    def score(m, ks, deps, stop_a=False, stop_b=False):
+        runs = [[k for k in ks if k == 0], [k for k in ks if 0 < k < 6], [k for k in ks if k >= 6]]
+        ta = None
+        for j, run in enumerate(runs):
+            if run:
+                lo, hi = cols(run)
+                out = bank(0) if j == 0 else T.pa[:, lo - 32:hi - 32] if j == 1 else T.pb[:, lo - 320:hi - 320]
+                tok = mm(deps, out, T.blkq[:], m[:, lo:hi], False, stop_a and j == 1)
+                ta = tok if j == 1 else ta
+        bs = [b for k in ks for b in blocks(k)]
         for b in bs:
-            tok = mm([], PB[t][:, 0:32], T.blkn[:], gm[:, 512 * b + 15:512 * b + 512:16], False, stop_b and b == bs[-1])
+            tok = mm([], T.pb[:, 0:32], T.blkt[:], m[:, 32 * b:32 * b + 32], False, stop_b and b == bs[-1])
         return ta, tok
 
-    def results(t):
-        y = v([], V.tensor_copy, T.res[:, t:t + 1], T.ki[:, 2 * t + 1:2 * t + 2])
-        return v([y], V.tensor_scalar, T.res[:, 2 + t:3 + t], T.ki[:, 2 * t:2 * t + 1], T.res[:, t:t + 1],
-                 -1.0 / 512, ALU.subtract, ALU.mult)
+    def best(t, half, deps):
+        return v(deps, V.tensor_reduce, T.kab[:, 4 * t + half:4 * t + half + 1], T.pb[:, 0:160] if half else T.pa[:, 0:352],
+                 AxisListType.X, ALU.max)
 
-    sdeps = SPEC
-    for t in range(2):
-        gb, gm = T["gb%d" % t], T["gm%d" % t]
-        first = t == 0
-        gtok, mtok = {}, {}
-        va = v(sdeps + [c0], V.tensor_copy, gb[:, 0:256], wb.indirect(offs(0, 0, 0, 16)))
-        sa = s(sdeps + [c0], gb[:, 256:512], wb.indirect(offs(0, 0, 16, 16)), ACT.Copy)
-        if first:
-            p64 = mm(SPEC, T.ps[:, 0:2], T.blkp[:], T.S[:, 64:66], True, True)
-        else:
-            results(0)
-        v([va], V.tensor_tensor, gm[:, 0:256], wy.indirect(offs(0, 1, 0, 16)), gb[:, 0:256], ALU.min)
-        mtok[0] = v([sa], V.tensor_tensor, gm[:, 256:512], wy.indirect(offs(0, 1, 16, 16)), gb[:, 256:512], ALU.min)
-        for b in range(1, NB):
-            k = (b + 1) // 2
-            if first and b == 2:
-                l23 = lists([2, 3], 0, [("rep1", nfar), c0])
-                ready[2] = ready[3] = conv([2, 3], 0, l23)
-                score(0, 0, [mtok[0]], False, False)
-            if first and b == 5:
-                l45 = lists([4, 5], 1, [("rep2", nfar), c1])
-                ready[4] = ready[5] = conv([4, 5], 1, l45)
-            if first and b == 8:
-                l67 = lists([6, 7], 0, [("rep3", nfar), ready[2]])
-                for p in range(16):
-                    tl = mm([], T.pt[:, 0:32], T.wd[:, 15 - p:143 - p], T.mass[:, p:512:16], p == 0, p == 15)
-                ready[6] = ready[7] = conv([6, 7], 0, l67)
-                ct = v([tl], V.tensor_copy, T.offt[:], T.pt[:, 0:32])
-                mm([ready[4]], T.pl1[:], T.ll[:, 1, :], T.mass[:], True, True)
-                tabp = mm([ready[6]], T.pl0[:], T.ll[:, 0, :], T.mass[:], True, True)
-            gtok[b] = s([ready[k]], gb[:, 512 * b:512 * b + 512], wb.indirect(offs(b, 0)), ACT.Copy)
-            if first and b == 9:
-                t_s64 = s([p64], T.s64[:, 0:1], T.ps[:, 0:1], ACT.Copy)
-                t_col = s([], T.s64[:, 1:2], T.S[:, 64:65], ACT.Copy)
-            mtok[b] = v([gtok[b]], V.tensor_tensor, gm[:, 512 * b:512 * b + 512], wy.indirect(offs(b, 1)),
-                        gb[:, 512 * b:512 * b + 512], ALU.min)
-            if b == 1 and not first:
-                score(t, 0, [mtok[0]], False, False)
-            if b % 2 == 0 and k < 7:
-                ta, tb = score(t, k, [mtok[b]], k == 6 and not first, False)
-        if first:
-            tg = s([ct, t_col], T.gt[:], wb.indirect(T.offt[:]), ACT.Relu, bias=T.s64[:, 1:2], scale=-1.0)
-            mm([tg], PB[0][:, 0:32], T.blkp[:], T.gt[:, 64 * r + 32:64 * r + 64], False, False)
-            mm([], PB[0][:, 32:96], T.blkp[:], T.gt[:, 64 * src[7]:64 * src[7] + 64], False, False)
-            mm([], PA[0][:, 384:416], T.blkp[:], T.gt[:, 64 * r:64 * r + 32], False, False)
-            for k in range(1, 7):
-                ta = mm([], PA[0][:, 64 * (k - 1):64 * k], T.blkp[:], T.gt[:, 64 * src[k]:64 * src[k] + 64], False, k == 6)
-            s([tabp], T.tabs[:, 0:512], T.pl0[:], ACT.Copy)
-            t_tab = s([], T.tabs[:, 512:1024], T.pl1[:], ACT.Copy)
-        tx, tb = score(t, 7, [mtok[NB - 1]], False, True)
-        ka, kb = T.kab[:, 2 * t:2 * t + 1], T.kab[:, 2 * t + 1:2 * t + 2]
-        v([ta], V.tensor_reduce, ka, PA[t][:, 0:416], AxisListType.X, ALU.min)
-        x = v([tb], V.tensor_reduce, kb, PB[t][:, 0:96], AxisListType.X, ALU.min)
-        key, cand = T.ki[:, 2 * t:2 * t + 1], T.ki[:, 2 * t + 1:2 * t + 2]
-        if first:
-            x = v([x, t_s64], V.tensor_scalar, key, kb, ka, T.s64[:, 0:1], ALU.min, ALU.subtract)
-        else:
-            x = v([x], V.tensor_scalar, key, kb, ka, None, ALU.min)
-        x = v([x], V.tensor_scalar, cand, key, 511, None, ALU.bitwise_and)
-        x = v([x, t_half], V.tensor_scalar, T.woff[:, 2 * t:2 * t + 1], cand, T.half[:, 0:1], None, ALU.add)
-        x = v([x, t_tab], V.tensor_copy, T.zl[:, 16 * t:16 * t + 16], T.tabs[:, 0:1024].indirect(T.woff[:, 2 * t:2 * t + 1]))
-        x = v([x, t_zero], V.tensor_copy, wb.indirect(T.zl[:, 16 * t:16 * t + 1]), T.zero[:])
-        x = v([x], V.tensor_copy, wy.indirect(T.zl[:, 16 * t + 8:16 * t + 9]), T.zero[:])
-        sdeps = [x]
+    def winner(t, deps, lo, hi):
+        ka, kb, key, up = [T.kab[:, 4 * t + j:4 * t + j + 1] for j in range(4)]
+        v(deps, V.tensor_scalar, up, kb, ka, BIG, ALU.max, ALU.add)
+        y = v([], V.tensor_scalar, key, kb, ka, None, ALU.max)
+        return y, v([y], V.tensor_scalar, T.woff[:, 4 * t:4 * t + hi - lo], T.nbig[:, lo:hi], up, key, ALU.add, ALU.subtract)
 
-    wait("y", sdeps)
+    def clear(t, off, deps):
+        x = v(deps, V.tensor_copy, T.zl[:, 16 * t:16 * t + 16], T.tabs[:, 0:1536].indirect(off))
+        x = v([x], V.tensor_copy, wb.indirect(T.zl[:, 16 * t:16 * t + 1]), T.zero[:])
+        return v([x], V.tensor_copy, wy.indirect(T.zl[:, 16 * t + 8:16 * t + 9]), T.zero[:])
+
+    M = {0: T.ma, 1: T.ma, 2: T.mb, 3: T.mb, 4: T.ma, 5: T.ma, 6: T.mb, 7: T.ma}
+    mtok, ctok, ktok = {}, {}, {}
+    va = v(SPEC + [c0], V.tensor_copy, gb[:, 0:256], wb.indirect(offs(0, 0, 0, 16)))
+    sa = s(SPEC + [c0], gb[:, 256:512], wb.indirect(offs(0, 0, 16, 16)), ACT.Copy)
+    made = lists([2, 3], [("rep1", nfar), c1])
+    p64 = mm(SPEC, T.pt[:, 0:2], T.blk[:], T.S[:, 64:66], True, True)
+    v([va], V.tensor_tensor, gm[:, 0:256], wy.indirect(offs(0, 1, 0, 16)), gb[:, 0:256], ALU.min)
+    mtok[0] = v([sa], V.tensor_tensor, gm[:, 256:512], wy.indirect(offs(0, 1, 16, 16)), gb[:, 256:512], ALU.min)
+    for b in range(1, NB):
+        k = (b + 1) // 2
+        if b == STAGE[0]:
+            ready[2] = ready[3] = conv([2, 3], made)
+            made = lists([4, 5], [("rep2", nfar), ready[2]])
+        if b == STAGE[1]:
+            ready[4] = ready[5] = conv([4, 5], made)
+            made = lists([6, 7], [("rep3", nfar), ready[4]])
+            for p in range(16):
+                tl = mm([t_s64], T.pt[:, 0:32], T.wd[:, 15 - p:143 - p], T.mass[:, p:512:16], p == 0, p == 15)
+        if b == STAGE[2]:
+            ready[6] = ready[7] = conv([6, 7], made)
+            ct = v([tl], V.tensor_copy, T.offt[:], T.pt[:, 0:32])
+            mm([], T.pz[:], T.ll[:, 1, :], T.mass[:], True, True)
+            tabp = mm([ct], T.pt[:], T.ll[:, 0, :], T.mass[:], True, True)
+        if b == 2:
+            compact(0, M[0], [mtok[0]])
+        if b == 3:
+            t_s64 = s([p64], T.s64[:, 0:1], T.pt[:, 0:1], ACT.Identity, bias=-BIG / 1024)
+            t_col = s([], T.s64[:, 1:2], T.S[:, 64:65], ACT.Copy)
+        if b in (6, 10, 14):
+            ks = [b // 2 - 3, b // 2 - 2]
+            ktok[ks[1]] = keep(ks, M[ks[0]], [ctok[ks[1]]])
+        gtok = s([ready[k]], gb[:, 512 * b:512 * b + 512], wb.indirect(offs(b, 0)), ACT.Copy)
+        mtok[b] = v([gtok], V.tensor_tensor, gm[:, 512 * b:512 * b + 512], wy.indirect(offs(b, 1)),
+                    gb[:, 512 * b:512 * b + 512], ALU.min)
+        if b in (6, 10, 14):
+            score(T.m0, ks, [ktok[ks[1]], t_blkt])
+        if b % 2 == 0 and k < 7:
+            ctok[k] = compact(k, M[k], [mtok[b]] + ([ktok[k - 3]] if k in (4, 6) else []))
+    k6 = keep([6], M[6], [ctok[6]])
+    tg = s([ct, t_col], T.gt[:], wb.indirect(T.offt[:]), ACT.Relu, bias=T.s64[:, 1:2], scale=-1.0)
+    s([tabp], T.tabs[:, 0:512], T.pt[:], ACT.Copy)
+    t_tab = s([], T.tabs[:, 1024:1536], T.pz[:], ACT.Copy)
+    score(T.m0, [6], [k6])
+    mm([tg], bank(0), T.blkn[:], T.gt[:, 64 * r:64 * r + 32], False, False)
+    for k in range(1, 6):
+        ta = mm([], bank(k), T.blkn[:], T.gt[:, 64 * src[k]:64 * src[k] + 64], False, k == 5)
+    mm([], T.pb[:, 0:32], T.blkn[:], T.gt[:, 64 * r + 32:64 * r + 64], False, False)
+    for k in (6, 7):
+        mm([], bank(k), T.blkn[:], T.gt[:, 64 * src[k]:64 * src[k] + 64], False, False)
+    for i in range(15):
+        mm([mtok[14]], bank(7), T.blkp[:], slot(7, i), False, False)
+    for b in blocks(7):
+        tb = mm([], T.pb[:, 0:32], T.blkp[:], gm[:, 512 * b + 15:512 * b + 512:16], False, b == 14)
+    k7 = keep([7], M[7], [compact(7, M[7], [ktok[5]])])
+    mm([t_cz, t_tab], T.pz[:, 0:NZ], T.ones[0:1, :], T.cz[0:1, 0:NZ], True, False)
+    best(0, 0, [ta])
+    e64 = v([], V.tensor_scalar, T.hit[:, 0, :], T.off[:, 0, :], 64.0, None, ALU.is_equal)
+    red0 = best(0, 1, [tb])
+    off0 = winner(0, [red0], 0, 3)[1]
+
+    x = v([off0], V.tensor_tensor, T.wm[:], T.mass[:, 0:512].indirect(T.woff[:, 0:2]), T.coef[:], ALU.mult)
+    z = mm([x], T.pz[:, 0:NZ], T.blk[:], T.wm[:, 0:NZ], False, True)
+    t_d = s([z], T.dist[:, 0:NZ], T.pz[:, 0:NZ], ACT.Abs)
+    t_u = [s([t_d], T.u[:, side, :], T.px[:, side, 0:NC], ACT.Abs, bias=T.dist[:, side:side + 1], scale=-1.0)
+           for side in range(2)]
+    PART = [(0, CA, T.ma), (CA, NC, T.mb)]
+    for lo, hi, bk in PART:
+        mm([k7], bk[:, lo:hi], T.eye[:], T.m0[:, lo:hi], True, False)
+        mm([e64], bk[:, lo:hi], T.eyen[:], T.hit[:, 0, lo:hi], False, False)
+    numbers([red0])
+    clear(0, T.woff[:, 2:3], [t_tab, t_gap])
+    x = v([t_d], V.tensor_copy, T.dhi[:, 0:KS + 2], T.dist[:, C_T:NZ])
+    v([], V.tensor_tensor, T.mid[:, 0:KP], T.dist[:, C_A:C_H], T.dist[:, C_H:C_T], ALU.max)
+    t_h = v([], V.tensor_tensor, T.hh[:, 0:KP], T.dist[:, C_A:C_H], T.dist[:, C_H:C_T], ALU.min)
+    x = v([x], V.tensor_tensor, T.dlo[:, 0:KS + 2], T.dist[:, C_T:NZ], T.dhi[:, 0:KS + 2], ALU.subtract)
+
+    def lose(buf, j, part, deps, stop=False):
+        lo, hi, bk = part
+        for side in range(2):
+            tok = mm(deps, bk[:, lo:hi], T.eyen[:], buf[:, 2 * j + side, lo:hi], False, stop and side == 1)
+        return tok
+
+    for side in range(2):
+        y = v([x], V.tensor_scalar, T.hit[:, 2 + side, :], T.off[:, side, :], T.dhi[:, side:side + 1],
+              T.dlo[:, side:side + 1], ALU.subtract, ALU.is_equal)
+    for part in PART:
+        lose(T.hit, 1, part, [y])
+    for side in range(2):
+        t_u2 = v([t_u[side]], V.tensor_scalar, T.u2[:, side, :], T.u[:, side, :], 2.0, None, ALU.mult)
+
+    def single(j, part, stop=False):
+        lo, hi, bk = part
+        x = v([t_u2], V.tensor_scalar, T.hit[:, 2 * j + 4:2 * j + 6, lo:hi], T.u2[:, :, lo:hi],
+              T.dhi[:, j + 2:j + 3], T.dlo[:, j + 2:j + 3], ALU.subtract, ALU.is_equal)
+        return lose(T.hit, j + 2, part, [x], stop)
+
+    def pair(p, part, stop=False):
+        lo, hi, bk = part
+        f = T.fold[:, 2 * p:2 * p + 2, lo:hi]
+        x = s([t_u[1], t_h], f, T.u[:, :, lo:hi], ACT.Abs, bias=T.mid[:, p:p + 1], scale=-1.0)
+        x = v([x], V.tensor_scalar, f, f, T.hh[:, p:p + 1], None, ALU.is_equal)
+        return lose(T.fold, p, part, [x], stop)
+
+    A, B = PART
+    singles = [[j for j in range(KS) if 15 - KS + j >= 2 * kp] for kp in PAIRS]
+    todo = [(j, A) for j in singles[0]] + [(j, B) for j in singles[1]]
+    for p in range(PAIRS[0]):
+        for j, part in todo[len(todo) * p // PAIRS[0]:len(todo) * (p + 1) // PAIRS[0]]:
+            single(j, part)
+        done = pair(p, A, p == PAIRS[0] - 1)
+    rest = []
+    for p in range(PAIRS[1]):
+        if p == CLOSE:
+            x = v([done], V.tensor_scalar, T.m1[:, 0:CA], T.ma[:, 0:CA], 0.0, None, ALU.max)
+        last = pair(p, B, p == PAIRS[1] - 1)
+        if p == CLOSE:
+            mm([x], bank(0), T.blkq[:], T.m1[:, 0:32], False, False)
+            ta = mm([], T.pa[:, 0:CA - 32], T.blkq[:], T.m1[:, 32:CA], False, True)
+            rest = list(range(CA // 32))
+        n = len(rest) if p == PAIRS[1] - 1 else min(len(rest), SPREAD)
+        for b in rest[:n]:
+            mm([], T.pb[:, 0:32], T.blkt[:], T.m1[:, 32 * b:32 * b + 32], False, False)
+        rest = rest[n:]
+    x = s([last], T.m1[:, CA:NC], T.mb[:, CA:NC], ACT.Relu)
+    tb = score(T.m1, [6, 7], [x], stop_b=True)[1]
+    best(1, 0, [ta])
+    key, up = T.kab[:, 2:3], T.kab[:, 3:4]
+    v([], V.tensor_scalar, T.res[:, 0:1], T.nbig[:, 0:1], up, key, ALU.add, ALU.subtract)
+    res0 = v([t_s64], V.tensor_scalar, T.res[:, 2:3], up, 1.0 / 1024, T.s64[:, 0:1], ALU.mult, ALU.add)
+    key1, off1 = winner(1, [best(1, 1, [tb])], 2, 3)
+    gone = clear(1, T.woff[:, 4:5], [off1])
+
+    wait("y", [gone])
     g.sync.dma_start(T.left[:], T.S[:]).then_inc(sem.dleft, 16)
-    x = results(1)
+    key, up = T.kab[:, 6:7], T.kab[:, 7:8]
+    x = s([key1, res0], T.s64[:, 2:3], up, ACT.Identity, bias=-BIG)
+    s([x], T.res[:, 1:2], key, ACT.Identity, bias=T.s64[:, 2:3], scale=-1.0)
+    x = s([], T.res[:, 3:4], T.s64[:, 2:3], ACT.Copy, scale=1.0 / 1024)
     wait("s", [x])
     g.scalar.dma_start(T.win[:], T.res[0:128:16, 0:2]).then_inc(sem.dres, 16)
     g.scalar.dma_start(T.score[:], T.res[0:128:16, 2:4]).then_inc(sem.dres, 16)
-    wait("g", [("sent", 4 * nfar + len(near)), ("qg", count["g"]), ("qp", count["p"]), ("qs", count["s"]),
+    wait("g", [("sent", 4 * nfar + 2 * len(near)), ("qg", count["g"]), ("qp", count["p"]), ("qs", count["s"]),
                ("qv", count["v"]), ("dres", 32), ("dleft", 16)])

@@ -2,38 +2,44 @@ from concourse.bass import DstId, RemoteDMATransfer
 from concourse.mybir import AluOpType, AxisListType, ActivationFunctionType
 
 N, KC, W = 8, 64, 3072
-NB = 15
-NC = 32 * NB
-CA = 352
-EARLY = 1024
-STAGE = (2, 5, 8)
-PAIRS = (6, 6)
+NT = 28
+COL = [0, 64, 100, 164, 228, 292, 356, 420, 484]
+NC, CA = COL[8], COL[6]
+NBK = NT + NC - CA
+HALF = 1536
+OWN, NEAR, CONV2 = 32, (64, 82, 100), 0
+EDGE = [100, 132, 164, 196, 228, 260, 292, 324, 356, 388, 420, 452, 484]
+MADE = (0, 3)
+STAGE = (2, 6)
+KEEP = (3, 7, 11)
+KP, KS = 6, 3
 CLOSE = 3
-SPREAD = 0
 BIG = 1.5 * 2.0 ** 33
-KP, KS = max(PAIRS), 15 - 2 * min(PAIRS)
-C_B, C_Y, C_A, C_H, C_T, C_S = 0, 1, 2, 2 + KP, 2 + 2 * KP, 4 + 2 * KP
-NZ = C_S + KS
+C_H, C_A, C_S = 0, KP, 2 * KP
+C_Y = C_S + KS
+C_T, C_B, NZ = C_Y + 1, C_Y + 2, C_Y + 3
 
 BF, F32, I32, U16 = "bfloat16", "float32", "int32", "uint16"
-SCRATCH = {"lland": ("sbuf", [128, 7, 32], I32), "ll": ("sbuf", [128, 2, 128], BF), "lt": ("sbuf", [128, 2, NB, 128], BF),
+SCRATCH = {"ll": ("sbuf", [128, 2, 8, 16], BF), "lt": ("sbuf", [128, 2, 128, 15], BF),
            "off": ("sbuf", [128, 2, NC], U16), "u": ("sbuf", [128, 2, NC], F32), "u2": ("sbuf", [128, 2, NC], U16),
            "fold": ("sbuf", [128, 2 * KP, NC], BF), "hit": ("sbuf", [128, 2 * KS + 4, NC], BF),
            "px": ("psum", [128, 2, 512], F32)}
 for _name, _cols, _dt in [
-        ("wants", 32, I32), ("loff", 32, U16), ("peps", W, BF), ("S", W, BF), ("gath", 448, BF), ("mass", 512, BF),
-        ("offt", 32, U16), ("gb", 512 * NB, BF), ("gm", 512 * NB, BF), ("gt", 512, BF), ("m0", NC, BF), ("m1", NC, BF),
-        ("iw", 128, I32), ("iu", 128, I32), ("sg", 128, I32), ("blk", 128, BF), ("blkn", 128, BF), ("blkp", 128, BF),
-        ("blkq", 128, BF), ("blkt", 128, BF), ("eye", 128, BF), ("eyen", 128, BF), ("ge", 128, BF), ("lbp", 128, BF),
-        ("wd", 144, BF), ("ones", 128, BF), ("lo", 448, BF), ("hi", 512, BF), ("zero", 16, BF), ("g16", 4, F32),
-        ("tri", 16, F32), ("coef", 32, BF), ("cz", 32, BF), ("nbig", 4, F32), ("wm", 32, BF), ("tabs", 1536, F32),
-        ("dist", 32, F32), ("mid", 8, F32), ("hh", 8, BF), ("dhi", 16, BF), ("dlo", 16, BF), ("s64", 4, F32),
-        ("kab", 8, F32), ("woff", 8, U16), ("zl", 32, U16), ("res", 4, F32)]:
+        ("wants", 32, I32), ("w16", 32, U16), ("loff", 32, U16), ("peps", W, BF), ("S", W, BF), ("gath", 448, BF),
+        ("mass", 512, BF), ("offt", 32, U16), ("gb", 16 * NC, BF), ("gm", 16 * NC, BF), ("gt", 512, BF), ("m0", NC, BF),
+        ("m1", NC, BF), ("iw", 128, I32), ("iu", 128, I32), ("sg", 128, I32), ("blk", 128, BF), ("blkn", 128, BF),
+        ("blkp", 128, BF), ("blkq", 128, BF), ("blkt", 128, BF), ("eye", 128, BF), ("eyen", 128, BF), ("ge", 128, BF),
+        ("lbp", 128, BF), ("wd", 144, BF), ("ones", 128, BF), ("lo", 256, BF), ("hi", 512, BF), ("zero", 16, BF),
+        ("g16", 4, F32), ("gap", 16, F32), ("tri", 16, F32), ("lane", 4, F32), ("coef", 32, BF), ("cz", 32, BF),
+        ("nbig", 4, F32), ("wm", 32, BF), ("tabs", 1536, F32), ("dist", 32, F32), ("mid", 8, F32), ("hh", 8, BF),
+        ("dhi", 16, BF), ("dlo", 16, BF), ("s64", 4, F32), ("kab", 8, F32), ("woff", 8, U16), ("zl", 32, U16),
+        ("res", 4, F32), ("up", 128, BF), ("swap", 128, BF), ("low", 128, BF), ("high", 128, BF), ("upp", 128, BF),
+        ("upn", 128, BF), ("c64", 8, BF)]:
     SCRATCH[_name] = ("sbuf", [128, _cols], _dt)
 for _name in ["ma", "mb", "pa", "pb", "pt", "pz"]:
     SCRATCH[_name] = ("psum", [128, 512], F32)
-SEMAPHORES = ["qv", "qs", "qp", "qg", "dwant", "dpep", "dsa", "dsb", "dleft", "dres", "go",
-              "lnear", "lfar", "sent", "rep0", "rep1", "rep2", "rep3"]
+SEMAPHORES = ["qv", "qs", "qp", "qg", "dwant", "dpep", "dspec", "dleft", "dres",
+              "ask0", "ask1", "ask2", "ask3", "dlow", "dcol", "dpea", "dpeb", "sent", "rep0", "rep1", "rep2", "rep3"]
 
 ALU = AluOpType
 ACT = ActivationFunctionType
@@ -54,6 +60,15 @@ def bits(engines):
     return sum(1 << e for e in engines)
 
 
+def tail_runs(lo, hi):
+    runs = []
+    for f in range(15):
+        a, b = max(lo, COL[1] + NT * f), min(hi, COL[1] + NT * (f + 1))
+        if a < b:
+            runs.append((f, a, b, a - COL[1] - NT * f))
+    return runs
+
+
 def rank_program(g, core, T, topo):
     r = T.rank_of(core)
     if r is None:
@@ -64,6 +79,7 @@ def rank_program(g, core, T, topo):
     addr = [topo.addr(T.cores[q]) for q in order]
     far = topo.engines(core, T.cores[order[1]])
     near = [e for e in topo.engines(core, T.cores[order[0]]) if e not in far]
+    nfar, hf = len(far), len(far) // 2
     sem = T.sem
     Q = {"v": g.vector, "s": g.scalar, "p": g.tensor, "g": g, "y": g.sync}
     QS = {"v": "qv", "s": "qs", "p": "qp", "g": "qg"}
@@ -94,163 +110,157 @@ def rank_program(g, core, T, topo):
         return op("p", deps, P.matmul, out, lhsT, rhs, start, stop)
 
     g.sync.dma_start(T.wants[:], T.want[:]).then_inc(sem.dwant, 16)
-    g.sync.dma_start(T.peps[:], T.pep[:]).then_inc(sem.dpep, 16)
-    WANT, PEP = ("dwant", 16), ("dpep", 16)
-    SPEC = [("dsb", 16)]
-    if EARLY:
-        g.sync.dma_start(T.S[:, 0:EARLY], T.spec[:, 0:EARLY]).then_inc(sem.dsa, 16)
-        SPEC.append(("dsa", 16))
+    g.sync.dma_start(T.peps[:, 0:HALF], T.pep[:, 0:HALF]).then_inc(sem.dpea, 16)
+    g.sync.dma_start(T.peps[:, HALF:W], T.pep[:, HALF:W]).then_inc(sem.dpeb, 16)
+    wait("y", [("dpea", 16)])
+    g.sync.dma_start(T.S[:, 0:HALF], T.spec[:, 0:HALF]).then_inc(sem.dlow, 16)
+    wait("y", [("dpeb", 16)])
+    g.sync.sem_inc(sem.dpep, 16)
+    g.sync.dma_start(T.S[:, HALF:W], T.spec[:, HALF:W]).then_inc(sem.dspec, 16)
+    g.sync.dma_start(T.c64[:, 0:2], T.spec[:, 64:66]).then_inc(sem.dcol, 16)
+    WANT, PEP, LOW, SPEC, COL64 = ("dwant", 16), ("dpep", 16), ("dlow", 16), ("dspec", 16), ("dcol", 16)
 
     t_iw = op("g", [], g.iota, T.iw[:], [[16, 8], [0, 16]], 15, -1)
     t_iu = op("g", [], g.iota, T.iu[:], [[1, 128]], 0, -1)
-    wait("g", [WANT])
-    g.remote_dma_fused([RemoteDMATransfer(
-        dst_ids=[DstId(rid=addr[k][0], pnc=addr[k][1]) for k in range(1, 7)], dma_engine_mask=bits(far),
-        remote_sem=sem.lfar, src=T.wants[:], dsts=[T.lland[:, place[k], :] for k in range(1, 7)])], local_sem=sem.sent)
-    g.remote_dma(T.lland[:, place[0], :], T.wants[:], sem.lnear, sem.sent, addr[0][1], addr[0][0], bits(near))
-    g.sem_inc(sem.go, 1)
-    t_lo = op("g", [], g.iota, T.lo[0:1, :], [[0, 7], [-1, 64]], 0, 0, allow_small_or_imprecise_dtypes=True)
-    wait("y", [("go", 1)])
-    g.sync.dma_start(T.S[:, EARLY:W], T.spec[:, EARLY:W]).then_inc(sem.dsb, 16)
+    t_up = op("g", [], g.iota, T.up[:], [[0, 8], [1, 2], [0, 8]], 0, 0, allow_small_or_imprecise_dtypes=True)
+    v([], V.memset, T.lt[:, 0], 0.0)
+    t_own = v([WANT], V.tensor_copy, T.w16[:], T.wants[:])
 
-    t_lt0 = v([], V.memset, T.lt[:], 0.0)
-    t_wd0 = v([], V.memset, T.wd[:], 0.0)
+    def transfer(k, name, source, landing):
+        engines = near if k == 0 else far[hf * ((k - 1) % 2):hf * ((k - 1) % 2) + hf]
+        return RemoteDMATransfer(dst_ids=[DstId(rid=addr[k][0], pnc=addr[k][1])], dma_engine_mask=bits(engines),
+                                 remote_sem=sem["%s%d" % (name, (k + 1) // 2)], src=source, dst=landing)
+
+    wait("g", [t_own])
+
+
+    def ask(ks):
+        g.remote_dma_fused([transfer(k, "ask", T.w16[:, 4 * order[k]:4 * order[k] + 4],
+                                     T.loff[:, 4 * place[k]:4 * place[k] + 4]) for k in ks], local_sem=sem.sent)
+
+    for ks in [(0, 1, 2), (3, 4), (5, 6)]:
+        ask(ks)
+    t_lo = op("g", [], g.iota, T.lo[0:1, :], [[0, 4], [-1, 64]], 0, 0, allow_small_or_imprecise_dtypes=True)
+
     t_sg = v([t_iw], V.tensor_scalar, T.sg[:], T.iw[:], 4, None, ALU.arith_shift_right)
     t_ge = v([t_iu], V.tensor_scalar, T.ge[:], T.iu[:], 0.0, None, ALU.is_ge)
-    t_own = v([WANT], V.tensor_copy, T.loff[:, 0:4], T.wants[:, 4 * r:4 * r + 4])
     t_blk = v([t_sg], V.tensor_scalar, T.blk[:], T.sg[:], 0.0, None, ALU.is_equal)
     t_g16 = v([], V.tensor_scalar, T.g16[:, 0:1], T.sg[:, 0:1], -16.0, None, ALU.mult)
-    t_lb = v([t_ge, t_blk], V.tensor_tensor, T.ll[:, 0, :], T.ge[:], T.blk[:], ALU.mult)
+    t_lb = v([t_ge, t_blk], V.tensor_tensor, T.ll[:, 0], T.ge[:], T.blk[:], ALU.mult)
+    t_dif = v([t_g16], V.tensor_scalar, T.gap[:], T.iu[:, 0:16], T.g16[:, 0:1], None, ALU.add)
+    t_ly = v([t_lb], V.tensor_tensor, T.ll[:, 1], T.blk[:], T.ll[:, 0], ALU.subtract)
+    t_tri = v([t_dif], V.tensor_scalar, T.tri[:], T.gap[:], 0.0, None, ALU.is_ge)
+    x = v([t_ly], V.tensor_tensor, T.ge[:], T.ll[:, 1], T.ll[:, 0], ALU.subtract)
+    t_wd0 = v([], V.memset, T.wd[:], 0.0)
+    x = v([x, t_up], V.tensor_tensor, T.swap[:], T.ge[:], T.up[:], ALU.mult)
+    v([], V.tensor_scalar, T.coef[:, C_H:C_A], T.gap[:, 1:2 * KP:2], 0.0, None, ALU.is_equal)
+    v([x], V.tensor_tensor, T.low[:], T.ll[:, 0], T.swap[:], ALU.add)
+    t_high = v([], V.tensor_tensor, T.high[:], T.ll[:, 1], T.swap[:], ALU.subtract)
     t_wd = v([t_wd0], V.tensor_copy, T.wd[:, 15:128:16], T.blk[:, 15:128:16])
-    t_tri = v([t_g16], V.tensor_scalar, T.tri[:], T.iu[:, 0:16], T.g16[:, 0:1], 0.0, ALU.add, ALU.is_ge)
-    t_ly = v([t_lb], V.tensor_tensor, T.ll[:, 1, :], T.blk[:], T.ll[:, 0, :], ALU.subtract)
-    v([t_wd], V.tensor_tensor, T.lbp[:], T.ll[:, 0, :], T.wd[:, 0:128], ALU.subtract)
-    for gg in range(8):
-        t_const = v([t_ly, t_lt0], V.tensor_copy, T.lt[:, :, :, 16 * gg + 15], T.ll[:, :, 16 * gg:16 * gg + 15])
-    t_eye = v([], V.tensor_scalar, T.eye[:], T.iu[:], 0.0, None, ALU.is_equal)
+
+    def constants_of_the_tail(x):
+        v([t_wd], V.tensor_tensor, T.lbp[:], T.ll[:, 0], T.wd[:, 0:128], ALU.subtract)
+        return v([x], V.tensor_copy, T.lt[:, :, 15:128:16, :], T.ll[:, :, :, 0:15])
+
+    def fill(out, like, value):
+        return s([], out, like, ACT.Identity, bias=float(value), scale=0.0)
+
+    banked = [(0, 0, 64), (1, 0, 64 - NT), (2, 0, 64), (3, 0, 64), (4, 0, 64), (5, 0, 64), (1, 64 - NT, 64), (6, 0, 64),
+              (7, 0, 64)]
+    s([t_up], T.upp[0:1, :], T.up[0:1, :], ACT.Copy, scale=64.0)
+    s([], T.upn[0:1, :], T.up[0:1, :], ACT.Copy, scale=-64.0)
+    t_ones = fill(T.ones[0:1, :], T.up[0:1, :], 1)
     t_blkp = s([t_blk], T.blkp[:], T.blk[:], ACT.Copy, scale=1024.0)
-    s([], T.blkn[:], T.blk[:], ACT.Copy, scale=-1024.0)
-    t_blkq = s([t_blkp, t_tri], T.blkq[:], T.blkp[:], ACT.Copy, scale=T.tri[:, 14:15])
+    t_blkn = s([], T.blkn[:], T.blk[:], ACT.Copy, scale=-1024.0)
+    fill(T.nbig[:, 0:2], T.blk[:, 0:2], -BIG)
+    s([t_dif], T.coef[:, C_A:C_S], T.gap[:, 1:2 * KP:2], ACT.Sign)
+    s([], T.coef[:, C_S:C_Y], T.gap[:, 15 - KS:15], ACT.Sign, bias=0.5)
+    x = s([], T.lane[:, 0:1], T.gap[:, 14:15], ACT.Relu, scale=-1.0)
+    s([t_tri], T.nbig[:, 2:3], T.tri[:, 7:8], ACT.Identity, bias=1024.0 - BIG, scale=-1024.0)
+    s([t_blkp], T.blkq[:], T.blkp[:], ACT.Copy, scale=T.tri[:, 14:15])
+    t_blkt = s([x], T.blkt[:], T.blkp[:], ACT.Copy, scale=T.lane[:, 0:1])
 
-    def constants_of_scores():
-        v([], V.memset, T.ones[0:1, :], 1.0)
-        for k in range(1, 6):
-            v([], V.memset, T.hi[0:1, 64 * (k - 1):64 * k], float(-64 * src[k]))
-        v([], V.memset, T.hi[0:1, 320:384], float(-64 * r))
-        v([], V.memset, T.hi[0:1, 384:448], float(-64 * src[6]))
-        v([], V.memset, T.hi[0:1, 448:512], float(-64 * src[7]))
-        return v([t_blkq], V.tensor_tensor, T.blkt[:], T.blkp[:], T.blkq[:], ALU.subtract)
+    def level(out, value):
+        return op("g", [], g.iota, out, [[0, out.shape[1]]], value, 0, allow_small_or_imprecise_dtypes=True)
 
-    def constants_of_round_1():
-        x = v([], V.memset, T.coef[:], 0.5)
-        v([], V.memset, T.zero[:], 0.0)
-        v([], V.memset, T.nbig[:, 0:2], -BIG)
-        v([], V.tensor_scalar, T.nbig[:, 2:3], T.tri[:, 7:8], -1024.0, 1024.0 - BIG, ALU.mult, ALU.add)
-        for lo, hi, val in [(C_B, C_Y, 32.0), (C_Y, C_H, -32.0), (C_H, C_T + 1, 0.0), (C_T + 1, NZ, -64.0)]:
-            v([], V.memset, T.cz[0:1, lo:hi], val)
-        even, odd = T.tri[:, 0:2 * KP:2], T.tri[:, 1:2 * KP:2]
-        v([x], V.memset, T.coef[:, C_T:C_S], 1.0)
-        v([], V.tensor_tensor, T.mid[:, 0:KP], odd, even, ALU.add)
-        x = v([], V.tensor_tensor, T.hh[:, 0:KP], odd, even, ALU.subtract)
-        v([], V.tensor_scalar, T.coef[:, C_S:NZ], T.tri[:, 15 - KS:15], 2.0, -1.0, ALU.mult, ALU.add)
-        v([x], V.tensor_scalar, T.coef[:, C_A:C_H], T.mid[:, 0:KP], 0.5, -0.5, ALU.mult, ALU.add)
-        return v([], V.tensor_scalar, T.coef[:, C_H:C_T], T.hh[:, 0:KP], 0.5, None, ALU.mult)
+    def late_constants():
+        for lo, hi, val in [(C_H, C_A, 0), (C_A, C_T, -64), (C_T, C_B, 0), (C_B, NZ, 64)]:
+            level(T.cz[0:1, lo:hi], val)
+        level(T.coef[:, C_Y:32], 1)
+        level(T.zero[:], 0)
+        level(T.tabs[:, 512:1024], 0)
+        op("g", [t_blk], g.affine_select, T.eye[:], T.blk[:], [[-1, 128]], ALU.is_equal, 0.0, 0, 1)
+        return op("g", [t_blkn], g.affine_select, T.eyen[:], T.blkn[:], [[-1, 128]], ALU.is_equal, 0.0, 0, 1)
 
     def numbers(deps):
-        mm(deps, T.pa[:, 0:352], T.ones[0:1, :], T.lo[0:1, 0:352], True, False)
-        mm([], T.pa[:, 0:352], T.ones[0:1, :], T.hi[0:1, 0:352], False, False)
-        mm([], T.pb[:, 0:160], T.ones[0:1, :], T.lo[0:1, 32:192], True, False)
-        mm([], T.pb[:, 0:160], T.ones[0:1, :], T.hi[0:1, 352:512], False, False)
+        mm(deps, T.pa[:, 0:CA], T.ones[0:1, :], T.hi[0:1, 0:CA], True, False)
+        mm([], T.pa[:, 0:COL[2]], T.ones[0:1, :], T.lo[0:1, 0:COL[2]], False, False)
+        mm([], T.pa[:, COL[2]:CA], T.ones[0:1, :], T.lo[0:1, 0:CA - COL[2]], False, False)
+        mm([], T.pb[:, 0:NBK], T.ones[0:1, :], T.hi[0:1, CA:512], True, False)
+        mm([], T.pb[:, 0:NBK], T.ones[0:1, :], T.lo[0:1, 64 - NT:64 - NT + NBK], False, False)
 
-    def bank(k):
-        return T.pa[:, 320:352] if k == 0 else T.pa[:, 64 * (k - 1):64 * k] if k < 6 else T.pb[:, 64 * k - 352:64 * k - 288]
+    def bank(lo, hi):
+        return T.pa[:, lo:hi] if lo < CA else T.pb[:, NT + lo - CA:NT + hi - CA]
 
     pepw = T.peps[:, 0:W]
     mine = T.mass[:, 64 * r:64 * r + 64]
-    tail = T.mass[:, 64 * r + 32:64 * r + 64]
-    t_mine = s([t_own, PEP], mine, pepw.indirect(T.loff[:, 0:4]), ACT.Copy)
-    t_blkt = constants_of_scores()
-    t_cn = v([("lnear", len(near))], V.tensor_copy, T.loff[:, 4:8], T.lland[:, 0, 4 * r:4 * r + 4])
-    t_gn = s([t_cn], T.gath[:, 0:64], pepw.indirect(T.loff[:, 4:8]), ACT.Copy)
-    wait("g", [t_gn])
-    g.remote_dma(mine, T.gath[:, 0:64], sem.rep0, sem.sent, addr[0][1], addr[0][0], bits(near))
+    tail = 64 * src[1] + 64 - NT
 
-    def blocks(k):
-        return [0] if k == 0 else [2 * k - 1, 2 * k]
-
-    def cols(ks):
-        return 32 * blocks(ks[0])[0], 32 * blocks(ks[-1])[-1] + 32
+    def answer(ks, q="s"):
+        asked = ("ask0", len(near)) if ks == [0] else ("ask%d" % (ks[1] // 2), nfar)
+        out, wanted = T.gath[:, 64 * ks[0]:64 * ks[-1] + 64], pepw.indirect(T.loff[:, 4 * ks[0]:4 * ks[-1] + 4])
+        wait("g", [s([asked], out, wanted, ACT.Copy) if q == "s" else v([asked, PEP], V.tensor_copy, out, wanted)])
+        g.remote_dma_fused([transfer(k, "rep", T.gath[:, 64 * k:64 * k + 64], mine) for k in ks], local_sem=sem.sent)
 
     def lists(ks, deps):
         for k in ks:
-            lo, hi = cols([k])
+            lo, hi = COL[k], COL[k + 1]
             rhs = T.mass[:, 64 * src[k]:64 * src[k] + hi - lo]
+            runs = tail_runs(lo, hi)
             for side in range(2):
-                mm(deps, T.px[:, side, lo:hi], T.lbp[:] if side == 0 else T.ll[:, 1, :], rhs, True, False)
-                for b in blocks(k):
-                    tok = mm([], T.px[:, side, 32 * b:32 * b + 32], T.lt[:, side, b, :], tail, False, b == blocks(k)[-1])
+                tok = mm(deps, T.px[:, side, lo:hi], T.ll[:, 1] if side else T.lbp[:], rhs, True, False)
+                for f, a, b, c in runs:
+                    tok = mm([], T.px[:, side, a:b], T.lt[:, side, :, f], T.mass[:, tail + c:tail + c + b - a], False, b == hi)
         return tok
 
     def conv(ks, tok):
-        lo, hi = cols(ks)
+        lo, hi = COL[ks[0]], COL[ks[-1] + 1]
         return v([tok], V.tensor_copy, T.off[:, :, lo:hi], T.px[:, :, lo:hi])
 
-    c0 = conv([0], lists([0], [t_mine, t_const]))
-    s([t_eye], T.eyen[:], T.eye[:], ACT.Copy, scale=-256.0)
-    nfar = len(far)
-    t_cf = v([("lfar", 6 * nfar)], V.tensor_copy, T.loff[:, 8:32], T.lland[:, 1:7, 4 * r:4 * r + 4])
-    back = [v([t_cf, PEP], V.tensor_copy, T.gath[:, 64:192], pepw.indirect(T.loff[:, 8:16])),
-            s([t_cf], T.gath[:, 192:320], pepw.indirect(T.loff[:, 16:24]), ACT.Copy),
-            s([t_cf], T.gath[:, 320:448], pepw.indirect(T.loff[:, 24:32]), ACT.Copy)]
-    hf = nfar // 2
-    for j in range(3):
-        wait("g", [back[j]])
-        g.remote_dma_fused([RemoteDMATransfer(
-            dst_ids=[DstId(rid=addr[k][0], pnc=addr[k][1])], dma_engine_mask=bits(far[hf * h:hf * h + hf]),
-            remote_sem=sem["rep%d" % (j + 1)], src=T.gath[:, 64 * k:64 * k + 64], dst=mine)
-            for h, k in enumerate((2 * j + 1, 2 * j + 2))], local_sem=sem.sent)
-    t_gap = op("g", [], g.iota, T.tabs[:, 512:1024], [[0, 512]], 0, 0, allow_small_or_imprecise_dtypes=True)
-    numbers([t_lo, t_blkt])
-    t_cz = constants_of_round_1()
-    c1 = conv([1], lists([1], [("rep0", len(near)), c0]))
-    ready = {0: c0, 1: c1}
-
     wb, wy = T.S[:, 0:W], T.S[:, 64:W]
-    gb, gm = T.gb, T.gm
 
-    def offs(b, side, lo=0, n=32):
-        return T.off[:, side, 32 * b + lo:32 * b + lo + n]
+    def look_b(q, lo, hi, deps):
+        if q == "v":
+            return v(deps, V.tensor_copy, T.gb[:, 16 * lo:16 * hi], wb.indirect(T.off[:, 0, lo:hi]))
+        return s(deps, T.gb[:, 16 * lo:16 * hi], wb.indirect(T.off[:, 0, lo:hi]), ACT.Copy)
 
-    def slot(k, i):
-        lo, hi = cols([k])
-        return gm[:, 16 * lo + i:16 * hi:16]
+    def look_y(lo, hi, deps):
+        return v(deps, V.tensor_tensor, T.gm[:, 16 * lo:16 * hi], wy.indirect(T.off[:, 1, lo:hi]), T.gb[:, 16 * lo:16 * hi],
+                 ALU.min)
+
+    def slot(lo, hi, i):
+        return T.gm[:, 16 * lo + i:16 * hi:16]
 
     def compact(k, M, deps):
-        lo, hi = cols([k])
-        for i in range(16):
-            tok = mm(deps, M[:, lo:hi], T.wd[:, 15 - i:143 - i], slot(k, i), i == 0, i == 15)
+        lo, hi = COL[k], COL[k + 1]
+        for i in range(16 if k else 15):
+            tok = mm(deps, M[:, lo:hi], T.wd[:, 15 - i:143 - i], slot(lo, hi, i), i == 0, i == (15 if k else 14))
         return tok
 
     def keep(ks, M, deps):
-        lo, hi = cols(ks)
+        lo, hi = COL[ks[0]], COL[ks[-1] + 1]
         return s(deps, T.m0[:, lo:hi], M[:, lo:hi], ACT.Copy)
 
-    def score(m, ks, deps, stop_a=False, stop_b=False):
-        runs = [[k for k in ks if k == 0], [k for k in ks if 0 < k < 6], [k for k in ks if k >= 6]]
-        ta = None
-        for j, run in enumerate(runs):
-            if run:
-                lo, hi = cols(run)
-                out = bank(0) if j == 0 else T.pa[:, lo - 32:hi - 32] if j == 1 else T.pb[:, lo - 320:hi - 320]
-                tok = mm(deps, out, T.blkq[:], m[:, lo:hi], False, stop_a and j == 1)
-                ta = tok if j == 1 else ta
-        bs = [b for k in ks for b in blocks(k)]
-        for b in bs:
-            tok = mm([], T.pb[:, 0:32], T.blkt[:], m[:, 32 * b:32 * b + 32], False, stop_b and b == bs[-1])
-        return ta, tok
+    def score_own(m, lo, hi, deps, stop=False):
+        return mm(deps, bank(lo, hi), T.blkq[:], m[:, lo:hi], False, stop)
+
+    def score_tail(m, lo, hi, stop=False):
+        for f, a, b, c in tail_runs(lo, hi):
+            tok = mm([], T.pb[:, c:c + b - a], T.blkt[:], m[:, a:b], False, stop and b == hi)
+        return tok
 
     def best(t, half, deps):
-        return v(deps, V.tensor_reduce, T.kab[:, 4 * t + half:4 * t + half + 1], T.pb[:, 0:160] if half else T.pa[:, 0:352],
+        return v(deps, V.tensor_reduce, T.kab[:, 4 * t + half:4 * t + half + 1], T.pb[:, 0:NBK] if half else T.pa[:, 0:CA],
                  AxisListType.X, ALU.max)
 
     def winner(t, deps, lo, hi):
@@ -264,81 +274,112 @@ def rank_program(g, core, T, topo):
         x = v([x], V.tensor_copy, wb.indirect(T.zl[:, 16 * t:16 * t + 1]), T.zero[:])
         return v([x], V.tensor_copy, wy.indirect(T.zl[:, 16 * t + 8:16 * t + 9]), T.zero[:])
 
+    t_mine = s([t_own, PEP], mine, pepw.indirect(T.w16[:, 4 * r:4 * r + 4]), ACT.Copy)
+    for side, (tri, shift) in enumerate([(T.low, T.upp), (T.high, T.upn)]):
+        mm([t_mine, t_high], T.px[:, side, 0:64], tri[:], mine, True, False)
+        made = mm([t_ones], T.px[:, side, 0:64], shift[0:1, :], T.ones[0:1, 0:64], False, True)
+    t_lt1 = v([], V.memset, T.lt[:, 1], 0.0)
+    c0 = conv([0], made)
+    at = 0
+    for k, a, b in banked:
+        t_hi = fill(T.hi[0:1, at:at + b - a], T.blk[0:1, 0:b - a], -64 * src[k])
+        at += b - a
+    answer([0], "v")
+    answer([1, 2], "v")
+    t_const = constants_of_the_tail(t_lt1)
+    x = s([LOW, c0], T.gb[:, 0:512], T.S[:, 0:HALF].indirect(T.off[:, 0, 0:32]), ACT.Copy)
+    y = s([], T.gb[:, 512:1024], T.S[:, 0:HALF].indirect(T.off[:, 0, 32:64]), ACT.Copy)
+    answer([3, 4])
+    answer([5, 6])
+    t_cz = late_constants()
+    look_y(0, 32, [x, SPEC, LOW])
+    if OWN > 32:
+        look_y(32, OWN, [y])
+    c1 = conv([1], lists([1], [("rep0", len(near)), c0, t_const]))
+    m_own = look_y(OWN, 64, [y])
+    made = lists([2], [("rep1", nfar), c1])
+    got = [look_b("s", a, b, [c1, SPEC]) for a, b in zip(NEAR, NEAR[1:])]
+    ready = {}
+    for n, x in enumerate(got):
+        if n == CONV2:
+            ready[2] = conv([2], made)
+            made = lists([3], [ready[2]])
+        m_near = look_y(NEAR[n], NEAR[n + 1], [x])
+    ready[3] = conv([3], made)
     M = {0: T.ma, 1: T.ma, 2: T.mb, 3: T.mb, 4: T.ma, 5: T.ma, 6: T.mb, 7: T.ma}
-    mtok, ctok, ktok = {}, {}, {}
-    va = v(SPEC + [c0], V.tensor_copy, gb[:, 0:256], wb.indirect(offs(0, 0, 0, 16)))
-    sa = s(SPEC + [c0], gb[:, 256:512], wb.indirect(offs(0, 0, 16, 16)), ACT.Copy)
-    made = lists([2, 3], [("rep1", nfar), c1])
-    p64 = mm(SPEC, T.pt[:, 0:2], T.blk[:], T.S[:, 64:66], True, True)
-    v([va], V.tensor_tensor, gm[:, 0:256], wy.indirect(offs(0, 1, 0, 16)), gb[:, 0:256], ALU.min)
-    mtok[0] = v([sa], V.tensor_tensor, gm[:, 256:512], wy.indirect(offs(0, 1, 16, 16)), gb[:, 256:512], ALU.min)
-    for b in range(1, NB):
-        k = (b + 1) // 2
+    compact(0, M[0], [m_own])
+    ctok, ktok = {1: compact(1, M[1], [m_near])}, {}
+    for b, (lo, hi) in enumerate(zip(EDGE, EDGE[1:])):
+        k = max(j for j in range(8) if COL[j] < hi)
+        if b == KEEP[0]:
+            numbers([t_lo, t_hi])
+        if b == MADE[0]:
+            made = lists([4, 5], [("rep2", nfar), ready[3]])
         if b == STAGE[0]:
-            ready[2] = ready[3] = conv([2, 3], made)
-            made = lists([4, 5], [("rep2", nfar), ready[2]])
-        if b == STAGE[1]:
             ready[4] = ready[5] = conv([4, 5], made)
+        if b == MADE[1]:
             made = lists([6, 7], [("rep3", nfar), ready[4]])
             for p in range(16):
-                tl = mm([t_s64], T.pt[:, 0:32], T.wd[:, 15 - p:143 - p], T.mass[:, p:512:16], p == 0, p == 15)
-        if b == STAGE[2]:
+                tl = mm([], T.pt[:, 0:32], T.wd[:, 15 - p:143 - p], T.mass[:, p:512:16], p == 0, p == 15)
+        if b == STAGE[1]:
             ready[6] = ready[7] = conv([6, 7], made)
             ct = v([tl], V.tensor_copy, T.offt[:], T.pt[:, 0:32])
-            mm([], T.pz[:], T.ll[:, 1, :], T.mass[:], True, True)
-            tabp = mm([ct], T.pt[:], T.ll[:, 0, :], T.mass[:], True, True)
-        if b == 2:
-            compact(0, M[0], [mtok[0]])
-        if b == 3:
-            t_s64 = s([p64], T.s64[:, 0:1], T.pt[:, 0:1], ACT.Identity, bias=-BIG / 1024)
-            t_col = s([], T.s64[:, 1:2], T.S[:, 64:65], ACT.Copy)
-        if b in (6, 10, 14):
-            ks = [b // 2 - 3, b // 2 - 2]
+            mm([], T.pz[:], T.ll[:, 1], T.mass[:], True, True)
+            tabp = mm([ct], T.pt[:], T.ll[:, 0], T.mass[:], True, True)
+        if b in KEEP:
+            ks = [2 * KEEP.index(b), 2 * KEEP.index(b) + 1]
             ktok[ks[1]] = keep(ks, M[ks[0]], [ctok[ks[1]]])
-        gtok = s([ready[k]], gb[:, 512 * b:512 * b + 512], wb.indirect(offs(b, 0)), ACT.Copy)
-        mtok[b] = v([gtok], V.tensor_tensor, gm[:, 512 * b:512 * b + 512], wy.indirect(offs(b, 1)),
-                    gb[:, 512 * b:512 * b + 512], ALU.min)
-        if b in (6, 10, 14):
-            score(T.m0, ks, [ktok[ks[1]], t_blkt])
-        if b % 2 == 0 and k < 7:
-            ctok[k] = compact(k, M[k], [mtok[b]] + ([ktok[k - 3]] if k in (4, 6) else []))
+        mtok = look_y(lo, hi, [look_b("s", lo, hi, [ready[k]])])
+        if b in KEEP:
+            score_own(T.m0, COL[ks[0]], COL[ks[1] + 1], [ktok[ks[1]], t_blkt])
+            score_tail(T.m0, COL[ks[0]], COL[ks[1] + 1])
+        for k in range(2, 7):
+            if lo < COL[k + 1] <= hi:
+                ctok[k] = compact(k, M[k], [mtok] + ([ktok[k - 3]] if k in (4, 6) else []))
+    q = min(src[6:8])
+    for a, b in [(0, q), (q + 2, N)]:
+        if a < b:
+            tg = s([ct, COL64], T.gt[:, 64 * a:64 * b], wb.indirect(T.offt[:, 4 * a:4 * b]), ACT.Relu, bias=T.c64[:, 0:1],
+                   scale=-1.0)
+    tv = v([COL64], V.tensor_scalar, T.gt[:, 64 * q:64 * q + 128], wb.indirect(T.offt[:, 4 * q:4 * q + 8]), T.c64[:, 0:1],
+           0.0, ALU.subtract, ALU.min)
     k6 = keep([6], M[6], [ctok[6]])
-    tg = s([ct, t_col], T.gt[:], wb.indirect(T.offt[:]), ACT.Relu, bias=T.s64[:, 1:2], scale=-1.0)
     s([tabp], T.tabs[:, 0:512], T.pt[:], ACT.Copy)
     t_tab = s([], T.tabs[:, 1024:1536], T.pz[:], ACT.Copy)
-    score(T.m0, [6], [k6])
-    mm([tg], bank(0), T.blkn[:], T.gt[:, 64 * r:64 * r + 32], False, False)
-    for k in range(1, 6):
-        ta = mm([], bank(k), T.blkn[:], T.gt[:, 64 * src[k]:64 * src[k] + 64], False, k == 5)
-    mm([], T.pb[:, 0:32], T.blkn[:], T.gt[:, 64 * r + 32:64 * r + 64], False, False)
-    for k in (6, 7):
-        mm([], bank(k), T.blkn[:], T.gt[:, 64 * src[k]:64 * src[k] + 64], False, False)
+    for k in range(6):
+        ta = mm([tg], bank(COL[k], COL[k + 1]), T.blkn[:], T.gt[:, 64 * src[k]:64 * src[k] + COL[k + 1] - COL[k]], False, k == 5)
+    mm([], T.pb[:, 0:NT], T.blkn[:], T.gt[:, tail:tail + NT], False, False)
+    score_own(T.m0, COL[6], COL[7], [k6])
+    score_tail(T.m0, COL[6], COL[7])
     for i in range(15):
-        mm([mtok[14]], bank(7), T.blkp[:], slot(7, i), False, False)
-    for b in blocks(7):
-        tb = mm([], T.pb[:, 0:32], T.blkp[:], gm[:, 512 * b + 15:512 * b + 512:16], False, b == 14)
+        mm([mtok], bank(COL[7], NC), T.blkp[:], slot(COL[7], NC, i), False, False)
+    for f, a, b, c in tail_runs(COL[7], NC):
+        mm([], T.pb[:, c:c + b - a], T.blkp[:], slot(a, b, 15), False, False)
+    for k in (6, 7):
+        tb = mm([tv], bank(COL[k], COL[k + 1]), T.blkp[:], T.gt[:, 64 * src[k]:64 * src[k] + 64], False, k == 7)
     k7 = keep([7], M[7], [compact(7, M[7], [ktok[5]])])
     mm([t_cz, t_tab], T.pz[:, 0:NZ], T.ones[0:1, :], T.cz[0:1, 0:NZ], True, False)
+    p64 = mm([COL64], T.pt[:, 0:2], T.blk[:], T.c64[:, 0:2], True, True)
     best(0, 0, [ta])
     e64 = v([], V.tensor_scalar, T.hit[:, 0, :], T.off[:, 0, :], 64.0, None, ALU.is_equal)
     red0 = best(0, 1, [tb])
-    off0 = winner(0, [red0], 0, 3)[1]
+    off0 = winner(0, [red0, t_cz], 0, 3)[1]
 
     x = v([off0], V.tensor_tensor, T.wm[:], T.mass[:, 0:512].indirect(T.woff[:, 0:2]), T.coef[:], ALU.mult)
     z = mm([x], T.pz[:, 0:NZ], T.blk[:], T.wm[:, 0:NZ], False, True)
     t_d = s([z], T.dist[:, 0:NZ], T.pz[:, 0:NZ], ACT.Abs)
-    t_u = [s([t_d], T.u[:, side, :], T.px[:, side, 0:NC], ACT.Abs, bias=T.dist[:, side:side + 1], scale=-1.0)
-           for side in range(2)]
+    t_u = [s([t_d], T.u[:, side, :], T.px[:, side, 0:NC], ACT.Abs, bias=T.dist[:, c:c + 1], scale=-2.0)
+           for side, c in enumerate((C_B, C_Y))]
     PART = [(0, CA, T.ma), (CA, NC, T.mb)]
     for lo, hi, bk in PART:
         mm([k7], bk[:, lo:hi], T.eye[:], T.m0[:, lo:hi], True, False)
         mm([e64], bk[:, lo:hi], T.eyen[:], T.hit[:, 0, lo:hi], False, False)
     numbers([red0])
-    clear(0, T.woff[:, 2:3], [t_tab, t_gap])
-    x = v([t_d], V.tensor_copy, T.dhi[:, 0:KS + 2], T.dist[:, C_T:NZ])
-    v([], V.tensor_tensor, T.mid[:, 0:KP], T.dist[:, C_A:C_H], T.dist[:, C_H:C_T], ALU.max)
-    t_h = v([], V.tensor_tensor, T.hh[:, 0:KP], T.dist[:, C_A:C_H], T.dist[:, C_H:C_T], ALU.min)
-    x = v([x], V.tensor_tensor, T.dlo[:, 0:KS + 2], T.dist[:, C_T:NZ], T.dhi[:, 0:KS + 2], ALU.subtract)
+    clear(0, T.woff[:, 2:3], [t_tab])
+    x = v([t_d], V.tensor_copy, T.dhi[:, 0:KS + 2], T.dist[:, C_S:C_B])
+    v([], V.tensor_tensor, T.mid[:, 0:KP], T.dist[:, C_A:C_S], T.dist[:, C_H:C_A], ALU.max)
+    t_h = v([], V.tensor_tensor, T.hh[:, 0:KP], T.dist[:, C_A:C_S], T.dist[:, C_H:C_A], ALU.min)
+    x = v([x], V.tensor_tensor, T.dlo[:, 0:KS + 2], T.dist[:, C_S:C_B], T.dhi[:, 0:KS + 2], ALU.subtract)
 
     def lose(buf, j, part, deps, stop=False):
         lo, hi, bk = part
@@ -346,49 +387,42 @@ def rank_program(g, core, T, topo):
             tok = mm(deps, bk[:, lo:hi], T.eyen[:], buf[:, 2 * j + side, lo:hi], False, stop and side == 1)
         return tok
 
-    for side in range(2):
-        y = v([x], V.tensor_scalar, T.hit[:, 2 + side, :], T.off[:, side, :], T.dhi[:, side:side + 1],
-              T.dlo[:, side:side + 1], ALU.subtract, ALU.is_equal)
+    for side, c in enumerate((KS + 1, KS)):
+        y = v([x], V.tensor_scalar, T.hit[:, 2 + side, :], T.off[:, side, :], T.dhi[:, c:c + 1], T.dlo[:, c:c + 1],
+              ALU.subtract, ALU.is_equal)
     for part in PART:
         lose(T.hit, 1, part, [y])
     for side in range(2):
-        t_u2 = v([t_u[side]], V.tensor_scalar, T.u2[:, side, :], T.u[:, side, :], 2.0, None, ALU.mult)
+        t_u2 = v([t_u[side]], V.tensor_copy, T.u2[:, side, :], T.u[:, side, :])
 
-    def single(j, part, stop=False):
-        lo, hi, bk = part
-        x = v([t_u2], V.tensor_scalar, T.hit[:, 2 * j + 4:2 * j + 6, lo:hi], T.u2[:, :, lo:hi],
-              T.dhi[:, j + 2:j + 3], T.dlo[:, j + 2:j + 3], ALU.subtract, ALU.is_equal)
-        return lose(T.hit, j + 2, part, [x], stop)
+    def single(j):
+        x = v([t_u2], V.tensor_scalar, T.hit[:, 2 * j + 4:2 * j + 6, :], T.u2[:], T.dhi[:, j:j + 1], T.dlo[:, j:j + 1],
+              ALU.subtract, ALU.is_equal)
+        for part in PART:
+            lose(T.hit, j + 2, part, [x])
 
-    def pair(p, part, stop=False):
+    def pair(p, part):
         lo, hi, bk = part
         f = T.fold[:, 2 * p:2 * p + 2, lo:hi]
         x = s([t_u[1], t_h], f, T.u[:, :, lo:hi], ACT.Abs, bias=T.mid[:, p:p + 1], scale=-1.0)
         x = v([x], V.tensor_scalar, f, f, T.hh[:, p:p + 1], None, ALU.is_equal)
-        return lose(T.fold, p, part, [x], stop)
+        return lose(T.fold, p, part, [x], p == KP - 1)
 
-    A, B = PART
-    singles = [[j for j in range(KS) if 15 - KS + j >= 2 * kp] for kp in PAIRS]
-    todo = [(j, A) for j in singles[0]] + [(j, B) for j in singles[1]]
-    for p in range(PAIRS[0]):
-        for j, part in todo[len(todo) * p // PAIRS[0]:len(todo) * (p + 1) // PAIRS[0]]:
-            single(j, part)
-        done = pair(p, A, p == PAIRS[0] - 1)
-    rest = []
-    for p in range(PAIRS[1]):
+    for p in range(KP):
+        if p < KS:
+            single(p)
+        done = pair(p, PART[0])
+    for p in range(KP):
         if p == CLOSE:
             x = v([done], V.tensor_scalar, T.m1[:, 0:CA], T.ma[:, 0:CA], 0.0, None, ALU.max)
-        last = pair(p, B, p == PAIRS[1] - 1)
+        last = pair(p, PART[1])
         if p == CLOSE:
-            mm([x], bank(0), T.blkq[:], T.m1[:, 0:32], False, False)
-            ta = mm([], T.pa[:, 0:CA - 32], T.blkq[:], T.m1[:, 32:CA], False, True)
-            rest = list(range(CA // 32))
-        n = len(rest) if p == PAIRS[1] - 1 else min(len(rest), SPREAD)
-        for b in rest[:n]:
-            mm([], T.pb[:, 0:32], T.blkt[:], T.m1[:, 32 * b:32 * b + 32], False, False)
-        rest = rest[n:]
+            ta = score_own(T.m1, 0, CA, [x], True)
+    score_tail(T.m1, 0, CA)
+    t_s64 = s([p64], T.s64[:, 0:1], T.pt[:, 0:1], ACT.Identity, bias=-BIG / 1024)
     x = s([last], T.m1[:, CA:NC], T.mb[:, CA:NC], ACT.Relu)
-    tb = score(T.m1, [6, 7], [x], stop_b=True)[1]
+    score_own(T.m1, CA, NC, [x])
+    tb = score_tail(T.m1, CA, NC, True)
     best(1, 0, [ta])
     key, up = T.kab[:, 2:3], T.kab[:, 3:4]
     v([], V.tensor_scalar, T.res[:, 0:1], T.nbig[:, 0:1], up, key, ALU.add, ALU.subtract)
@@ -405,5 +439,5 @@ def rank_program(g, core, T, topo):
     wait("s", [x])
     g.scalar.dma_start(T.win[:], T.res[0:128:16, 0:2]).then_inc(sem.dres, 16)
     g.scalar.dma_start(T.score[:], T.res[0:128:16, 2:4]).then_inc(sem.dres, 16)
-    wait("g", [("sent", 4 * nfar + 2 * len(near)), ("qg", count["g"]), ("qp", count["p"]), ("qs", count["s"]),
+    wait("g", [("sent", 6 * nfar + 2 * len(near)), ("qg", count["g"]), ("qp", count["p"]), ("qs", count["s"]),
                ("qv", count["v"]), ("dres", 32), ("dleft", 16)])

@@ -12,18 +12,15 @@ EDGE = [100, 132, 164, 196, 228, 260, 292, 324, 356, 388, 420, 452, 484]
 MADE = (0, 3)
 STAGE = (2, 6)
 KEEP = (3, 7, 11)
-KP, KS = 6, 3
-CLOSE = 3
+PARTS = [0, 178, CA, NC]
 BIG = 1.5 * 2.0 ** 33
-C_H, C_A, C_S = 0, KP, 2 * KP
-C_Y = C_S + KS
-C_T, C_B, NZ = C_Y + 1, C_Y + 2, C_Y + 3
+C_B, C_Y, C_Q, C_D, NZ = 16, 17, 18, 19, 20
+MID, SHIFT = 1536, 1024
 
-BF, F32, I32, U16 = "bfloat16", "float32", "int32", "uint16"
+BF, F16, F32, I32, U16 = "bfloat16", "float16", "float32", "int32", "uint16"
 SCRATCH = {"ll": ("sbuf", [128, 2, 8, 16], BF), "lt": ("sbuf", [128, 2, 128, 15], BF),
-           "off": ("sbuf", [128, 2, NC], U16), "u": ("sbuf", [128, 2, NC], F32), "u2": ("sbuf", [128, 2, NC], U16),
-           "fold": ("sbuf", [128, 2 * KP, NC], BF), "hit": ("sbuf", [128, 2 * KS + 4, NC], BF),
-           "px": ("psum", [128, 2, 512], F32)}
+           "off": ("sbuf", [128, 2, NC], U16), "u": ("sbuf", [128, 2, NC], U16), "ul": ("sbuf", [128, 2, NC], F16),
+           "zig": ("sbuf", [128, 16, NC], F16), "px": ("psum", [128, 2, 512], F32)}
 for _name, _cols, _dt in [
         ("wants", 32, I32), ("w16", 32, U16), ("loff", 32, U16), ("peps", W, BF), ("S", W, BF), ("gath", 448, BF),
         ("mass", 512, BF), ("offt", 32, U16), ("gb", 16 * NC, BF), ("gm", 16 * NC, BF), ("gt", 512, BF), ("m0", NC, BF),
@@ -31,8 +28,9 @@ for _name, _cols, _dt in [
         ("blkp", 128, BF), ("blkq", 128, BF), ("blkt", 128, BF), ("eye", 128, BF), ("eyen", 128, BF), ("ge", 128, BF),
         ("lbp", 128, BF), ("wd", 144, BF), ("ones", 128, BF), ("lo", 256, BF), ("hi", 512, BF), ("zero", 16, BF),
         ("g16", 4, F32), ("gap", 16, F32), ("tri", 16, F32), ("lane", 4, F32), ("coef", 32, BF), ("cz", 32, BF),
-        ("nbig", 4, F32), ("wm", 32, BF), ("tabs", 1536, F32), ("dist", 32, F32), ("mid", 8, F32), ("hh", 8, BF),
-        ("dhi", 16, BF), ("dlo", 16, BF), ("s64", 4, F32), ("kab", 8, F32), ("woff", 8, U16), ("zl", 32, U16),
+        ("nbig", 4, F32), ("wm", 32, BF), ("tabs", 1536, F32), ("dist", 32, F32), ("rk", 16, F32), ("ksh", 16, F32),
+        ("kco", 16, F32), ("kn", 16, F16), ("ranked", 16, F16), ("junk", 32, F32), ("col", 4, F32), ("blkh", 128, BF),
+        ("eyeh", 128, BF), ("s64", 4, F32), ("kab", 8, F32), ("woff", 8, U16), ("zl", 32, U16),
         ("res", 4, F32), ("up", 128, BF), ("swap", 128, BF), ("low", 128, BF), ("high", 128, BF), ("upp", 128, BF),
         ("upn", 128, BF), ("c64", 8, BF)]:
     SCRATCH[_name] = ("sbuf", [128, _cols], _dt)
@@ -133,7 +131,6 @@ def rank_program(g, core, T, topo):
 
     wait("g", [t_own])
 
-
     def ask(ks):
         g.remote_dma_fused([transfer(k, "ask", T.w16[:, 4 * order[k]:4 * order[k] + 4],
                                      T.loff[:, 4 * place[k]:4 * place[k] + 4]) for k in ks], local_sem=sem.sent)
@@ -153,7 +150,6 @@ def rank_program(g, core, T, topo):
     x = v([t_ly], V.tensor_tensor, T.ge[:], T.ll[:, 1], T.ll[:, 0], ALU.subtract)
     t_wd0 = v([], V.memset, T.wd[:], 0.0)
     x = v([x, t_up], V.tensor_tensor, T.swap[:], T.ge[:], T.up[:], ALU.mult)
-    v([], V.tensor_scalar, T.coef[:, C_H:C_A], T.gap[:, 1:2 * KP:2], 0.0, None, ALU.is_equal)
     v([x], V.tensor_tensor, T.low[:], T.ll[:, 0], T.swap[:], ALU.add)
     t_high = v([], V.tensor_tensor, T.high[:], T.ll[:, 1], T.swap[:], ALU.subtract)
     t_wd = v([t_wd0], V.tensor_copy, T.wd[:, 15:128:16], T.blk[:, 15:128:16])
@@ -173,31 +169,43 @@ def rank_program(g, core, T, topo):
     t_blkp = s([t_blk], T.blkp[:], T.blk[:], ACT.Copy, scale=1024.0)
     t_blkn = s([], T.blkn[:], T.blk[:], ACT.Copy, scale=-1024.0)
     fill(T.nbig[:, 0:2], T.blk[:, 0:2], -BIG)
-    s([t_dif], T.coef[:, C_A:C_S], T.gap[:, 1:2 * KP:2], ACT.Sign)
-    s([], T.coef[:, C_S:C_Y], T.gap[:, 15 - KS:15], ACT.Sign, bias=0.5)
+    t_blkh = s([], T.blkh[:], T.blk[:], ACT.Copy, scale=512.0)
+    s([t_dif], T.coef[:, 0:16], T.gap[:], ACT.Sign, bias=0.5)
+    fill(T.cz[0:1, 0:C_B], T.up[0:1, 0:C_B], -63.75)
+    fill(T.cz[0:1, C_Q:C_D], T.up[0:1, 0:1], 63.75)
     x = s([], T.lane[:, 0:1], T.gap[:, 14:15], ACT.Relu, scale=-1.0)
     s([t_tri], T.nbig[:, 2:3], T.tri[:, 7:8], ACT.Identity, bias=1024.0 - BIG, scale=-1024.0)
     s([t_blkp], T.blkq[:], T.blkp[:], ACT.Copy, scale=T.tri[:, 14:15])
     t_blkt = s([x], T.blkt[:], T.blkp[:], ACT.Copy, scale=T.lane[:, 0:1])
 
-    def level(out, value):
-        return op("g", [], g.iota, out, [[0, out.shape[1]]], value, 0, allow_small_or_imprecise_dtypes=True)
+    def level(out, value, pattern=None):
+        return op("g", [], g.iota, out, pattern or [[0, out.shape[1]]], value, 0, allow_small_or_imprecise_dtypes=True)
 
     def late_constants():
-        for lo, hi, val in [(C_H, C_A, 0), (C_A, C_T, -64), (C_T, C_B, 0), (C_B, NZ, 64)]:
-            level(T.cz[0:1, lo:hi], val)
-        level(T.coef[:, C_Y:32], 1)
+        level(T.cz[0:1, C_B:C_Q], 64, [[-128, 2]])
+        level(T.cz[0:1, C_D:NZ], 64)
+        level(T.coef[:, 16:32], 1)
         level(T.zero[:], 0)
         level(T.tabs[:, 512:1024], 0)
-        op("g", [t_blk], g.affine_select, T.eye[:], T.blk[:], [[-1, 128]], ALU.is_equal, 0.0, 0, 1)
-        return op("g", [t_blkn], g.affine_select, T.eyen[:], T.blkn[:], [[-1, 128]], ALU.is_equal, 0.0, 0, 1)
+        level(T.rk[:], -15, [[2, 16]])
+        for lo, hi, val in [(0, 9, MID), (9, 15, MID - SHIFT), (15, 16, 0)]:
+            level(T.ksh[:, lo:hi], val)
+        level(T.kco[:, 0:8], 0, [[0, 4], [-1024, 2]])
+        level(T.kco[:, 8:9], 512)
+        level(T.kco[:, 9:15], 0, [[0, 3], [1024, 2]])
+        level(T.kco[:, 15:16], -1024)
+        for eye, blk, tok in [(T.eye, T.blkp, t_blkp), (T.eyen, T.blkn, t_blkn), (T.eyeh, T.blkh, t_blkh)]:
+            x = op("g", [tok], g.affine_select, eye[:], blk[:], [[-1, 128]], ALU.is_equal, 0.0, 0, 1)
+        return x
 
-    def numbers(deps):
-        mm(deps, T.pa[:, 0:CA], T.ones[0:1, :], T.hi[0:1, 0:CA], True, False)
-        mm([], T.pa[:, 0:COL[2]], T.ones[0:1, :], T.lo[0:1, 0:COL[2]], False, False)
-        mm([], T.pa[:, COL[2]:CA], T.ones[0:1, :], T.lo[0:1, 0:CA - COL[2]], False, False)
-        mm([], T.pb[:, 0:NBK], T.ones[0:1, :], T.hi[0:1, CA:512], True, False)
-        mm([], T.pb[:, 0:NBK], T.ones[0:1, :], T.lo[0:1, 64 - NT:64 - NT + NBK], False, False)
+    def numbers(deps, banks="ab"):
+        if "a" in banks:
+            mm(deps, T.pa[:, 0:CA], T.ones[0:1, :], T.hi[0:1, 0:CA], True, False)
+            mm([], T.pa[:, 0:COL[2]], T.ones[0:1, :], T.lo[0:1, 0:COL[2]], False, False)
+            mm([], T.pa[:, COL[2]:CA], T.ones[0:1, :], T.lo[0:1, 0:CA - COL[2]], False, False)
+        if "b" in banks:
+            mm([], T.pb[:, 0:NBK], T.ones[0:1, :], T.hi[0:1, CA:512], True, False)
+            mm([], T.pb[:, 0:NBK], T.ones[0:1, :], T.lo[0:1, 64 - NT:64 - NT + NBK], False, False)
 
     def bank(lo, hi):
         return T.pa[:, lo:hi] if lo < CA else T.pb[:, NT + lo - CA:NT + hi - CA]
@@ -271,8 +279,10 @@ def rank_program(g, core, T, topo):
 
     def clear(t, off, deps):
         x = v(deps, V.tensor_copy, T.zl[:, 16 * t:16 * t + 16], T.tabs[:, 0:1536].indirect(off))
+        yield x
         x = v([x], V.tensor_copy, wb.indirect(T.zl[:, 16 * t:16 * t + 1]), T.zero[:])
-        return v([x], V.tensor_copy, wy.indirect(T.zl[:, 16 * t + 8:16 * t + 9]), T.zero[:])
+        yield x
+        yield v([x], V.tensor_copy, wy.indirect(T.zl[:, 16 * t + 8:16 * t + 9]), T.zero[:])
 
     t_mine = s([t_own, PEP], mine, pepw.indirect(T.w16[:, 4 * r:4 * r + 4]), ACT.Copy)
     for side, (tri, shift) in enumerate([(T.low, T.upp), (T.high, T.upn)]):
@@ -361,74 +371,94 @@ def rank_program(g, core, T, topo):
     mm([t_cz, t_tab], T.pz[:, 0:NZ], T.ones[0:1, :], T.cz[0:1, 0:NZ], True, False)
     p64 = mm([COL64], T.pt[:, 0:2], T.blk[:], T.c64[:, 0:2], True, True)
     best(0, 0, [ta])
-    e64 = v([], V.tensor_scalar, T.hit[:, 0, :], T.off[:, 0, :], 64.0, None, ALU.is_equal)
     red0 = best(0, 1, [tb])
     off0 = winner(0, [red0, t_cz], 0, 3)[1]
 
     x = v([off0], V.tensor_tensor, T.wm[:], T.mass[:, 0:512].indirect(T.woff[:, 0:2]), T.coef[:], ALU.mult)
-    z = mm([x], T.pz[:, 0:NZ], T.blk[:], T.wm[:, 0:NZ], False, True)
+    mm([x], T.pz[:, 0:C_Q], T.blk[:], T.wm[:, 0:C_Q], False, False)
+    z = mm([], T.pz[:, C_Q:NZ], T.ge[:], T.wm[:, C_Q:NZ], False, True)
+    t_s64 = s([p64], T.s64[:, 0:1], T.pt[:, 0:1], ACT.Copy)
     t_d = s([z], T.dist[:, 0:NZ], T.pz[:, 0:NZ], ACT.Abs)
-    t_u = [s([t_d], T.u[:, side, :], T.px[:, side, 0:NC], ACT.Abs, bias=T.dist[:, c:c + 1], scale=-2.0)
-           for side, c in enumerate((C_B, C_Y))]
-    PART = [(0, CA, T.ma), (CA, NC, T.mb)]
-    for lo, hi, bk in PART:
-        mm([k7], bk[:, lo:hi], T.eye[:], T.m0[:, lo:hi], True, False)
-        mm([e64], bk[:, lo:hi], T.eyen[:], T.hit[:, 0, lo:hi], False, False)
-    numbers([red0])
-    clear(0, T.woff[:, 2:3], [t_tab])
-    x = v([t_d], V.tensor_copy, T.dhi[:, 0:KS + 2], T.dist[:, C_S:C_B])
-    v([], V.tensor_tensor, T.mid[:, 0:KP], T.dist[:, C_A:C_S], T.dist[:, C_H:C_A], ALU.max)
-    t_h = v([], V.tensor_tensor, T.hh[:, 0:KP], T.dist[:, C_A:C_S], T.dist[:, C_H:C_A], ALU.min)
-    x = v([x], V.tensor_tensor, T.dlo[:, 0:KS + 2], T.dist[:, C_S:C_B], T.dhi[:, 0:KS + 2], ALU.subtract)
+    t_rank = s([t_d], T.junk[:, 0:16], T.dist[:, 0:16], ACT.Sign, bias=T.dist[:, C_Q:C_D], scale=-1.0, accum_out=T.col[:, 0:1])
+    steps = clear(0, T.woff[:, 2:3], [t_tab])
+    next(steps)
+    next(steps)
+    x = v([t_d], V.tensor_scalar, T.col[:, 1:2], T.dist[:, C_D:NZ], float(MID), 0.5, ALU.subtract, ALU.mult)
+    x = v([x, t_rank], V.tensor_scalar, T.ranked[:], T.rk[:], T.col[:, 0:1], T.col[:, 1:2], ALU.is_equal, ALU.mult)
+    numbers([red0], "a")
+    mm([x], T.pz[:, 32:48], T.blk[:], T.ranked[:], True, False)
+    x = mm([], T.pz[:, 32:47], T.blk[:], T.ranked[:, 1:16], False, True)
+    numbers([], "b")
+    next(steps)
+    t_kn = v([x], V.tensor_tensor, T.kn[:], T.pz[:, 32:48], T.ksh[:], ALU.add)
 
-    def lose(buf, j, part, deps, stop=False):
-        lo, hi, bk = part
-        for side in range(2):
-            tok = mm(deps, bk[:, lo:hi], T.eyen[:], buf[:, 2 * j + side, lo:hi], False, stop and side == 1)
-        return tok
+    def fold(lo, hi):
+        for side, c in enumerate((C_B, C_Y)):
+            x = s([t_d], T.u[:, side, lo:hi], T.px[:, side, lo:hi], ACT.Abs, bias=T.dist[:, c:c + 1], scale=-2.0)
+        return x
 
-    for side, c in enumerate((KS + 1, KS)):
-        y = v([x], V.tensor_scalar, T.hit[:, 2 + side, :], T.off[:, side, :], T.dhi[:, c:c + 1], T.dlo[:, c:c + 1],
-              ALU.subtract, ALU.is_equal)
-    for part in PART:
-        lose(T.hit, 1, part, [y])
-    for side in range(2):
-        t_u2 = v([t_u[side]], V.tensor_copy, T.u2[:, side, :], T.u[:, side, :])
+    def lower(lo, hi, x):
+        return s([x], T.ul[:, :, lo:hi], T.u[:, :, lo:hi], ACT.Identity, bias=-float(SHIFT))
 
-    def single(j):
-        x = v([t_u2], V.tensor_scalar, T.hit[:, 2 * j + 4:2 * j + 6, :], T.u2[:], T.dhi[:, j:j + 1], T.dlo[:, j:j + 1],
-              ALU.subtract, ALU.is_equal)
-        for part in PART:
-            lose(T.hit, j + 2, part, [x])
+    def vee(lo, hi, x):
+        return s([x, t_kn], T.zig[:, 14:16, lo:hi], T.u[:, :, lo:hi], ACT.Abs, bias=T.kn[:, 8:9], scale=-1.0)
 
-    def pair(p, part):
-        lo, hi, bk = part
-        f = T.fold[:, 2 * p:2 * p + 2, lo:hi]
-        x = s([t_u[1], t_h], f, T.u[:, :, lo:hi], ACT.Abs, bias=T.mid[:, p:p + 1], scale=-1.0)
-        x = v([x], V.tensor_scalar, f, f, T.hh[:, p:p + 1], None, ALU.is_equal)
-        return lose(T.fold, p, part, [x], p == KP - 1)
+    H = [T.mb, T.ma, T.pt]
+    t_u, t_ul, t_v = {}, {}, {}
+    t_u[0] = fold(0, PARTS[1])
+    t_u[1] = t_u[2] = fold(PARTS[1], NC)
+    t_ul[0] = lower(0, PARTS[1], t_u[0])
+    t_v[0] = vee(0, PARTS[1], t_u[0])
+    t_ul[1] = t_ul[2] = lower(PARTS[1], NC, t_u[1])
+    t_v[1] = t_v[2] = vee(PARTS[1], NC, t_u[1])
 
-    for p in range(KP):
-        if p < KS:
-            single(p)
-        done = pair(p, PART[0])
-    for p in range(KP):
-        if p == CLOSE:
-            x = v([done], V.tensor_scalar, T.m1[:, 0:CA], T.ma[:, 0:CA], 0.0, None, ALU.max)
-        last = pair(p, PART[1])
-        if p == CLOSE:
-            ta = score_own(T.m1, 0, CA, [x], True)
-    score_tail(T.m1, 0, CA)
-    t_s64 = s([p64], T.s64[:, 0:1], T.pt[:, 0:1], ACT.Identity, bias=-BIG / 1024)
-    x = s([last], T.m1[:, CA:NC], T.mb[:, CA:NC], ACT.Relu)
-    score_own(T.m1, CA, NC, [x])
-    tb = score_tail(T.m1, CA, NC, True)
-    best(1, 0, [ta])
+    def clamps(n, js):
+        lo, hi = PARTS[n], PARTS[n + 1]
+        for j in js:
+            a, source, tok = (2 * j, T.u, t_u[n]) if j < 4 else (2 * j + 1, T.ul, t_ul[n])
+            x = v([t_kn, tok], V.tensor_scalar, T.zig[:, 2 * j:2 * j + 2, lo:hi], source[:, :, lo:hi], T.kn[:, a:a + 1],
+                  T.kn[:, a + 1:a + 2], ALU.max, ALU.min)
+            if j == 6:
+                mm([t_v[n]], H[n][:, 0:2 * (hi - lo)], T.eyeh[:], T.zig[:, 14:16, lo:hi], False, False)
+            x = mm([x, k7, t_s64], H[n][:, 0:2 * (hi - lo)], T.eye[:] if j < 4 else T.eyen[:], T.zig[:, 2 * j:2 * j + 2, lo:hi],
+                   j == 0, j == 6)
+        return x
+
+    def size(n, deps):
+        width = 2 * (PARTS[n + 1] - PARTS[n])
+        return s(deps, H[n][:, 0:width], H[n][:, 0:width], ACT.Abs, bias=T.col[:, 2:3])
+
+    def kept(n, side, deps):
+        lo, hi = PARTS[n], PARTS[n + 1]
+        return v(deps, V.tensor_tensor, T.m1[:, lo:hi], H[n][:, side * (hi - lo):(side + 1) * (hi - lo)],
+                 (T.m1 if side else T.m0)[:, lo:hi], ALU.min)
+
+    def scores(n, x):
+        lo, hi = PARTS[n], PARTS[n + 1]
+        return score_own(T.m1, lo, hi, [x], hi == CA), score_tail(T.m1, lo, hi, hi == NC)
+
+    LOWER, UPPER = range(0, 4), range(4, 7)
+    x = v([t_kn], V.tensor_tensor, T.junk[:, 16:32], T.kn[:], T.kco[:], ALU.mult)
+    t_k = s([x], T.junk[:, 16:32], T.junk[:, 16:32], ACT.Identity, bias=-512.0 * MID / 16, accum_out=T.col[:, 2:3])
+    clamps(0, LOWER)
+    clamps(1, LOWER)
+    h0 = clamps(0, UPPER)
+    clamps(2, LOWER)
+    h1 = clamps(1, UPPER)
+    h2 = clamps(2, UPPER)
+    a0 = size(0, [h0, t_k])
     key, up = T.kab[:, 2:3], T.kab[:, 3:4]
-    v([], V.tensor_scalar, T.res[:, 0:1], T.nbig[:, 0:1], up, key, ALU.add, ALU.subtract)
-    res0 = v([t_s64], V.tensor_scalar, T.res[:, 2:3], up, 1.0 / 1024, T.s64[:, 0:1], ALU.mult, ALU.add)
+    y = s([], T.s64[:, 1:2], up, ACT.Identity, bias=-BIG)
+    a1 = size(1, [h1])
+    a2 = size(2, [h2])
+    s([y], T.res[:, 0:1], key, ACT.Identity, bias=T.s64[:, 1:2], scale=-1.0)
+    res0 = s([], T.res[:, 2:3], T.s64[:, 1:2], ACT.Identity, bias=T.s64[:, 0:1], scale=1.0 / 1024)
+    scores(0, kept(0, 1, [kept(0, 0, [a0])]))
+    ta = scores(1, kept(1, 1, [kept(1, 0, [a1])]))[0]
+    tb = scores(2, kept(2, 1, [kept(2, 0, [a2])]))[1]
+    best(1, 0, [ta])
     key1, off1 = winner(1, [best(1, 1, [tb])], 2, 3)
-    gone = clear(1, T.woff[:, 4:5], [off1])
+    *_, gone = clear(1, T.woff[:, 4:5], [off1])
 
     wait("y", [gone])
     g.sync.dma_start(T.left[:], T.S[:]).then_inc(sem.dleft, 16)

@@ -5,39 +5,45 @@ N, KC, W = 8, 64, 3072
 NT = 28
 COL = [0, 64, 100, 164, 228, 292, 356, 420, 484]
 NC, CA = COL[8], COL[6]
-NBK = NT + NC - CA
+NB = 512 - CA
 HALF = 1536
-OWN, NEAR, CONV2 = 32, (64, 82, 100), 0
-EDGE = [100, 132, 164, 196, 228, 260, 292, 324, 356, 388, 420, 452, 484]
-MADE = (0, 3)
-STAGE = (2, 6)
-KEEP = (3, 7, 11)
-PARTS = [0, 178, CA, NC]
+EARLY = [("s", 0, 32), ("s", 32, 64)]
+GAP = ["p5", "p4"]
+ROUND0 = {
+    "v": "y0-32 y32-64 c2 y64-82 y82-100 c3 a56 y100-132 y132-164 c45 y164-196 y196-228 y228-260 y260-292 c67 t y292-324 "
+         "k23 y324-356 y356-388 y388-420 y420-452 y452-484",
+    "s": "a34 c1 b64-82 b82-100 b100-132 b132-164 b164-196 b196-228 b228-260 b260-292 b292-324 b324-356 "
+         "b356-388 b388-420 b420-452 b452-484 f0123 x",
+    "p": "m1 m2 n m3 d0 m45 d1 p01 m67 t p23 x s23 d45 d6 eA eB d7 p67",
+}
+PARTS = [0, 190, 356, 428, NC]
+ASKS, LATER = [(0, 1, 2), (3, 4)], [(5, 6)]
+NA = 2
+ROUND1 = "u0 u123 l0 v0 l123 v123 L0 k K L1 U0 U1 L2 U2 L3 U3 a0 a1 a2 a3 r b0 y0 b1 s0 y1 s1 b2 b3 y2 y3 s2 s3 A"
 BIG = 1.5 * 2.0 ** 33
-C_B, C_Y, C_Q, C_D, NZ = 16, 17, 18, 19, 20
+C_B, C_Y, C_Q, C_P, C_N, C_S, NZ = 0, 1, 2, 18, 19, 20, 22
 MID, SHIFT = 1536, 1024
 
 BF, F16, F32, I32, U16 = "bfloat16", "float16", "float32", "int32", "uint16"
-SCRATCH = {"ll": ("sbuf", [128, 2, 8, 16], BF), "lt": ("sbuf", [128, 2, 128, 15], BF),
+SCRATCH = {"ll": ("sbuf", [128, 2, 8, 16], BF), "lh": ("sbuf", [128, 2, 8, 16], BF), "lt": ("sbuf", [128, 2, 128, 15], BF),
            "off": ("sbuf", [128, 2, NC], U16), "u": ("sbuf", [128, 2, NC], U16), "ul": ("sbuf", [128, 2, NC], F16),
-           "zig": ("sbuf", [128, 16, NC], F16), "px": ("psum", [128, 2, 512], F32)}
+           "run": ("sbuf", [128, 2, NB], F32), "zig": ("sbuf", [128, 16, NC], F16), "px": ("psum", [128, 2, 512], F32)}
 for _name, _cols, _dt in [
         ("wants", 32, I32), ("w16", 32, U16), ("loff", 32, U16), ("peps", W, BF), ("S", W, BF), ("gath", 448, BF),
         ("mass", 512, BF), ("offt", 32, U16), ("gb", 16 * NC, BF), ("gm", 16 * NC, BF), ("gt", 512, BF), ("m0", NC, BF),
         ("m1", NC, BF), ("iw", 128, I32), ("iu", 128, I32), ("sg", 128, I32), ("blk", 128, BF), ("blkn", 128, BF),
         ("blkp", 128, BF), ("blkq", 128, BF), ("blkt", 128, BF), ("eye", 128, BF), ("eyen", 128, BF), ("ge", 128, BF),
-        ("lbp", 128, BF), ("wd", 144, BF), ("ones", 128, BF), ("lo", 256, BF), ("hi", 512, BF), ("zero", 16, BF),
-        ("g16", 4, F32), ("gap", 16, F32), ("tri", 16, F32), ("lane", 4, F32), ("coef", 32, BF), ("cz", 32, BF),
-        ("nbig", 4, F32), ("wm", 32, BF), ("tabs", 1536, F32), ("dist", 32, F32), ("rk", 16, F32), ("ksh", 16, F32),
-        ("kco", 16, F32), ("kn", 16, F16), ("ranked", 16, F16), ("junk", 32, F32), ("col", 4, F32), ("blkh", 128, BF),
-        ("eyeh", 128, BF), ("s64", 4, F32), ("kab", 8, F32), ("woff", 8, U16), ("zl", 32, U16),
-        ("res", 4, F32), ("up", 128, BF), ("swap", 128, BF), ("low", 128, BF), ("high", 128, BF), ("upp", 128, BF),
-        ("upn", 128, BF), ("c64", 8, BF)]:
+        ("lbp", 128, BF), ("wd", 144, BF), ("ones", 128, BF), ("lo", 64, BF), ("num", 512, F16), ("zero", 16, BF),
+        ("g16", 4, F32), ("gap", 16, F32), ("tri", 16, F32), ("lane", 4, F32), ("coef", 48, BF), ("cz", 32, BF),
+        ("nbig", 8, F32), ("wm", 48, BF), ("tabs", 1536, F32), ("dist", 32, F32), ("rk", 32, F32), ("ksh", 16, F32),
+        ("kco", 16, F32), ("kn", 16, F16), ("ranked", 32, F16), ("junk", 32, F32), ("col", 4, F32), ("blkh", 128, BF),
+        ("eyeh", 128, BF), ("s64", 4, F32), ("kab", 8, F32), ("woff", 8, U16), ("zl", 32, U16), ("sgn", 128, BF),
+        ("res", 4, F32), ("upp", 128, BF), ("upn", 128, BF), ("c64", 8, BF)]:
     SCRATCH[_name] = ("sbuf", [128, _cols], _dt)
 for _name in ["ma", "mb", "pa", "pb", "pt", "pz"]:
     SCRATCH[_name] = ("psum", [128, 512], F32)
-SEMAPHORES = ["qv", "qs", "qp", "qg", "dwant", "dpep", "dspec", "dleft", "dres",
-              "ask0", "ask1", "ask2", "ask3", "dlow", "dcol", "dpea", "dpeb", "sent", "rep0", "rep1", "rep2", "rep3"]
+SEMAPHORES = ["qv", "qs", "qp", "qg", "dwant", "dspec", "dleft", "dres", "dlow", "dcol", "dpea", "dpeb", "sent",
+              "ask0", "ask1", "ask2", "ask3", "rep0", "rep1", "rep2", "rep3", "rep4"]
 
 ALU = AluOpType
 ACT = ActivationFunctionType
@@ -72,7 +78,7 @@ def rank_program(g, core, T, topo):
     if r is None:
         return
     order = partner_order(T, topo, core)
-    src = [r] + order
+    src = [r] + order[0:3] + sorted(order[3:5]) + sorted(order[5:7])
     place = [partner_order(T, topo, T.cores[q]).index(r) for q in order]
     addr = [topo.addr(T.cores[q]) for q in order]
     far = topo.engines(core, T.cores[order[1]])
@@ -107,87 +113,91 @@ def rank_program(g, core, T, topo):
     def mm(deps, out, lhsT, rhs, start, stop):
         return op("p", deps, P.matmul, out, lhsT, rhs, start, stop)
 
+    def copy(q, deps, out, in_):
+        return s(deps, out, in_, ACT.Copy) if q == "s" else v(deps, V.tensor_copy, out, in_)
+
     g.sync.dma_start(T.wants[:], T.want[:]).then_inc(sem.dwant, 16)
     g.sync.dma_start(T.peps[:, 0:HALF], T.pep[:, 0:HALF]).then_inc(sem.dpea, 16)
     g.sync.dma_start(T.peps[:, HALF:W], T.pep[:, HALF:W]).then_inc(sem.dpeb, 16)
     wait("y", [("dpea", 16)])
     g.sync.dma_start(T.S[:, 0:HALF], T.spec[:, 0:HALF]).then_inc(sem.dlow, 16)
     wait("y", [("dpeb", 16)])
-    g.sync.sem_inc(sem.dpep, 16)
     g.sync.dma_start(T.S[:, HALF:W], T.spec[:, HALF:W]).then_inc(sem.dspec, 16)
     g.sync.dma_start(T.c64[:, 0:2], T.spec[:, 64:66]).then_inc(sem.dcol, 16)
-    WANT, PEP, LOW, SPEC, COL64 = ("dwant", 16), ("dpep", 16), ("dlow", 16), ("dspec", 16), ("dcol", 16)
+    WANT, LOW, SPEC, COL64 = ("dwant", 16), ("dlow", 16), ("dspec", 16), ("dcol", 16)
+    PEP = [("dpea", 16), ("dpeb", 16)]
+
+    def level(out, value, pattern=None):
+        return op("g", [], g.iota, out, pattern or [[0, out.shape[1]]], value, 0, allow_small_or_imprecise_dtypes=True)
 
     t_iw = op("g", [], g.iota, T.iw[:], [[16, 8], [0, 16]], 15, -1)
     t_iu = op("g", [], g.iota, T.iu[:], [[1, 128]], 0, -1)
-    t_up = op("g", [], g.iota, T.up[:], [[0, 8], [1, 2], [0, 8]], 0, 0, allow_small_or_imprecise_dtypes=True)
+    t_up = level(T.upp[0:1, :], 0, [[0, 8], [64, 2], [0, 8]])
+    t_lo = level(T.lo[0:1, :], 0, [[-1, 64]])
     v([], V.memset, T.lt[:, 0], 0.0)
     t_own = v([WANT], V.tensor_copy, T.w16[:], T.wants[:])
 
     def transfer(k, name, source, landing):
         engines = near if k == 0 else far[hf * ((k - 1) % 2):hf * ((k - 1) % 2) + hf]
+        if name == "rep" and k in (1, 2):
+            engines = far
         return RemoteDMATransfer(dst_ids=[DstId(rid=addr[k][0], pnc=addr[k][1])], dma_engine_mask=bits(engines),
-                                 remote_sem=sem["%s%d" % (name, (k + 1) // 2)], src=source, dst=landing)
+                                 remote_sem=sem[name + ("0142233" if name == "rep" else "0112233")[k]], src=source, dst=landing)
 
     wait("g", [t_own])
-
     def ask(ks):
         g.remote_dma_fused([transfer(k, "ask", T.w16[:, 4 * order[k]:4 * order[k] + 4],
                                      T.loff[:, 4 * place[k]:4 * place[k] + 4]) for k in ks], local_sem=sem.sent)
 
-    for ks in [(0, 1, 2), (3, 4), (5, 6)]:
+    for ks in ASKS:
         ask(ks)
-    t_lo = op("g", [], g.iota, T.lo[0:1, :], [[0, 4], [-1, 64]], 0, 0, allow_small_or_imprecise_dtypes=True)
 
     t_sg = v([t_iw], V.tensor_scalar, T.sg[:], T.iw[:], 4, None, ALU.arith_shift_right)
     t_ge = v([t_iu], V.tensor_scalar, T.ge[:], T.iu[:], 0.0, None, ALU.is_ge)
+    t_ones = v([], V.memset, T.ones[0:1, :], 1.0)
     t_blk = v([t_sg], V.tensor_scalar, T.blk[:], T.sg[:], 0.0, None, ALU.is_equal)
     t_g16 = v([], V.tensor_scalar, T.g16[:, 0:1], T.sg[:, 0:1], -16.0, None, ALU.mult)
+    t_wd0 = v([], V.memset, T.wd[:], 0.0)
     t_lb = v([t_ge, t_blk], V.tensor_tensor, T.ll[:, 0], T.ge[:], T.blk[:], ALU.mult)
     t_dif = v([t_g16], V.tensor_scalar, T.gap[:], T.iu[:, 0:16], T.g16[:, 0:1], None, ALU.add)
+    t_wd = v([t_wd0], V.tensor_copy, T.wd[:, 15:128:16], T.blk[:, 15:128:16])
     t_ly = v([t_lb], V.tensor_tensor, T.ll[:, 1], T.blk[:], T.ll[:, 0], ALU.subtract)
     t_tri = v([t_dif], V.tensor_scalar, T.tri[:], T.gap[:], 0.0, None, ALU.is_ge)
-    x = v([t_ly], V.tensor_tensor, T.ge[:], T.ll[:, 1], T.ll[:, 0], ALU.subtract)
-    t_wd0 = v([], V.memset, T.wd[:], 0.0)
-    x = v([x, t_up], V.tensor_tensor, T.swap[:], T.ge[:], T.up[:], ALU.mult)
-    v([x], V.tensor_tensor, T.low[:], T.ll[:, 0], T.swap[:], ALU.add)
-    t_high = v([], V.tensor_tensor, T.high[:], T.ll[:, 1], T.swap[:], ALU.subtract)
-    t_wd = v([t_wd0], V.tensor_copy, T.wd[:, 15:128:16], T.blk[:, 15:128:16])
-
-    def constants_of_the_tail(x):
-        v([t_wd], V.tensor_tensor, T.lbp[:], T.ll[:, 0], T.wd[:, 0:128], ALU.subtract)
-        return v([x], V.tensor_copy, T.lt[:, :, 15:128:16, :], T.ll[:, :, :, 0:15])
+    v([], V.memset, T.nbig[:, 0:4], -BIG)
+    v([], V.memset, T.cz[0:1, C_Q:C_P], -127.5)
+    for j in range(2):
+        v([], V.memset, T.coef[:, 34 + j:35 + j], j - 0.5)
+    v([t_ly], V.tensor_copy, T.lh[:, :, :, 0:8], T.ll[:, :, :, 0:8])
+    for side in range(2):
+        t_high = v([], V.tensor_copy, T.lh[:, side, :, 8:16], T.ll[:, 1 - side, :, 8:16])
+    v([t_wd], V.tensor_tensor, T.lbp[:], T.ll[:, 0], T.wd[:, 0:128], ALU.subtract)
+    t_lt = v([], V.memset, T.lt[:, 1], 0.0)
 
     def fill(out, like, value):
         return s([], out, like, ACT.Identity, bias=float(value), scale=0.0)
 
-    banked = [(0, 0, 64), (1, 0, 64 - NT), (2, 0, 64), (3, 0, 64), (4, 0, 64), (5, 0, 64), (1, 64 - NT, 64), (6, 0, 64),
-              (7, 0, 64)]
-    s([t_up], T.upp[0:1, :], T.up[0:1, :], ACT.Copy, scale=64.0)
-    s([], T.upn[0:1, :], T.up[0:1, :], ACT.Copy, scale=-64.0)
-    t_ones = fill(T.ones[0:1, :], T.up[0:1, :], 1)
+    t_upn = s([t_up], T.upn[0:1, :], T.upp[0:1, :], ACT.Copy, scale=-1.0)
     t_blkp = s([t_blk], T.blkp[:], T.blk[:], ACT.Copy, scale=1024.0)
     t_blkn = s([], T.blkn[:], T.blk[:], ACT.Copy, scale=-1024.0)
-    fill(T.nbig[:, 0:2], T.blk[:, 0:2], -BIG)
     t_blkh = s([], T.blkh[:], T.blk[:], ACT.Copy, scale=512.0)
-    s([t_dif], T.coef[:, 0:16], T.gap[:], ACT.Sign, bias=0.5)
-    fill(T.cz[0:1, 0:C_B], T.up[0:1, 0:C_B], -63.75)
-    fill(T.cz[0:1, C_Q:C_D], T.up[0:1, 0:1], 63.75)
-    x = s([], T.lane[:, 0:1], T.gap[:, 14:15], ACT.Relu, scale=-1.0)
-    s([t_tri], T.nbig[:, 2:3], T.tri[:, 7:8], ACT.Identity, bias=1024.0 - BIG, scale=-1024.0)
-    s([t_blkp], T.blkq[:], T.blkp[:], ACT.Copy, scale=T.tri[:, 14:15])
+    x = s([t_dif], T.lane[:, 0:1], T.gap[:, 14:15], ACT.Relu, scale=-1.0)
+    s([], T.coef[:, C_Q:C_P], T.gap[:], ACT.Sign, bias=0.5)
+    t_lane = s([], T.lane[:, 1:2], T.gap[:, 0:1], ACT.Identity, bias=14.0, scale=4.0)
+    s([t_blkp, t_tri], T.blkq[:], T.blkp[:], ACT.Copy, scale=T.tri[:, 14:15])
+    s([], T.nbig[:, 4:5], T.tri[:, 7:8], ACT.Identity, bias=1024.0 - BIG, scale=-1024.0)
     t_blkt = s([x], T.blkt[:], T.blkp[:], ACT.Copy, scale=T.lane[:, 0:1])
-
-    def level(out, value, pattern=None):
-        return op("g", [], g.iota, out, pattern or [[0, out.shape[1]]], value, 0, allow_small_or_imprecise_dtypes=True)
+    s([], T.rk[:, 0:16], T.gap[:], ACT.Identity, bias=16.0, scale=2.0)
+    s([t_lane], T.rk[:, 16:32], T.gap[:], ACT.Identity, bias=T.lane[:, 1:2], scale=-2.0)
 
     def late_constants():
         level(T.cz[0:1, C_B:C_Q], 64, [[-128, 2]])
-        level(T.cz[0:1, C_D:NZ], 64)
-        level(T.coef[:, 16:32], 1)
+        level(T.cz[0:1, C_P:C_S], -32 - MID // 2, [[64, 2]])
+        level(T.cz[0:1, C_S:NZ], 0)
+        level(T.coef[:, C_B:C_Q], 1)
+        level(T.coef[:, C_P:34], -1)
+        level(T.coef[:, 36:48], 0)
         level(T.zero[:], 0)
         level(T.tabs[:, 512:1024], 0)
-        level(T.rk[:], -15, [[2, 16]])
         for lo, hi, val in [(0, 9, MID), (9, 15, MID - SHIFT), (15, 16, 0)]:
             level(T.ksh[:, lo:hi], val)
         level(T.kco[:, 0:8], 0, [[0, 4], [-1024, 2]])
@@ -198,66 +208,43 @@ def rank_program(g, core, T, topo):
             x = op("g", [tok], g.affine_select, eye[:], blk[:], [[-1, 128]], ALU.is_equal, 0.0, 0, 1)
         return x
 
+    split = [CA]
+
     def numbers(deps, banks="ab"):
         if "a" in banks:
-            mm(deps, T.pa[:, 0:CA], T.ones[0:1, :], T.hi[0:1, 0:CA], True, False)
-            mm([], T.pa[:, 0:COL[2]], T.ones[0:1, :], T.lo[0:1, 0:COL[2]], False, False)
-            mm([], T.pa[:, COL[2]:CA], T.ones[0:1, :], T.lo[0:1, 0:CA - COL[2]], False, False)
+            x = mm(deps, T.pa[:, 0:CA], T.ones[0:1, :], T.num[0:1, 0:CA], True, False)
         if "b" in banks:
-            mm([], T.pb[:, 0:NBK], T.ones[0:1, :], T.hi[0:1, CA:512], True, False)
-            mm([], T.pb[:, 0:NBK], T.ones[0:1, :], T.lo[0:1, 64 - NT:64 - NT + NBK], False, False)
+            x = mm([], T.pb[:, 0:512 - CA], T.ones[0:1, :], T.num[0:1, CA:512], True, False)
+        return x
 
     def bank(lo, hi):
-        return T.pa[:, lo:hi] if lo < CA else T.pb[:, NT + lo - CA:NT + hi - CA]
+        ca = split[0]
+        return T.pa[:, lo:hi] if lo < ca else T.pb[:, NT + lo - ca:NT + hi - ca]
 
     pepw = T.peps[:, 0:W]
     mine = T.mass[:, 64 * r:64 * r + 64]
     tail = 64 * src[1] + 64 - NT
 
-    def answer(ks, q="s"):
-        asked = ("ask0", len(near)) if ks == [0] else ("ask%d" % (ks[1] // 2), nfar)
-        out, wanted = T.gath[:, 64 * ks[0]:64 * ks[-1] + 64], pepw.indirect(T.loff[:, 4 * ks[0]:4 * ks[-1] + 4])
-        wait("g", [s([asked], out, wanted, ACT.Copy) if q == "s" else v([asked, PEP], V.tensor_copy, out, wanted)])
+    def answer(ks, q):
+        asked = ("ask%d" % ((ks[0] + 1) // 2), nfar if ks[0] else len(near))
+        x = copy(q, [asked] + PEP, T.gath[:, 64 * ks[0]:64 * ks[-1] + 64], pepw.indirect(T.loff[:, 4 * ks[0]:4 * ks[-1] + 4]))
+        wait("g", [x])
         g.remote_dma_fused([transfer(k, "rep", T.gath[:, 64 * k:64 * k + 64], mine) for k in ks], local_sem=sem.sent)
+        return x
 
-    def lists(ks, deps):
-        for k in ks:
-            lo, hi = COL[k], COL[k + 1]
-            rhs = T.mass[:, 64 * src[k]:64 * src[k] + hi - lo]
-            runs = tail_runs(lo, hi)
-            for side in range(2):
-                tok = mm(deps, T.px[:, side, lo:hi], T.ll[:, 1] if side else T.lbp[:], rhs, True, False)
-                for f, a, b, c in runs:
-                    tok = mm([], T.px[:, side, a:b], T.lt[:, side, :, f], T.mass[:, tail + c:tail + c + b - a], False, b == hi)
-        return tok
-
-    def conv(ks, tok):
+    def lists(ks, sides, deps):
         lo, hi = COL[ks[0]], COL[ks[-1] + 1]
-        return v([tok], V.tensor_copy, T.off[:, :, lo:hi], T.px[:, :, lo:hi])
+        rhs = T.mass[:, 64 * src[ks[0]]:64 * src[ks[0]] + hi - lo]
+        for side in sides:
+            tok = mm(deps, T.px[:, side, lo:hi], T.ll[:, 1] if side else T.lbp[:], rhs, True, False)
+            for f, a, b, c in tail_runs(lo, hi):
+                tok = mm([], T.px[:, side, a:b], T.lt[:, side, :, f], T.mass[:, tail + c:tail + c + b - a], False, b == hi)
+        return tok
 
     wb, wy = T.S[:, 0:W], T.S[:, 64:W]
 
-    def look_b(q, lo, hi, deps):
-        if q == "v":
-            return v(deps, V.tensor_copy, T.gb[:, 16 * lo:16 * hi], wb.indirect(T.off[:, 0, lo:hi]))
-        return s(deps, T.gb[:, 16 * lo:16 * hi], wb.indirect(T.off[:, 0, lo:hi]), ACT.Copy)
-
-    def look_y(lo, hi, deps):
-        return v(deps, V.tensor_tensor, T.gm[:, 16 * lo:16 * hi], wy.indirect(T.off[:, 1, lo:hi]), T.gb[:, 16 * lo:16 * hi],
-                 ALU.min)
-
     def slot(lo, hi, i):
         return T.gm[:, 16 * lo + i:16 * hi:16]
-
-    def compact(k, M, deps):
-        lo, hi = COL[k], COL[k + 1]
-        for i in range(16 if k else 15):
-            tok = mm(deps, M[:, lo:hi], T.wd[:, 15 - i:143 - i], slot(lo, hi, i), i == 0, i == (15 if k else 14))
-        return tok
-
-    def keep(ks, M, deps):
-        lo, hi = COL[ks[0]], COL[ks[-1] + 1]
-        return s(deps, T.m0[:, lo:hi], M[:, lo:hi], ACT.Copy)
 
     def score_own(m, lo, hi, deps, stop=False):
         return mm(deps, bank(lo, hi), T.blkq[:], m[:, lo:hi], False, stop)
@@ -268,14 +255,15 @@ def rank_program(g, core, T, topo):
         return tok
 
     def best(t, half, deps):
-        return v(deps, V.tensor_reduce, T.kab[:, 4 * t + half:4 * t + half + 1], T.pb[:, 0:NBK] if half else T.pa[:, 0:CA],
-                 AxisListType.X, ALU.max)
+        ka = T.kab[:, 2 * t:2 * t + 1]
+        if half:
+            return v(deps, V.tensor_tensor_scan, T.run[:, t], T.pb[:, 0:NB], T.tabs[:, 512:512 + NB], ka, ALU.max, ALU.add)
+        return v(deps, V.tensor_reduce, ka, T.pa[:, 0:CA], AxisListType.X, ALU.max)
 
-    def winner(t, deps, lo, hi):
-        ka, kb, key, up = [T.kab[:, 4 * t + j:4 * t + j + 1] for j in range(4)]
-        v(deps, V.tensor_scalar, up, kb, ka, BIG, ALU.max, ALU.add)
-        y = v([], V.tensor_scalar, key, kb, ka, None, ALU.max)
-        return y, v([y], V.tensor_scalar, T.woff[:, 4 * t:4 * t + hi - lo], T.nbig[:, lo:hi], up, key, ALU.add, ALU.subtract)
+    def winner(t, deps, out, base):
+        key, up = T.run[:, t, NB - 1:NB], T.kab[:, 2 * t + 1:2 * t + 2]
+        y = v(deps, V.tensor_scalar, up, key, BIG, None, ALU.add)
+        return y, v([y], V.tensor_scalar, out, base, up, key, ALU.add, ALU.subtract)
 
     def clear(t, off, deps):
         x = v(deps, V.tensor_copy, T.zl[:, 16 * t:16 * t + 16], T.tabs[:, 0:1536].indirect(off))
@@ -284,113 +272,160 @@ def rank_program(g, core, T, topo):
         yield x
         yield v([x], V.tensor_copy, wy.indirect(T.zl[:, 16 * t + 8:16 * t + 9]), T.zero[:])
 
-    t_mine = s([t_own, PEP], mine, pepw.indirect(T.w16[:, 4 * r:4 * r + 4]), ACT.Copy)
-    for side, (tri, shift) in enumerate([(T.low, T.upp), (T.high, T.upn)]):
-        mm([t_mine, t_high], T.px[:, side, 0:64], tri[:], mine, True, False)
-        made = mm([t_ones], T.px[:, side, 0:64], shift[0:1, :], T.ones[0:1, 0:64], False, True)
-    t_lt1 = v([], V.memset, T.lt[:, 1], 0.0)
-    c0 = conv([0], made)
+    t_mine = s([t_own] + PEP, mine, pepw.indirect(T.w16[:, 4 * r:4 * r + 4]), ACT.Copy)
+    for side, shift in enumerate([T.upp, T.upn]):
+        mm([t_mine, t_high], T.px[:, side, 0:64], T.lh[:, side], mine, True, False)
+        made = mm([t_ones, t_upn], T.px[:, side, 0:64], shift[0:1, :], T.ones[0:1, 0:64], False, True)
+    c0 = v([made], V.tensor_copy, T.off[:, :, 0:64], T.px[:, :, 0:64])
     at = 0
-    for k, a, b in banked:
-        t_hi = fill(T.hi[0:1, at:at + b - a], T.blk[0:1, 0:b - a], -64 * src[k])
+    for k, a, b in [(k, 0, COL[k + 1] - COL[k]) for k in range(6)] + [(1, 64 - NT, 64), (6, 0, 64), (7, 0, 64)]:
+        t_num = s([t_lo], T.num[0:1, at:at + b - a], T.lo[0:1, a:b], ACT.Identity, bias=-64.0 * src[k])
         at += b - a
+    t_const = v([t_lt], V.tensor_copy, T.lt[:, :, 15:128:16, :], T.ll[:, :, :, 0:15])
     answer([0], "v")
-    answer([1, 2], "v")
-    t_const = constants_of_the_tail(t_lt1)
-    x = s([LOW, c0], T.gb[:, 0:512], T.S[:, 0:HALF].indirect(T.off[:, 0, 0:32]), ACT.Copy)
-    y = s([], T.gb[:, 512:1024], T.S[:, 0:HALF].indirect(T.off[:, 0, 32:64]), ACT.Copy)
-    answer([3, 4])
-    answer([5, 6])
-    t_cz = late_constants()
-    look_y(0, 32, [x, SPEC, LOW])
-    if OWN > 32:
-        look_y(32, OWN, [y])
-    c1 = conv([1], lists([1], [("rep0", len(near)), c0, t_const]))
-    m_own = look_y(OWN, 64, [y])
-    made = lists([2], [("rep1", nfar), c1])
-    got = [look_b("s", a, b, [c1, SPEC]) for a, b in zip(NEAR, NEAR[1:])]
-    ready = {}
-    for n, x in enumerate(got):
-        if n == CONV2:
-            ready[2] = conv([2], made)
-            made = lists([3], [ready[2]])
-        m_near = look_y(NEAR[n], NEAR[n + 1], [x])
-    ready[3] = conv([3], made)
-    M = {0: T.ma, 1: T.ma, 2: T.mb, 3: T.mb, 4: T.ma, 5: T.ma, 6: T.mb, 7: T.ma}
-    compact(0, M[0], [m_own])
-    ctok, ktok = {1: compact(1, M[1], [m_near])}, {}
-    for b, (lo, hi) in enumerate(zip(EDGE, EDGE[1:])):
-        k = max(j for j in range(8) if COL[j] < hi)
-        if b == KEEP[0]:
-            numbers([t_lo, t_hi])
-        if b == MADE[0]:
-            made = lists([4, 5], [("rep2", nfar), ready[3]])
-        if b == STAGE[0]:
-            ready[4] = ready[5] = conv([4, 5], made)
-        if b == MADE[1]:
-            made = lists([6, 7], [("rep3", nfar), ready[4]])
-            for p in range(16):
-                tl = mm([], T.pt[:, 0:32], T.wd[:, 15 - p:143 - p], T.mass[:, p:512:16], p == 0, p == 15)
-        if b == STAGE[1]:
-            ready[6] = ready[7] = conv([6, 7], made)
-            ct = v([tl], V.tensor_copy, T.offt[:], T.pt[:, 0:32])
-            mm([], T.pz[:], T.ll[:, 1], T.mass[:], True, True)
-            tabp = mm([ct], T.pt[:], T.ll[:, 0], T.mass[:], True, True)
-        if b in KEEP:
-            ks = [2 * KEEP.index(b), 2 * KEEP.index(b) + 1]
-            ktok[ks[1]] = keep(ks, M[ks[0]], [ctok[ks[1]]])
-        mtok = look_y(lo, hi, [look_b("s", lo, hi, [ready[k]])])
-        if b in KEEP:
-            score_own(T.m0, COL[ks[0]], COL[ks[1] + 1], [ktok[ks[1]], t_blkt])
-            score_tail(T.m0, COL[ks[0]], COL[ks[1] + 1])
-        for k in range(2, 7):
-            if lo < COL[k + 1] <= hi:
-                ctok[k] = compact(k, M[k], [mtok] + ([ktok[k - 3]] if k in (4, 6) else []))
-    q = min(src[6:8])
-    for a, b in [(0, q), (q + 2, N)]:
-        if a < b:
-            tg = s([ct, COL64], T.gt[:, 64 * a:64 * b], wb.indirect(T.offt[:, 4 * a:4 * b]), ACT.Relu, bias=T.c64[:, 0:1],
-                   scale=-1.0)
-    tv = v([COL64], V.tensor_scalar, T.gt[:, 64 * q:64 * q + 128], wb.indirect(T.offt[:, 4 * q:4 * q + 8]), T.c64[:, 0:1],
-           0.0, ALU.subtract, ALU.min)
-    k6 = keep([6], M[6], [ctok[6]])
-    s([tabp], T.tabs[:, 0:512], T.pt[:], ACT.Copy)
-    t_tab = s([], T.tabs[:, 1024:1536], T.pz[:], ACT.Copy)
-    for k in range(6):
-        ta = mm([tg], bank(COL[k], COL[k + 1]), T.blkn[:], T.gt[:, 64 * src[k]:64 * src[k] + COL[k + 1] - COL[k]], False, k == 5)
-    mm([], T.pb[:, 0:NT], T.blkn[:], T.gt[:, tail:tail + NT], False, False)
-    score_own(T.m0, COL[6], COL[7], [k6])
-    score_tail(T.m0, COL[6], COL[7])
-    for i in range(15):
-        mm([mtok], bank(COL[7], NC), T.blkp[:], slot(COL[7], NC, i), False, False)
-    for f, a, b, c in tail_runs(COL[7], NC):
-        mm([], T.pb[:, c:c + b - a], T.blkp[:], slot(a, b, 15), False, False)
-    for k in (6, 7):
-        tb = mm([tv], bank(COL[k], COL[k + 1]), T.blkp[:], T.gt[:, 64 * src[k]:64 * src[k] + 64], False, k == 7)
-    k7 = keep([7], M[7], [compact(7, M[7], [ktok[5]])])
-    mm([t_cz, t_tab], T.pz[:, 0:NZ], T.ones[0:1, :], T.cz[0:1, 0:NZ], True, False)
-    p64 = mm([COL64], T.pt[:, 0:2], T.blk[:], T.c64[:, 0:2], True, True)
-    best(0, 0, [ta])
-    red0 = best(0, 1, [tb])
-    off0 = winner(0, [red0, t_cz], 0, 3)[1]
+    answer([1], "v")
+    answer([2], "v")
+    for ks in LATER:
+        ask(ks)
+    tok = {("c", 0, 0): c0, ("c", 0, 1): c0}
+    for q, lo, hi in EARLY:
+        x = copy(q, [LOW, c0], T.gb[:, 16 * lo:16 * hi], T.S[:, 0:HALF].indirect(T.off[:, 0, lo:hi]))
+        tok.update({("b", c): x for c in range(lo, hi)})
+    last_made = {0: [0], 1: [0]}
 
-    x = v([off0], V.tensor_tensor, T.wm[:], T.mass[:, 0:512].indirect(T.woff[:, 0:2]), T.coef[:], ALU.mult)
-    mm([x], T.pz[:, 0:C_Q], T.blk[:], T.wm[:, 0:C_Q], False, False)
-    z = mm([], T.pz[:, C_Q:NZ], T.ge[:], T.wm[:, C_Q:NZ], False, True)
-    t_s64 = s([p64], T.s64[:, 0:1], T.pt[:, 0:1], ACT.Copy)
-    t_d = s([z], T.dist[:, 0:NZ], T.pz[:, 0:NZ], ACT.Abs)
-    t_rank = s([t_d], T.junk[:, 0:16], T.dist[:, 0:16], ACT.Sign, bias=T.dist[:, C_Q:C_D], scale=-1.0, accum_out=T.col[:, 0:1])
-    steps = clear(0, T.woff[:, 2:3], [t_tab])
+    def step(q, word):
+        kind, rest = word[0], word[1:]
+        if kind in "by":
+            lo, hi = [int(c) for c in rest.split("-")]
+            side = int(kind == "y")
+            need = [("c", k, side) for k in range(8) if COL[k] < hi and lo < COL[k + 1]]
+            need += [("b", c) for c in range(lo, hi)] if side else []
+            gives = [(kind, c) for c in range(lo, hi)]
+        elif kind in "cm":
+            sides = [0] if rest[-1] == "b" else [1] if rest[-1] == "y" else [0, 1]
+            ks = [int(c) for c in rest if c.isdigit()]
+            if kind == "c":
+                need = [("m", k, side) for k in ks for side in sides]
+            else:
+                need = [("c", k, side) for side in sides for k in last_made[side]]
+            gives = [(kind, k, side) for k in ks for side in sides]
+            lo, hi = COL[ks[0]], COL[ks[-1] + 1]
+        elif kind in "pdks":
+            ks = [int(c) for c in rest]
+            lo, hi = COL[ks[0]], COL[ks[-1] + 1]
+            need = [("y", c) for c in range(lo, hi)] if kind in "pd" else [("p" if kind == "k" else "k", ks[0])]
+            need += [w for w in tok if w[0] == "k"] if kind == "p" else []
+            gives = [(kind, k) for k in ks]
+        elif kind == "f":
+            need, gives = [("t",)], [("f", int(c)) for c in rest]
+        else:
+            need = {"tv": [("tp",)], "ts": [("tp",)], "tp": [("m", 7, 0)], "xp": [("t",)], "xs": [("xp",)],
+                    "eA": [("f", 0), ("f", 1), ("f", 2)], "eB": [("f", 3)]}.get(
+                        word if len(word) == 2 else kind + q, [])
+            gives = [(word + q if word in "tx" and q == "p" else word,)]
+        if any(n not in tok for n in need):
+            return None
+        deps = sorted(set(tok[n] for n in need))
+        if kind == "b":
+            x = copy(q, deps + [SPEC], T.gb[:, 16 * lo:16 * hi], wb.indirect(T.off[:, 0, lo:hi]))
+        elif kind == "y":
+            x = v(deps + [LOW, SPEC], V.tensor_tensor, T.gm[:, 16 * lo:16 * hi], wy.indirect(T.off[:, 1, lo:hi]),
+                  T.gb[:, 16 * lo:16 * hi], ALU.min)
+        elif kind == "c":
+            x = copy(q, deps, T.off[:, sides[0]:sides[-1] + 1, lo:hi], T.px[:, sides[0]:sides[-1] + 1, lo:hi])
+        elif kind == "m":
+            x = lists(ks, sides, deps + [("rep" + "0142233"[ks[0] - 1], nfar if ks[0] > 1 else len(near)), t_const])
+            last_made.update({side: ks for side in sides})
+        elif kind == "p":
+            for i in range(16):
+                x = mm(deps, T.ma[:, lo:hi], T.wd[:, 15 - i:143 - i], slot(lo, hi, i), i == 0, i == 15)
+        elif kind == "k":
+            x = copy(q, deps, T.m0[:, lo:hi], T.ma[:, lo:hi])
+        elif kind == "s":
+            x = score_own(T.m0, lo, hi, deps + [t_blkt])
+            x = score_tail(T.m0, lo, hi)
+        elif kind == "d":
+            for f, a, b, c in tail_runs(lo, hi):
+                mm(deps + [t_blkp], T.pb[:, c:c + b - a], T.blkp[:], slot(a, b, 15), False, False)
+            for i in range(15):
+                x = mm(deps + [t_blkp], bank(lo, hi), T.blkp[:], slot(lo, hi, i), False, hi == NC and i == 14)
+        elif kind == "a":
+            x = answer([int(c) for c in rest], q)
+            if rest == "56":
+                tok["late",] = late_constants()
+        elif kind == "n":
+            x = numbers([t_num])
+        elif word == "t" and q == "p":
+            for p in range(16):
+                x = mm([], T.pt[:, 0:32], T.wd[:, 15 - p:143 - p], T.mass[:, p:512:16], p == 0, p == 15)
+        elif word == "t":
+            x = copy(q, deps, T.offt[:], T.pt[:, 0:32])
+        elif word == "x" and q == "p":
+            mm([], T.pz[:], T.ll[:, 1], T.mass[:], True, True)
+            x = mm(deps, T.pt[:], T.ll[:, 0], T.mass[:], True, True)
+        elif word == "x":
+            copy(q, deps, T.tabs[:, 0:512], T.pt[:])
+            x = copy(q, [], T.tabs[:, 1024:1536], T.pz[:])
+        elif kind == "f":
+            ranks = sorted(src[2 * int(c) + j] for c in rest for j in range(2))
+            for a in [a for a in ranks if a - 1 not in ranks]:
+                b = min(b for b in range(a, N + 1) if b not in ranks)
+                out, at = T.gt[:, 64 * a:64 * b], wb.indirect(T.offt[:, 4 * a:4 * b])
+                if q == "s":
+                    x = s(deps + [COL64], out, at, ACT.Relu, bias=T.c64[:, 0:1], scale=-1.0)
+                else:
+                    x = v(deps + [COL64], V.tensor_scalar, out, at, T.c64[:, 0:1], 0.0, ALU.subtract, ALU.min)
+            tok.update({("sign", int(c)): T.blkn if q == "s" else T.blkp for c in rest})
+        elif word == "eA":
+            for k, end in [(0, 1), (1, 2), (2, 3), (3, 4), (4, 6)]:
+                x = mm(deps, bank(COL[k], COL[end]), tok["sign", k // 2][:],
+                       T.gt[:, 64 * src[k]:64 * src[k] + COL[end] - COL[k]], False, k == 4)
+            mm([], T.pb[:, 0:NT], tok["sign", 0][:], T.gt[:, tail:tail + NT], False, False)
+        elif word == "eB":
+            x = mm(deps, bank(COL[6], NC), tok["sign", 3][:], T.gt[:, 64 * src[6]:64 * src[6] + 128], False, False)
+        tok.update({n: x for n in gives})
+        return x
+
+    todo = {q: words.split() for q, words in ROUND0.items()}
+    while any(todo.values()):
+        moved = False
+        for q in "svp":
+            while todo[q] and step(q, todo[q][0]) is not None:
+                todo[q].pop(0)
+                moved = True
+        assert moved, todo
+    t_cz, t_tab = tok["late",], tok["x",]
+    mm([t_cz, t_tab], T.pz[:, 0:NZ], T.ones[0:1, :], T.cz[0:1, 0:NZ], True, False)
+    mm([COL64], T.pz[:, C_S:NZ], T.blk[:], T.c64[:, 0:2], False, False)
+    mm([], T.pt[:, 0:2], T.ones[0:1, :], T.cz[0:1, C_P:C_S], True, False)
+    x = best(0, 0, [tok["eA",]])
+    v([], V.tensor_tensor, T.sgn[:], T.ll[:, 1], T.ll[:, 0], ALU.subtract)
+    red0 = best(0, 1, [x, t_cz, tok["d", 7]])
+    off0 = winner(0, [red0], T.woff[:, 0:5], T.nbig[:, 0:5])[1]
+
+    x = v([off0, t_cz], V.tensor_tensor, T.wm[:], T.mass[:, 0:512].indirect(T.woff[:, 0:3]), T.coef[:], ALU.mult)
+    mm([x], T.pz[:, 0:C_P], T.blk[:], T.wm[:, 0:C_P], False, False)
+    z = mm([], T.pz[:, C_Q:C_P], T.sgn[:], T.wm[:, C_P:34], False, True)
+    own = mm([], T.pt[:, 0:2], T.sgn[:], T.wm[:, 34:36], False, True)
+    t_rank = s([z], T.junk[:, 0:16], T.pz[:, C_Q:C_P], ACT.Sign, accum_out=T.col[:, 0:1])
+    t_d = s([], T.dist[:, 0:NZ], T.pz[:, 0:NZ], ACT.Copy)
+    steps = clear(0, T.woff[:, 4:5], [t_tab])
     next(steps)
     next(steps)
-    x = v([t_d], V.tensor_scalar, T.col[:, 1:2], T.dist[:, C_D:NZ], float(MID), 0.5, ALU.subtract, ALU.mult)
-    x = v([x, t_rank], V.tensor_scalar, T.ranked[:], T.rk[:], T.col[:, 0:1], T.col[:, 1:2], ALU.is_equal, ALU.mult)
+    placed = [v([t_rank, own], V.tensor_scalar, T.ranked[:, 16 * j:16 * j + 16], T.rk[:, 16 * j:16 * j + 16], T.col[:, 0:1],
+                T.pt[:, j:j + 1], ALU.is_equal, ALU.mult) for j in range(2)]
+    split[0] = PARTS[NA]
     numbers([red0], "a")
-    mm([x], T.pz[:, 32:48], T.blk[:], T.ranked[:], True, False)
-    x = mm([], T.pz[:, 32:47], T.blk[:], T.ranked[:, 1:16], False, True)
+    for word in GAP[0].split():
+        step("p", word)
+    for j in range(2):
+        mm([placed[j], t_d], T.pz[:, 32:48], T.blk[:], T.ranked[:, 16 * j:16 * j + 16], j == 0, False)
+        y = mm([], T.pz[:, 32:47], T.blk[:], T.ranked[:, 16 * j + 1:16 * j + 16], False, j == 1)
     numbers([], "b")
+    for word in GAP[1].split():
+        step("p", word)
     next(steps)
-    t_kn = v([x], V.tensor_tensor, T.kn[:], T.pz[:, 32:48], T.ksh[:], ALU.add)
+    t_kn = v([y], V.tensor_tensor, T.kn[:], T.pz[:, 32:48], T.ksh[:], ALU.add)
 
     def fold(lo, hi):
         for side, c in enumerate((C_B, C_Y)):
@@ -403,71 +438,79 @@ def rank_program(g, core, T, topo):
     def vee(lo, hi, x):
         return s([x, t_kn], T.zig[:, 14:16, lo:hi], T.u[:, :, lo:hi], ACT.Abs, bias=T.kn[:, 8:9], scale=-1.0)
 
-    H = [T.mb, T.ma, T.pt]
+    def H(n, a, b):
+        return T.px[:, 0, a:b] if n == 3 else [T.mb, T.pt, T.pz][n][:, a:b]
+
     t_u, t_ul, t_v = {}, {}, {}
-    t_u[0] = fold(0, PARTS[1])
-    t_u[1] = t_u[2] = fold(PARTS[1], NC)
-    t_ul[0] = lower(0, PARTS[1], t_u[0])
-    t_v[0] = vee(0, PARTS[1], t_u[0])
-    t_ul[1] = t_ul[2] = lower(PARTS[1], NC, t_u[1])
-    t_v[1] = t_v[2] = vee(PARTS[1], NC, t_u[1])
 
     def clamps(n, js):
         lo, hi = PARTS[n], PARTS[n + 1]
+        out = H(n, 0, 2 * (hi - lo))
         for j in js:
-            a, source, tok = (2 * j, T.u, t_u[n]) if j < 4 else (2 * j + 1, T.ul, t_ul[n])
-            x = v([t_kn, tok], V.tensor_scalar, T.zig[:, 2 * j:2 * j + 2, lo:hi], source[:, :, lo:hi], T.kn[:, a:a + 1],
+            a, source, ready = (2 * j, T.u, t_u[n]) if j < 4 else (2 * j + 1, T.ul, t_ul[n])
+            x = v([t_kn, ready], V.tensor_scalar, T.zig[:, 2 * j:2 * j + 2, lo:hi], source[:, :, lo:hi], T.kn[:, a:a + 1],
                   T.kn[:, a + 1:a + 2], ALU.max, ALU.min)
             if j == 6:
-                mm([t_v[n]], H[n][:, 0:2 * (hi - lo)], T.eyeh[:], T.zig[:, 14:16, lo:hi], False, False)
-            x = mm([x, k7, t_s64], H[n][:, 0:2 * (hi - lo)], T.eye[:] if j < 4 else T.eyen[:], T.zig[:, 2 * j:2 * j + 2, lo:hi],
+                mm([t_v[n]], out, T.eyeh[:], T.zig[:, 14:16, lo:hi], False, False)
+            x = mm([x, max(t_u.values())] if n == 3 else [x], out, T.eye[:] if j < 4 else T.eyen[:], T.zig[:, 2 * j:2 * j + 2, lo:hi],
                    j == 0, j == 6)
         return x
 
     def size(n, deps):
-        width = 2 * (PARTS[n + 1] - PARTS[n])
-        return s(deps, H[n][:, 0:width], H[n][:, 0:width], ACT.Abs, bias=T.col[:, 2:3])
+        lo, hi = PARTS[n], PARTS[n + 1]
+        x = s(deps, T.m0[:, lo:hi], H(n, 0, hi - lo), ACT.Abs, bias=T.col[:, 2:3])
+        return x, s([], H(n, hi - lo, 2 * (hi - lo)), H(n, hi - lo, 2 * (hi - lo)), ACT.Abs, bias=T.col[:, 2:3])
 
     def kept(n, side, deps):
         lo, hi = PARTS[n], PARTS[n + 1]
-        return v(deps, V.tensor_tensor, T.m1[:, lo:hi], H[n][:, side * (hi - lo):(side + 1) * (hi - lo)],
+        return v(deps, V.tensor_tensor, T.m1[:, lo:hi], H(n, hi - lo, 2 * (hi - lo)) if side else T.ma[:, lo:hi],
                  (T.m1 if side else T.m0)[:, lo:hi], ALU.min)
 
     def scores(n, x):
         lo, hi = PARTS[n], PARTS[n + 1]
-        return score_own(T.m1, lo, hi, [x], hi == CA), score_tail(T.m1, lo, hi, hi == NC)
+        return score_own(T.m1, lo, hi, [x], hi == split[0]), score_tail(T.m1, lo, hi, hi == NC)
 
-    LOWER, UPPER = range(0, 4), range(4, 7)
-    x = v([t_kn], V.tensor_tensor, T.junk[:, 16:32], T.kn[:], T.kco[:], ALU.mult)
-    t_k = s([x], T.junk[:, 16:32], T.junk[:, 16:32], ACT.Identity, bias=-512.0 * MID / 16, accum_out=T.col[:, 2:3])
-    clamps(0, LOWER)
-    clamps(1, LOWER)
-    h0 = clamps(0, UPPER)
-    clamps(2, LOWER)
-    h1 = clamps(1, UPPER)
-    h2 = clamps(2, UPPER)
-    a0 = size(0, [h0, t_k])
-    key, up = T.kab[:, 2:3], T.kab[:, 3:4]
-    y = s([], T.s64[:, 1:2], up, ACT.Identity, bias=-BIG)
-    a1 = size(1, [h1])
-    a2 = size(2, [h2])
-    s([y], T.res[:, 0:1], key, ACT.Identity, bias=T.s64[:, 1:2], scale=-1.0)
-    res0 = s([], T.res[:, 2:3], T.s64[:, 1:2], ACT.Identity, bias=T.s64[:, 0:1], scale=1.0 / 1024)
-    scores(0, kept(0, 1, [kept(0, 0, [a0])]))
-    ta = scores(1, kept(1, 1, [kept(1, 0, [a1])]))[0]
-    tb = scores(2, kept(2, 1, [kept(2, 0, [a2])]))[1]
-    best(1, 0, [ta])
-    key1, off1 = winner(1, [best(1, 1, [tb])], 2, 3)
-    *_, gone = clear(1, T.woff[:, 4:5], [off1])
+    key, up = T.run[:, 0, NB - 1:NB], T.kab[:, 1:2]
+    for word in ROUND1.split():
+        kind, ns = word[0], [int(c) for c in word[1:]]
+        n = ns[0] if ns else 0
+        lo, hi = PARTS[n], PARTS[ns[-1] + 1] if ns else 0
+        if kind in "ulv":
+            x = fold(lo, hi) if kind == "u" else (lower if kind == "l" else vee)(lo, hi, t_u[ns[-1]])
+            for m in ns:
+                {"u": t_u, "l": t_ul, "v": t_v}[kind][m] = x
+        elif kind in "LU":
+            tok["h", n] = clamps(n, range(0, 4) if kind == "L" else range(4, 7))
+        elif kind == "k":
+            tok["k"] = v([t_kn], V.tensor_tensor, T.junk[:, 16:32], T.kn[:], T.kco[:], ALU.mult)
+        elif kind == "K":
+            tok["K"] = s([tok["k"]], T.junk[:, 16:32], T.junk[:, 16:32], ACT.Identity, bias=-512.0 * MID / 16,
+                         accum_out=T.col[:, 2:3])
+        elif kind == "a":
+            tok["a", n] = size(n, [tok["h", n], tok["K"]])
+        elif kind == "b":
+            tok["B", n] = kept(n, 0, [tok["a", n][0]])
+        elif kind == "y":
+            tok["Y", n] = kept(n, 1, [tok["B", n], tok["a", n][1]])
+        elif kind == "s":
+            tok["S", n] = scores(n, tok["Y", n])
+        elif kind == "A":
+            tok["A"] = best(1, 0, [tok["S", NA - 1][0]])
+        elif kind == "r":
+            x = s([], T.s64[:, 1:2], up, ACT.Identity, bias=-BIG)
+            s([x], T.res[:, 0:1], key, ACT.Identity, bias=T.s64[:, 1:2], scale=-1.0)
+            res0 = s([], T.res[:, 2:3], T.s64[:, 1:2], ACT.Identity, bias=T.dist[:, C_S:C_S + 1], scale=1.0 / 1024)
+    key1, off1 = winner(1, [best(1, 1, [tok["A"], tok["S", len(PARTS) - 2][1]])], T.woff[:, 6:7], T.nbig[:, 4:5])
+    *_, gone = clear(1, T.woff[:, 6:7], [off1])
 
     wait("y", [gone])
     g.sync.dma_start(T.left[:], T.S[:]).then_inc(sem.dleft, 16)
-    key, up = T.kab[:, 6:7], T.kab[:, 7:8]
+    key, up = T.run[:, 1, NB - 1:NB], T.kab[:, 3:4]
     x = s([key1, res0], T.s64[:, 2:3], up, ACT.Identity, bias=-BIG)
     s([x], T.res[:, 1:2], key, ACT.Identity, bias=T.s64[:, 2:3], scale=-1.0)
     x = s([], T.res[:, 3:4], T.s64[:, 2:3], ACT.Copy, scale=1.0 / 1024)
     wait("s", [x])
     g.scalar.dma_start(T.win[:], T.res[0:128:16, 0:2]).then_inc(sem.dres, 16)
     g.scalar.dma_start(T.score[:], T.res[0:128:16, 2:4]).then_inc(sem.dres, 16)
-    wait("g", [("sent", 6 * nfar + 2 * len(near)), ("qg", count["g"]), ("qp", count["p"]), ("qs", count["s"]),
+    wait("g", [("sent", 7 * nfar + 2 * len(near)), ("qg", count["g"]), ("qp", count["p"]), ("qs", count["s"]),
                ("qv", count["v"]), ("dres", 32), ("dleft", 16)])

from concourse.bass import DstId, RemoteDMATransfer
from concourse.mybir import AluOpType, AxisListType, ActivationFunctionType

N, KC, W = 8, 64, 3072
NT = 28
COL = [0, 64, 100, 164, 228, 292, 356, 420, 484]
NC, CA = COL[8], COL[6]
NB = 512 - CA
HALF = 1536
EARLY = [("s", 0, 32), ("s", 32, 64)]
GAP = ["p5", "p4"]
ROUND0 = {
    "v": "y0-32 y32-64 c2 y64-82 y82-100 c3 a56 y100-132 y132-164 c45 y164-196 y196-228 y228-260 y260-292 c67 t y292-324 "
         "k23 y324-356 y356-388 y388-420 y420-452 y452-484",
    "s": "a34 c1 b64-82 b82-100 b100-132 b132-164 b164-196 b196-228 b228-260 b260-292 b292-324 b324-356 "
         "b356-388 b388-420 b420-452 b452-484 f0123 x",
    "p": "m1 m2 n m3 d0 m45 d1 p01 m67 t p23 x s23 d45 d6 eA eB d7 p67",
}
PARTS = [0, 190, 356, 428, NC]
ASKS, LATER = [(0, 1, 2), (3, 4)], [(5, 6)]
NA = 2
ROUND1 = "u0 u123 l0 v0 l123 v123 L0 k K L1 U0 U1 L2 U2 L3 U3 a0 a1 a2 a3 r b0 y0 b1 s0 y1 s1 b2 b3 y2 y3 s2 s3 A"
BIG = 1.5 * 2.0 ** 33
C_B, C_Y, C_Q, C_P, C_N, C_S, NZ = 0, 1, 2, 18, 19, 20, 22
MID, SHIFT = 1536, 1024

BF, F16, F32, I32, U16 = "bfloat16", "float16", "float32", "int32", "uint16"
SCRATCH = {"ll": ("sbuf", [128, 2, 8, 16], BF), "lh": ("sbuf", [128, 2, 8, 16], BF), "lt": ("sbuf", [128, 2, 128, 15], BF),
           "off": ("sbuf", [128, 2, NC], U16), "u": ("sbuf", [128, 2, NC], U16), "ul": ("sbuf", [128, 2, NC], F16),
           "run": ("sbuf", [128, 2, NB], F32), "zig": ("sbuf", [128, 16, NC], F16), "px": ("psum", [128, 2, 512], F32)}
for _name, _cols, _dt in [
        ("wants", 32, I32), ("w16", 32, U16), ("loff", 32, U16), ("peps", W, BF), ("S", W, BF), ("gath", 448, BF),
        ("mass", 512, BF), ("offt", 32, U16), ("gb", 16 * NC, BF), ("gm", 16 * NC, BF), ("gt", 512, BF), ("m0", NC, BF),
        ("m1", NC, BF), ("iw", 128, I32), ("iu", 128, I32), ("sg", 128, I32), ("blk", 128, BF), ("blkn", 128, BF),
        ("blkp", 128, BF), ("blkq", 128, BF), ("blkt", 128, BF), ("eye", 128, BF), ("eyen", 128, BF), ("ge", 128, BF),
        ("lbp", 128, BF), ("wd", 144, BF), ("ones", 128, BF), ("lo", 64, BF), ("num", 512, F16), ("zero", 16, BF),
        ("g16", 4, F32), ("gap", 16, F32), ("tri", 16, F32), ("lane", 4, F32), ("coef", 48, BF), ("cz", 32, BF),
        ("nbig", 8, F32), ("wm", 48, BF), ("tabs", 1536, F32), ("dist", 32, F32), ("rk", 32, F32), ("ksh", 16, F32),
        ("kco", 16, F32), ("kn", 16, F16), ("ranked", 32, F16), ("junk", 32, F32), ("col", 4, F32), ("blkh", 128, BF),
        ("eyeh", 128, BF), ("s64", 4, F32), ("kab", 8, F32), ("woff", 8, U16), ("zl", 32, U16), ("sgn", 128, BF),
        ("res", 4, F32), ("upp", 128, BF), ("upn", 128, BF), ("c64", 8, BF)]:
    SCRATCH[_name] = ("sbuf", [128, _cols], _dt)
for _name in ["ma", "mb", "pa", "pb", "pt", "pz"]:
    SCRATCH[_name] = ("psum", [128, 512], F32)
SEMAPHORES = ["qv", "qs", "qp", "qg", "dwant", "dspec", "dleft", "dres", "dlow", "dcol", "dpea", "dpeb", "sent",
              "ask0", "ask1", "ask2", "ask3", "rep0", "rep1", "rep2", "rep3", "rep4"]

ALU = AluOpType
ACT = ActivationFunctionType


def partner_order(T, topo, core):
    ch = topo.chip(core)

    def key(q):
        c = T.cores[q]
        cc = topo.chip(c)
        kind = 0 if cc == ch else 1 if topo.mates(ch, cc) else 2 if topo.same_plane(ch, cc) else 3
        return (kind, 0 if topo.die(c) == topo.die(core) else 1, q)
    return sorted([q for q in range(N) if T.cores[q] != core], key=key)


def bits(engines):
    return sum(1 << e for e in engines)


def tail_runs(lo, hi):
    runs = []
    for f in range(15):
        a, b = max(lo, COL[1] + NT * f), min(hi, COL[1] + NT * (f + 1))
        if a < b:
            runs.append((f, a, b, a - COL[1] - NT * f))
    return runs


def rank_program(g, core, T, topo):
    r = T.rank_of(core)
    if r is None:
        return
    order = partner_order(T, topo, core)
    src = [r] + order[0:3] + sorted(order[3:5]) + sorted(order[5:7])
    place = [partner_order(T, topo, T.cores[q]).index(r) for q in order]
    addr = [topo.addr(T.cores[q]) for q in order]
    far = topo.engines(core, T.cores[order[1]])
    near = [e for e in topo.engines(core, T.cores[order[0]]) if e not in far]
    nfar, hf = len(far), len(far) // 2
    sem = T.sem
    Q = {"v": g.vector, "s": g.scalar, "p": g.tensor, "g": g, "y": g.sync}
    QS = {"v": "qv", "s": "qs", "p": "qp", "g": "qg"}
    count = {"v": 0, "s": 0, "p": 0, "g": 0}
    seen = {}

    def wait(q, deps):
        for name, val in deps:
            if seen.get((q, name), 0) < val:
                Q[q].wait_ge(sem[name], val)
                seen[(q, name)] = val

    def op(q, deps, method, *a, **k):
        wait(q, deps)
        method(*a, **k).then_inc(sem[QS[q]], 1)
        count[q] += 1
        return (QS[q], count[q])

    V, S, P = g.vector, g.scalar, g.tensor

    def v(deps, m, *a, **k):
        return op("v", deps, m, *a, **k)

    def s(deps, *a, **k):
        return op("s", deps, S.activation, *a, **k)

    def mm(deps, out, lhsT, rhs, start, stop):
        return op("p", deps, P.matmul, out, lhsT, rhs, start, stop)

    def copy(q, deps, out, in_):
        return s(deps, out, in_, ACT.Copy) if q == "s" else v(deps, V.tensor_copy, out, in_)

    g.sync.dma_start(T.wants[:], T.want[:]).then_inc(sem.dwant, 16)
    g.sync.dma_start(T.peps[:, 0:HALF], T.pep[:, 0:HALF]).then_inc(sem.dpea, 16)
    g.sync.dma_start(T.peps[:, HALF:W], T.pep[:, HALF:W]).then_inc(sem.dpeb, 16)
    wait("y", [("dpea", 16)])
    g.sync.dma_start(T.S[:, 0:HALF], T.spec[:, 0:HALF]).then_inc(sem.dlow, 16)
    wait("y", [("dpeb", 16)])
    g.sync.dma_start(T.S[:, HALF:W], T.spec[:, HALF:W]).then_inc(sem.dspec, 16)
    g.sync.dma_start(T.c64[:, 0:2], T.spec[:, 64:66]).then_inc(sem.dcol, 16)
    WANT, LOW, SPEC, COL64 = ("dwant", 16), ("dlow", 16), ("dspec", 16), ("dcol", 16)
    PEP = [("dpea", 16), ("dpeb", 16)]

    def level(out, value, pattern=None):
        return op("g", [], g.iota, out, pattern or [[0, out.shape[1]]], value, 0, allow_small_or_imprecise_dtypes=True)

    t_iw = op("g", [], g.iota, T.iw[:], [[16, 8], [0, 16]], 15, -1)
    t_iu = op("g", [], g.iota, T.iu[:], [[1, 128]], 0, -1)
    t_up = level(T.upp[0:1, :], 0, [[0, 8], [64, 2], [0, 8]])
    t_lo = level(T.lo[0:1, :], 0, [[-1, 64]])
    v([], V.memset, T.lt[:, 0], 0.0)
    t_own = v([WANT], V.tensor_copy, T.w16[:], T.wants[:])

    def transfer(k, name, source, landing):
        engines = near if k == 0 else far[hf * ((k - 1) % 2):hf * ((k - 1) % 2) + hf]
        if name == "rep" and k in (1, 2):
            engines = far
        return RemoteDMATransfer(dst_ids=[DstId(rid=addr[k][0], pnc=addr[k][1])], dma_engine_mask=bits(engines),
                                 remote_sem=sem[name + ("0142233" if name == "rep" else "0112233")[k]], src=source, dst=landing)

    wait("g", [t_own])
    def ask(ks):
        g.remote_dma_fused([transfer(k, "ask", T.w16[:, 4 * order[k]:4 * order[k] + 4],
                                     T.loff[:, 4 * place[k]:4 * place[k] + 4]) for k in ks], local_sem=sem.sent)

    for ks in ASKS:
        ask(ks)

    t_sg = v([t_iw], V.tensor_scalar, T.sg[:], T.iw[:], 4, None, ALU.arith_shift_right)
    t_ge = v([t_iu], V.tensor_scalar, T.ge[:], T.iu[:], 0.0, None, ALU.is_ge)
    t_ones = v([], V.memset, T.ones[0:1, :], 1.0)
    t_blk = v([t_sg], V.tensor_scalar, T.blk[:], T.sg[:], 0.0, None, ALU.is_equal)
    t_g16 = v([], V.tensor_scalar, T.g16[:, 0:1], T.sg[:, 0:1], -16.0, None, ALU.mult)
    t_wd0 = v([], V.memset, T.wd[:], 0.0)
    t_lb = v([t_ge, t_blk], V.tensor_tensor, T.ll[:, 0], T.ge[:], T.blk[:], ALU.mult)
    t_dif = v([t_g16], V.tensor_scalar, T.gap[:], T.iu[:, 0:16], T.g16[:, 0:1], None, ALU.add)
    t_wd = v([t_wd0], V.tensor_copy, T.wd[:, 15:128:16], T.blk[:, 15:128:16])
    t_ly = v([t_lb], V.tensor_tensor, T.ll[:, 1], T.blk[:], T.ll[:, 0], ALU.subtract)
    t_tri = v([t_dif], V.tensor_scalar, T.tri[:], T.gap[:], 0.0, None, ALU.is_ge)
    v([], V.memset, T.nbig[:, 0:4], -BIG)
    v([], V.memset, T.cz[0:1, C_Q:C_P], -127.5)
    for j in range(2):
        v([], V.memset, T.coef[:, 34 + j:35 + j], j - 0.5)
    v([t_ly], V.tensor_copy, T.lh[:, :, :, 0:8], T.ll[:, :, :, 0:8])
    for side in range(2):
        t_high = v([], V.tensor_copy, T.lh[:, side, :, 8:16], T.ll[:, 1 - side, :, 8:16])
    v([t_wd], V.tensor_tensor, T.lbp[:], T.ll[:, 0], T.wd[:, 0:128], ALU.subtract)
    t_lt = v([], V.memset, T.lt[:, 1], 0.0)

    def fill(out, like, value):
        return s([], out, like, ACT.Identity, bias=float(value), scale=0.0)

    t_upn = s([t_up], T.upn[0:1, :], T.upp[0:1, :], ACT.Copy, scale=-1.0)
    t_blkp = s([t_blk], T.blkp[:], T.blk[:], ACT.Copy, scale=1024.0)
    t_blkn = s([], T.blkn[:], T.blk[:], ACT.Copy, scale=-1024.0)
    t_blkh = s([], T.blkh[:], T.blk[:], ACT.Copy, scale=512.0)
    x = s([t_dif], T.lane[:, 0:1], T.gap[:, 14:15], ACT.Relu, scale=-1.0)
    s([], T.coef[:, C_Q:C_P], T.gap[:], ACT.Sign, bias=0.5)
    t_lane = s([], T.lane[:, 1:2], T.gap[:, 0:1], ACT.Identity, bias=14.0, scale=4.0)
    s([t_blkp, t_tri], T.blkq[:], T.blkp[:], ACT.Copy, scale=T.tri[:, 14:15])
    s([], T.nbig[:, 4:5], T.tri[:, 7:8], ACT.Identity, bias=1024.0 - BIG, scale=-1024.0)
    t_blkt = s([x], T.blkt[:], T.blkp[:], ACT.Copy, scale=T.lane[:, 0:1])
    s([], T.rk[:, 0:16], T.gap[:], ACT.Identity, bias=16.0, scale=2.0)
    s([t_lane], T.rk[:, 16:32], T.gap[:], ACT.Identity, bias=T.lane[:, 1:2], scale=-2.0)

    def late_constants():
        level(T.cz[0:1, C_B:C_Q], 64, [[-128, 2]])
        level(T.cz[0:1, C_P:C_S], -32 - MID // 2, [[64, 2]])
        level(T.cz[0:1, C_S:NZ], 0)
        level(T.coef[:, C_B:C_Q], 1)
        level(T.coef[:, C_P:34], -1)
        level(T.coef[:, 36:48], 0)
        level(T.zero[:], 0)
        level(T.tabs[:, 512:1024], 0)
        for lo, hi, val in [(0, 9, MID), (9, 15, MID - SHIFT), (15, 16, 0)]:
            level(T.ksh[:, lo:hi], val)
        level(T.kco[:, 0:8], 0, [[0, 4], [-1024, 2]])
        level(T.kco[:, 8:9], 512)
        level(T.kco[:, 9:15], 0, [[0, 3], [1024, 2]])
        level(T.kco[:, 15:16], -1024)
        for eye, blk, tok in [(T.eye, T.blkp, t_blkp), (T.eyen, T.blkn, t_blkn), (T.eyeh, T.blkh, t_blkh)]:
            x = op("g", [tok], g.affine_select, eye[:], blk[:], [[-1, 128]], ALU.is_equal, 0.0, 0, 1)
        return x

    split = [CA]

    def numbers(deps, banks="ab"):
        if "a" in banks:
            x = mm(deps, T.pa[:, 0:CA], T.ones[0:1, :], T.num[0:1, 0:CA], True, False)
        if "b" in banks:
            x = mm([], T.pb[:, 0:512 - CA], T.ones[0:1, :], T.num[0:1, CA:512], True, False)
        return x

    def bank(lo, hi):
        ca = split[0]
        return T.pa[:, lo:hi] if lo < ca else T.pb[:, NT + lo - ca:NT + hi - ca]

    pepw = T.peps[:, 0:W]
    mine = T.mass[:, 64 * r:64 * r + 64]
    tail = 64 * src[1] + 64 - NT

    def answer(ks, q):
        asked = ("ask%d" % ((ks[0] + 1) // 2), nfar if ks[0] else len(near))
        x = copy(q, [asked] + PEP, T.gath[:, 64 * ks[0]:64 * ks[-1] + 64], pepw.indirect(T.loff[:, 4 * ks[0]:4 * ks[-1] + 4]))
        wait("g", [x])
        g.remote_dma_fused([transfer(k, "rep", T.gath[:, 64 * k:64 * k + 64], mine) for k in ks], local_sem=sem.sent)
        return x

    def lists(ks, sides, deps):
        lo, hi = COL[ks[0]], COL[ks[-1] + 1]
        rhs = T.mass[:, 64 * src[ks[0]]:64 * src[ks[0]] + hi - lo]
        for side in sides:
            tok = mm(deps, T.px[:, side, lo:hi], T.ll[:, 1] if side else T.lbp[:], rhs, True, False)
            for f, a, b, c in tail_runs(lo, hi):
                tok = mm([], T.px[:, side, a:b], T.lt[:, side, :, f], T.mass[:, tail + c:tail + c + b - a], False, b == hi)
        return tok

    wb, wy = T.S[:, 0:W], T.S[:, 64:W]

    def slot(lo, hi, i):
        return T.gm[:, 16 * lo + i:16 * hi:16]

    def score_own(m, lo, hi, deps, stop=False):
        return mm(deps, bank(lo, hi), T.blkq[:], m[:, lo:hi], False, stop)

    def score_tail(m, lo, hi, stop=False):
        for f, a, b, c in tail_runs(lo, hi):
            tok = mm([], T.pb[:, c:c + b - a], T.blkt[:], m[:, a:b], False, stop and b == hi)
        return tok

    def best(t, half, deps):
        ka = T.kab[:, 2 * t:2 * t + 1]
        if half:
            return v(deps, V.tensor_tensor_scan, T.run[:, t], T.pb[:, 0:NB], T.tabs[:, 512:512 + NB], ka, ALU.max, ALU.add)
        return v(deps, V.tensor_reduce, ka, T.pa[:, 0:CA], AxisListType.X, ALU.max)

    def winner(t, deps, out, base):
        key, up = T.run[:, t, NB - 1:NB], T.kab[:, 2 * t + 1:2 * t + 2]
        y = v(deps, V.tensor_scalar, up, key, BIG, None, ALU.add)
        return y, v([y], V.tensor_scalar, out, base, up, key, ALU.add, ALU.subtract)

    def clear(t, off, deps):
        x = v(deps, V.tensor_copy, T.zl[:, 16 * t:16 * t + 16], T.tabs[:, 0:1536].indirect(off))
        yield x
        x = v([x], V.tensor_copy, wb.indirect(T.zl[:, 16 * t:16 * t + 1]), T.zero[:])
        yield x
        yield v([x], V.tensor_copy, wy.indirect(T.zl[:, 16 * t + 8:16 * t + 9]), T.zero[:])

    t_mine = s([t_own] + PEP, mine, pepw.indirect(T.w16[:, 4 * r:4 * r + 4]), ACT.Copy)
    for side, shift in enumerate([T.upp, T.upn]):
        mm([t_mine, t_high], T.px[:, side, 0:64], T.lh[:, side], mine, True, False)
        made = mm([t_ones, t_upn], T.px[:, side, 0:64], shift[0:1, :], T.ones[0:1, 0:64], False, True)
    c0 = v([made], V.tensor_copy, T.off[:, :, 0:64], T.px[:, :, 0:64])
    at = 0
    for k, a, b in [(k, 0, COL[k + 1] - COL[k]) for k in range(6)] + [(1, 64 - NT, 64), (6, 0, 64), (7, 0, 64)]:
        t_num = s([t_lo], T.num[0:1, at:at + b - a], T.lo[0:1, a:b], ACT.Identity, bias=-64.0 * src[k])
        at += b - a
    t_const = v([t_lt], V.tensor_copy, T.lt[:, :, 15:128:16, :], T.ll[:, :, :, 0:15])
    answer([0], "v")
    answer([1], "v")
    answer([2], "v")
    for ks in LATER:
        ask(ks)
    tok = {("c", 0, 0): c0, ("c", 0, 1): c0}
    for q, lo, hi in EARLY:
        x = copy(q, [LOW, c0], T.gb[:, 16 * lo:16 * hi], T.S[:, 0:HALF].indirect(T.off[:, 0, lo:hi]))
        tok.update({("b", c): x for c in range(lo, hi)})
    last_made = {0: [0], 1: [0]}

    def step(q, word):
        kind, rest = word[0], word[1:]
        if kind in "by":
            lo, hi = [int(c) for c in rest.split("-")]
            side = int(kind == "y")
            need = [("c", k, side) for k in range(8) if COL[k] < hi and lo < COL[k + 1]]
            need += [("b", c) for c in range(lo, hi)] if side else []
            gives = [(kind, c) for c in range(lo, hi)]
        elif kind in "cm":
            sides = [0] if rest[-1] == "b" else [1] if rest[-1] == "y" else [0, 1]
            ks = [int(c) for c in rest if c.isdigit()]
            if kind == "c":
                need = [("m", k, side) for k in ks for side in sides]
            else:
                need = [("c", k, side) for side in sides for k in last_made[side]]
            gives = [(kind, k, side) for k in ks for side in sides]
            lo, hi = COL[ks[0]], COL[ks[-1] + 1]
        elif kind in "pdks":
            ks = [int(c) for c in rest]
            lo, hi = COL[ks[0]], COL[ks[-1] + 1]
            need = [("y", c) for c in range(lo, hi)] if kind in "pd" else [("p" if kind == "k" else "k", ks[0])]
            need += [w for w in tok if w[0] == "k"] if kind == "p" else []
            gives = [(kind, k) for k in ks]
        elif kind == "f":
            need, gives = [("t",)], [("f", int(c)) for c in rest]
        else:
            need = {"tv": [("tp",)], "ts": [("tp",)], "tp": [("m", 7, 0)], "xp": [("t",)], "xs": [("xp",)],
                    "eA": [("f", 0), ("f", 1), ("f", 2)], "eB": [("f", 3)]}.get(
                        word if len(word) == 2 else kind + q, [])
            gives = [(word + q if word in "tx" and q == "p" else word,)]
        if any(n not in tok for n in need):
            return None
        deps = sorted(set(tok[n] for n in need))
        if kind == "b":
            x = copy(q, deps + [SPEC], T.gb[:, 16 * lo:16 * hi], wb.indirect(T.off[:, 0, lo:hi]))
        elif kind == "y":
            x = v(deps + [LOW, SPEC], V.tensor_tensor, T.gm[:, 16 * lo:16 * hi], wy.indirect(T.off[:, 1, lo:hi]),
                  T.gb[:, 16 * lo:16 * hi], ALU.min)
        elif kind == "c":
            x = copy(q, deps, T.off[:, sides[0]:sides[-1] + 1, lo:hi], T.px[:, sides[0]:sides[-1] + 1, lo:hi])
        elif kind == "m":
            x = lists(ks, sides, deps + [("rep" + "0142233"[ks[0] - 1], nfar if ks[0] > 1 else len(near)), t_const])
            last_made.update({side: ks for side in sides})
        elif kind == "p":
            for i in range(16):
                x = mm(deps, T.ma[:, lo:hi], T.wd[:, 15 - i:143 - i], slot(lo, hi, i), i == 0, i == 15)
        elif kind == "k":
            x = copy(q, deps, T.m0[:, lo:hi], T.ma[:, lo:hi])
        elif kind == "s":
            x = score_own(T.m0, lo, hi, deps + [t_blkt])
            x = score_tail(T.m0, lo, hi)
        elif kind == "d":
            for f, a, b, c in tail_runs(lo, hi):
                mm(deps + [t_blkp], T.pb[:, c:c + b - a], T.blkp[:], slot(a, b, 15), False, False)
            for i in range(15):
                x = mm(deps + [t_blkp], bank(lo, hi), T.blkp[:], slot(lo, hi, i), False, hi == NC and i == 14)
        elif kind == "a":
            x = answer([int(c) for c in rest], q)
            if rest == "56":
                tok["late",] = late_constants()
        elif kind == "n":
            x = numbers([t_num])
        elif word == "t" and q == "p":
            for p in range(16):
                x = mm([], T.pt[:, 0:32], T.wd[:, 15 - p:143 - p], T.mass[:, p:512:16], p == 0, p == 15)
        elif word == "t":
            x = copy(q, deps, T.offt[:], T.pt[:, 0:32])
        elif word == "x" and q == "p":
            mm([], T.pz[:], T.ll[:, 1], T.mass[:], True, True)
            x = mm(deps, T.pt[:], T.ll[:, 0], T.mass[:], True, True)
        elif word == "x":
            copy(q, deps, T.tabs[:, 0:512], T.pt[:])
            x = copy(q, [], T.tabs[:, 1024:1536], T.pz[:])
        elif kind == "f":
            ranks = sorted(src[2 * int(c) + j] for c in rest for j in range(2))
            for a in [a for a in ranks if a - 1 not in ranks]:
                b = min(b for b in range(a, N + 1) if b not in ranks)
                out, at = T.gt[:, 64 * a:64 * b], wb.indirect(T.offt[:, 4 * a:4 * b])
                if q == "s":
                    x = s(deps + [COL64], out, at, ACT.Relu, bias=T.c64[:, 0:1], scale=-1.0)
                else:
                    x = v(deps + [COL64], V.tensor_scalar, out, at, T.c64[:, 0:1], 0.0, ALU.subtract, ALU.min)
            tok.update({("sign", int(c)): T.blkn if q == "s" else T.blkp for c in rest})
        elif word == "eA":
            for k, end in [(0, 1), (1, 2), (2, 3), (3, 4), (4, 6)]:
                x = mm(deps, bank(COL[k], COL[end]), tok["sign", k // 2][:],
                       T.gt[:, 64 * src[k]:64 * src[k] + COL[end] - COL[k]], False, k == 4)
            mm([], T.pb[:, 0:NT], tok["sign", 0][:], T.gt[:, tail:tail + NT], False, False)
        elif word == "eB":
            x = mm(deps, bank(COL[6], NC), tok["sign", 3][:], T.gt[:, 64 * src[6]:64 * src[6] + 128], False, False)
        tok.update({n: x for n in gives})
        return x

    todo = {q: words.split() for q, words in ROUND0.items()}
    while any(todo.values()):
        moved = False
        for q in "svp":
            while todo[q] and step(q, todo[q][0]) is not None:
                todo[q].pop(0)
                moved = True
        assert moved, todo
    t_cz, t_tab = tok["late",], tok["x",]
    mm([t_cz, t_tab], T.pz[:, 0:NZ], T.ones[0:1, :], T.cz[0:1, 0:NZ], True, False)
    mm([COL64], T.pz[:, C_S:NZ], T.blk[:], T.c64[:, 0:2], False, False)
    mm([], T.pt[:, 0:2], T.ones[0:1, :], T.cz[0:1, C_P:C_S], True, False)
    x = best(0, 0, [tok["eA",]])
    v([], V.tensor_tensor, T.sgn[:], T.ll[:, 1], T.ll[:, 0], ALU.subtract)
    red0 = best(0, 1, [x, t_cz, tok["d", 7]])
    off0 = winner(0, [red0], T.woff[:, 0:5], T.nbig[:, 0:5])[1]

    x = v([off0, t_cz], V.tensor_tensor, T.wm[:], T.mass[:, 0:512].indirect(T.woff[:, 0:3]), T.coef[:], ALU.mult)
    mm([x], T.pz[:, 0:C_P], T.blk[:], T.wm[:, 0:C_P], False, False)
    z = mm([], T.pz[:, C_Q:C_P], T.sgn[:], T.wm[:, C_P:34], False, True)
    own = mm([], T.pt[:, 0:2], T.sgn[:], T.wm[:, 34:36], False, True)
    t_rank = s([z], T.junk[:, 0:16], T.pz[:, C_Q:C_P], ACT.Sign, accum_out=T.col[:, 0:1])
    t_d = s([], T.dist[:, 0:NZ], T.pz[:, 0:NZ], ACT.Copy)
    steps = clear(0, T.woff[:, 4:5], [t_tab])
    next(steps)
    next(steps)
    placed = [v([t_rank, own], V.tensor_scalar, T.ranked[:, 16 * j:16 * j + 16], T.rk[:, 16 * j:16 * j + 16], T.col[:, 0:1],
                T.pt[:, j:j + 1], ALU.is_equal, ALU.mult) for j in range(2)]
    split[0] = PARTS[NA]
    numbers([red0], "a")
    for word in GAP[0].split():
        step("p", word)
    for j in range(2):
        mm([placed[j], t_d], T.pz[:, 32:48], T.blk[:], T.ranked[:, 16 * j:16 * j + 16], j == 0, False)
        y = mm([], T.pz[:, 32:47], T.blk[:], T.ranked[:, 16 * j + 1:16 * j + 16], False, j == 1)
    numbers([], "b")
    for word in GAP[1].split():
        step("p", word)
    next(steps)
    t_kn = v([y], V.tensor_tensor, T.kn[:], T.pz[:, 32:48], T.ksh[:], ALU.add)

    def fold(lo, hi):
        for side, c in enumerate((C_B, C_Y)):
            x = s([t_d], T.u[:, side, lo:hi], T.px[:, side, lo:hi], ACT.Abs, bias=T.dist[:, c:c + 1], scale=-2.0)
        return x

    def lower(lo, hi, x):
        return s([x], T.ul[:, :, lo:hi], T.u[:, :, lo:hi], ACT.Identity, bias=-float(SHIFT))

    def vee(lo, hi, x):
        return s([x, t_kn], T.zig[:, 14:16, lo:hi], T.u[:, :, lo:hi], ACT.Abs, bias=T.kn[:, 8:9], scale=-1.0)

    def H(n, a, b):
        return T.px[:, 0, a:b] if n == 3 else [T.mb, T.pt, T.pz][n][:, a:b]

    t_u, t_ul, t_v = {}, {}, {}

    def clamps(n, js):
        lo, hi = PARTS[n], PARTS[n + 1]
        out = H(n, 0, 2 * (hi - lo))
        for j in js:
            a, source, ready = (2 * j, T.u, t_u[n]) if j < 4 else (2 * j + 1, T.ul, t_ul[n])
            x = v([t_kn, ready], V.tensor_scalar, T.zig[:, 2 * j:2 * j + 2, lo:hi], source[:, :, lo:hi], T.kn[:, a:a + 1],
                  T.kn[:, a + 1:a + 2], ALU.max, ALU.min)
            if j == 6:
                mm([t_v[n]], out, T.eyeh[:], T.zig[:, 14:16, lo:hi], False, False)
            x = mm([x, max(t_u.values())] if n == 3 else [x], out, T.eye[:] if j < 4 else T.eyen[:], T.zig[:, 2 * j:2 * j + 2, lo:hi],
                   j == 0, j == 6)
        return x

    def size(n, deps):
        lo, hi = PARTS[n], PARTS[n + 1]
        x = s(deps, T.m0[:, lo:hi], H(n, 0, hi - lo), ACT.Abs, bias=T.col[:, 2:3])
        return x, s([], H(n, hi - lo, 2 * (hi - lo)), H(n, hi - lo, 2 * (hi - lo)), ACT.Abs, bias=T.col[:, 2:3])

    def kept(n, side, deps):
        lo, hi = PARTS[n], PARTS[n + 1]
        return v(deps, V.tensor_tensor, T.m1[:, lo:hi], H(n, hi - lo, 2 * (hi - lo)) if side else T.ma[:, lo:hi],
                 (T.m1 if side else T.m0)[:, lo:hi], ALU.min)

    def scores(n, x):
        lo, hi = PARTS[n], PARTS[n + 1]
        return score_own(T.m1, lo, hi, [x], hi == split[0]), score_tail(T.m1, lo, hi, hi == NC)

    key, up = T.run[:, 0, NB - 1:NB], T.kab[:, 1:2]
    for word in ROUND1.split():
        kind, ns = word[0], [int(c) for c in word[1:]]
        n = ns[0] if ns else 0
        lo, hi = PARTS[n], PARTS[ns[-1] + 1] if ns else 0
        if kind in "ulv":
            x = fold(lo, hi) if kind == "u" else (lower if kind == "l" else vee)(lo, hi, t_u[ns[-1]])
            for m in ns:
                {"u": t_u, "l": t_ul, "v": t_v}[kind][m] = x
        elif kind in "LU":
            tok["h", n] = clamps(n, range(0, 4) if kind == "L" else range(4, 7))
        elif kind == "k":
            tok["k"] = v([t_kn], V.tensor_tensor, T.junk[:, 16:32], T.kn[:], T.kco[:], ALU.mult)
        elif kind == "K":
            tok["K"] = s([tok["k"]], T.junk[:, 16:32], T.junk[:, 16:32], ACT.Identity, bias=-512.0 * MID / 16,
                         accum_out=T.col[:, 2:3])
        elif kind == "a":
            tok["a", n] = size(n, [tok["h", n], tok["K"]])
        elif kind == "b":
            tok["B", n] = kept(n, 0, [tok["a", n][0]])
        elif kind == "y":
            tok["Y", n] = kept(n, 1, [tok["B", n], tok["a", n][1]])
        elif kind == "s":
            tok["S", n] = scores(n, tok["Y", n])
        elif kind == "A":
            tok["A"] = best(1, 0, [tok["S", NA - 1][0]])
        elif kind == "r":
            x = s([], T.s64[:, 1:2], up, ACT.Identity, bias=-BIG)
            s([x], T.res[:, 0:1], key, ACT.Identity, bias=T.s64[:, 1:2], scale=-1.0)
            res0 = s([], T.res[:, 2:3], T.s64[:, 1:2], ACT.Identity, bias=T.dist[:, C_S:C_S + 1], scale=1.0 / 1024)
    key1, off1 = winner(1, [best(1, 1, [tok["A"], tok["S", len(PARTS) - 2][1]])], T.woff[:, 6:7], T.nbig[:, 4:5])
    *_, gone = clear(1, T.woff[:, 6:7], [off1])

    wait("y", [gone])
    g.sync.dma_start(T.left[:], T.S[:]).then_inc(sem.dleft, 16)
    key, up = T.run[:, 1, NB - 1:NB], T.kab[:, 3:4]
    x = s([key1, res0], T.s64[:, 2:3], up, ACT.Identity, bias=-BIG)
    s([x], T.res[:, 1:2], key, ACT.Identity, bias=T.s64[:, 2:3], scale=-1.0)
    x = s([], T.res[:, 3:4], T.s64[:, 2:3], ACT.Copy, scale=1.0 / 1024)
    wait("s", [x])
    g.scalar.dma_start(T.win[:], T.res[0:128:16, 0:2]).then_inc(sem.dres, 16)
    g.scalar.dma_start(T.score[:], T.res[0:128:16, 2:4]).then_inc(sem.dres, 16)
    wait("g", [("sent", 7 * nfar + 2 * len(near)), ("qg", count["g"]), ("qp", count["p"]), ("qs", count["s"]),
               ("qv", count["v"]), ("dres", 32), ("dleft", 16)])
